import numpy as np, ml_dtypes
CORES = [2,6,10,14,18,22,26,30]
N = 8
BF = ml_dtypes.bfloat16
L, S, ST, GENS, K = 192, 8, 3, 2, 48
GW, XW = S * L, 16 * L
def parts(rng):
    g = rng.integers(0, XW, (N, 8, 16, GW)); h = rng.integers(0, GW, (N, 8, 16, GW)); x = rng.integers(0, 256, (N, 8, 16, XW))
    return g, h, x, rng.integers(0, 256, (N, 8, 16, L)), rng.integers(800, 1151, (N, 8))
def pack(g, h, x, a, t):
    return {"gn": np.ascontiguousarray(g.reshape(N, 128, GW)).astype(np.int32), "nb": np.ascontiguousarray(h.reshape(N, 128, GW)).astype(np.int32),
            "x": x.reshape(N, 128, XW).astype(np.float32).astype(BF), "th": np.repeat(t, 16, axis=1).reshape(N, 128, 1).astype(np.int32), "a0": a.reshape(N, 128, L).astype(np.float32).astype(BF)}
def setup_inputs(rng):
    return pack(*parts(rng))
def uneven(rng, n):
    v = np.floor(256 * rng.random((N, 8, 16, n)) * np.exp2(-rng.integers(0, 8, (N, 8, 1, n)).astype(np.float64))).astype(np.int64)
    return np.where(rng.random((N, 8, 1, n)) < 0.5, 255 - v, v)
def setup_inputs_spread(rng):
    g = (XW * rng.random((N, 8, 16, GW)) ** 3).astype(np.int64); h = (GW * rng.random((N, 8, 16, GW)) ** 2).astype(np.int64)
    g[:, 1::2] = XW - 1 - g[:, 1::2]; h[:, :, ::2] = GW - 1 - h[:, :, ::2]
    t = np.argsort(rng.random((N, 8)), axis=1) * 510 + rng.integers(0, 510, (N, 8))
    return pack(g, h, uneven(rng, XW), uneven(rng, L), t)
def twoends(rng, n):
    return np.where(rng.random((N, 8, 1, n)) < 0.7, 255 * rng.integers(0, 2, (N, 8, 1, n)), 255 * rng.integers(0, 2, (N, 8, 16, n)))
def setup_inputs_ends(rng):
    g, h, x, a, t = parts(rng)
    g = np.where(rng.random(g.shape) < 0.8, (XW - 1) * rng.integers(0, 2, g.shape), g); h = np.where(rng.random(h.shape) < 0.8, (GW - 1) * rng.integers(0, 2, h.shape), h)
    x = twoends(rng, XW); a = twoends(rng, L); x[..., 0] = 0; x[..., XW - 1] = 255
    for q in range(N): t[q, :7] = rng.permutation(np.array([0, 0, 4080, 4080, 4080, 2294, 2294]))
    t[:, 7] = 0
    for i in (0, 1, L - 2, L - 1):
        g[:, 7, 0, S * i] = XW - 1; h[:, 7, :, S * i] = GW - 1; a[:, 7, :, i] = 0
    g[:, 7, :15, GW - 1] = XW - 1; g[:, 7, 15, GW - 1] = 0
    return pack(g, h, x, a, t)
def setup_inputs_corners(rng):
    g, h, x, a, t = parts(rng); o = rng.permutation(8); t[:, o[0]] = 0; t[:, o[1]] = 4080
    for q in range(N):
        w = rng.permutation(o[2:])
        h[q, w[0]] = np.arange(GW); h[q, w[1]] = (GW - 1) * rng.integers(0, 2, (16, GW)); h[q, w[2]] = np.roll(np.arange(GW), -1)
        g[q, w[3]] = (XW - 1) * rng.integers(0, 2, (16, GW))
        b = w[4]; t[q, b] = 0; x[q, b, :, XW - 1] = 255; g[q, b, 15] = XW - 1
        i = rng.permutation(L)[:L // 2]; a[q, b][:, i] = x[q, b][:, g[q, b, 0, S * i]]
        x[q, w[5]] = 255 * rng.integers(0, 2, (16, XW))
    return pack(g, h, x, a, t)
def setup_inputs_ties(rng):
    g, h, x, a, t = parts(rng)
    x = 8 * rng.integers(0, 32, (N, 8, 1, XW)) + ((np.arange(16)[:, None] == rng.integers(0, 16, (N, 8, 1, XW))) & (rng.random((N, 8, 1, XW)) < 0.5))
    a = 8 * rng.integers(0, 32, (N, 8, 1, L)) + np.zeros((16, 1), np.int64)
    h[:, ::2] = h[:, ::2, :1]
    return pack(g, h, x, a, 16 * (8 * rng.integers(0, 6, (N, 8)) + 1))
def setup_inputs_counts(rng):
    g, h, x, a, t = parts(rng); q = rng.permutation(N); o = rng.permutation(8); w = int(o[0])
    t[q[0]] = 0; t[q[1]] = 4080; t[q[2]] = 4080; t[q[2], o[1:4]] = 0; t[q[3]] = 0
    if N > 4: t[q[4]] = 1170
    if N > 5: t[q[5], o[1:5]] = 0
    t[:, w] = 0; t[q[1], w] = 4080
    u = np.floor(rng.integers(2, 7, (N, 1, XW)) * rng.random((N, 16, XW))).astype(np.int64); u[:, 0] = 0
    x[:, w] = u; x[q[1], w] = 255 - u[q[1]]; x[q[1], w, 0] = 254
    a[:, w] = 255; a[:, w, 0] = 254
    for r, n in ((q[2], 64), (q[3], 8 * int(rng.integers(3, 5)) + int(rng.choice(np.array([2, 3, 5, 6]))))):
        i = rng.permutation(L)[:n]; a[r, w, 0, i] = 255; h[r, w, 0, S * i] = S * i
    return pack(g, h, x, a, t)
def check_inputs(d):
    bad = []
    for k, lo, hi in (("gn", 0, XW - 1), ("nb", 0, GW - 1), ("x", 0, 255), ("th", 0, 4080), ("a0", 0, 255)):
        v = np.asarray(d[k]).astype(np.float64)
        if not (np.min(v) >= lo and np.max(v) <= hi): bad.append("range of " + k)
        elif np.any(v != np.floor(v)): bad.append("whole numbers of " + k)
    v = np.asarray(d["th"]).reshape(-1, 16)
    if np.any(v != v[:, :1]): bad.append("equal rows of th in a group")
    return bad
def reference(gn, nb, x, th, a0):
    G = gn.astype(np.int64).reshape(N, 8, 16, GW); H = nb.astype(np.int64).reshape(N, 8, 16, GW); X = x.astype(np.float32).astype(np.int64).reshape(N, 8, 16, XW)
    lim = th.astype(np.int64).reshape(N, 8, 16)[:, :, :1]; a = a0.astype(np.float32).astype(np.int64).reshape(N, 8, 16, L)
    A = np.zeros(N, np.int64); lane = np.arange(L); kk = np.arange(16)[None, :, None]
    for gen in range(GENS):
        h = np.zeros((N, 8, L), np.int64) + S * lane; p = np.zeros((N, 8, L), np.int64); err = np.zeros((N, 8, L), np.int64)
        dau = G[..., ::S].copy()
        for t in range(ST):
            now = np.zeros(N, np.int64)
            for r in range(N):
                q = (r + t) % N; hr = h[r][:, None, :]; pr = p[r]
                n = np.take_along_axis(np.take_along_axis(G[q], hr, 2), pr[:, None, :], 1)[:, 0]
                T = np.abs(np.take_along_axis(X[q], n[:, None, :], 2) - a[r])
                ho = np.take_along_axis(H[q], hr, 2)
                at = ((pr[:, None, :] + kk) & 15) * GW + ho
                e = np.take_along_axis(G[q].reshape(8, 16 * GW), at.reshape(8, 16 * L), 1)
                v = np.take_along_axis(X[q], e[:, None, :], 2).reshape(8, 16, 16, L)
                D = np.add.reduce(np.abs(v + T[:, :, None, :] - 255), axis=1)
                ok = D <= (lim[q] + (A[q] & 63))[:, :, None]
                found = np.any(ok, axis=1); m = np.argmax(ok, axis=1)
                em = np.take_along_axis(e.reshape(8, 16, L), m[:, None, :], 1)[:, 0]; hm = np.take_along_axis(ho, m[:, None, :], 1)[:, 0]
                an = np.where(found[:, None, :], np.take_along_axis(X[q], em[:, None, :], 2), T)
                dau[r, :, t] = np.where(found, em, n); h[r] = np.where(found, hm, h[r]); p[r] = (pr + 1 + np.where(found, m, 0)) & 15
                err[r] = err[r] + np.where(found, 0, 1); now[q] = np.sum(np.where(found, 0, 1)); a[r] = an
                np.put_along_axis(X[q], (16 * lane + p[r])[:, None, :], an, 2)
            A = now
        order = np.argsort(err * L + lane, axis=2)
        best = np.take_along_axis(dau, order[:, :, None, :K], 3)
        come = np.where((np.arange(K) & 1) == 1, np.roll(best, 1, axis=0), best)
        worst = order[:, :, ::-1][:, :, :K]
        np.put_along_axis(G, (S * worst)[:, :, None, :], come, 3)
    return {"yg": G[..., ::S].reshape(N, 128, L).astype(np.float32), "ya": a.reshape(N, 128, L).astype(np.float32), "ys": np.add.reduce(X.reshape(N, 8, 16, L, 16), axis=4).reshape(N, 128, L).astype(np.float32)}

@@ -1,0 +1,556 @@
+from concourse.bass import DstId, RemoteDMATransfer
+from concourse.mybir import AluOpType, ActivationFunctionType
+
+AL, AF = AluOpType, ActivationFunctionType
+NR, L, ST, GENS = 8, 192, 3, 2
+GW, XW = 1536, 3072
+C = 12
+EC, CW = 4, 48
+NC, W, KG = 2, 96, 4
+SM = 4
+VG = "SSSV"
+POOL = {"f32": ("float32", 11000), "bf": ("bfloat16", 28000), "hf": ("float16", 15000), "u16": ("uint16", 4600), "i32": ("int32", 3600)}
+SIZE = {"f32": 4, "bf": 2, "hf": 2, "u16": 2, "i32": 4}
+SCRATCH = {"p_" + k: ("sbuf", [128, v[1]], v[0]) for k, v in POOL.items()}
+SCRATCH.update({"bank%d" % b: ("psum", [128, 512], "float32") for b in range(8)})
+SEMAPHORES = ["sV", "sS", "sP", "sG", "left"] + ["d%d" % i for i in range(10)] + ["r%d" % i for i in range(40)]
+CY = 0.00083
+COST = {"f": 1.25, "gather": 1.56, "scatter": 3.5, "issue": 0.9, "hop": 2.2, "sem": 0.06, "pe": 0.00042}
+
+
+def rank_program(g, core, T, topo):
+    rank = T.rank_of(core)
+    if rank is None:
+        return
+    tasks, used, rings = [], {k: 0 for k in POOL}, {}
+    bank_use = [dict() for _ in range(8)]
+    ndma, nrem = [0], [0]
+
+    def mk(b, lo, n, mut=False, pre=()):
+        return {"b": b, "lo": lo, "n": n, "wr": [], "rd": [], "mut": mut, "pre": pre}
+
+    def tile(pool, n, mut=False):
+        lo, al = used[pool], 32 // SIZE[pool]
+        used[pool] = (lo + n + al - 1) // al * al
+        assert used[pool] <= POOL[pool][1]
+        return mk("p_" + pool, lo, n, mut)
+
+    def ring(pool, n, key):
+        if key not in rings:
+            rings[key] = tile(pool, n)
+        else:
+            o = rings[key]
+            rings[key] = mk(o["b"], o["lo"], n, False, [i for i, _ in o["wr"]] + o["rd"])
+        return rings[key]
+
+    def ps(bank):
+        t = mk("bank%d" % bank, 0, 512)
+        t["bank"] = bank
+        return t
+
+    def ap(t, a=0, b=None, st=1):
+        b = t["n"] if b is None else b
+        buf = T[t["b"]]
+        return buf[:, t["lo"] + a:t["lo"] + b] if st == 1 else buf[:, t["lo"] + a:t["lo"] + b:st]
+
+    def task(q, dur, ins, outs, fn, kind="c", extra=None, boost=0.0):
+        i, deps = len(tasks), {}
+        for t in ins:
+            for w, lag in t["wr"]:
+                deps[w] = max(deps.get(w, 0), lag)
+        for t in outs:
+            for w in t["pre"]:
+                deps.setdefault(w, 0)
+            if t["mut"]:
+                for w, lag in t["wr"]:
+                    deps[w] = max(deps.get(w, 0), lag)
+                for r in t["rd"]:
+                    deps.setdefault(r, 0)
+        for t in list(ins) + list(outs):
+            if "bank" in t:
+                bu = bank_use[t["bank"]]
+                for q2 in list(bu):
+                    if q2 != q:
+                        for j in bu[q2]:
+                            deps.setdefault(j, 0)
+                        bu[q2] = []
+                if i not in bu.setdefault(q, []):
+                    bu[q].append(i)
+        deps.pop(i, None)
+        tasks.append({"q": q, "dur": dur, "deps": deps, "fn": fn, "kind": kind, "x": extra, "soft": set(), "boost": boost})
+        for t in outs:
+            if t["mut"]:
+                t["wr"], t["rd"] = [], []
+            t["wr"].append((i, 0))
+        for t in ins:
+            t["rd"].append(i)
+        return i
+
+    def soft(i, j):
+        if j not in tasks[i]["deps"]:
+            tasks[i]["deps"][j] = 0
+            tasks[i]["soft"].add(j)
+
+    def vc(n, f=1.0):
+        return (0.05 + max(64, n * f) * CY) * COST["f"]
+
+    def gc_(n, k="gather"):
+        return (0.06 + n * COST[k] * CY) * COST["f"]
+
+    def ts(out, oa, in0, s1, op0, s2, op1, ins, n, f=1.0, boost=0.0):
+        def fn():
+            if op1 is None:
+                return [g.vector.tensor_scalar(oa, in0, s1, None, op0)]
+            return [g.vector.tensor_scalar(oa, in0, s1, s2, op0, op1)]
+        return task("V", vc(n, f), ins, [out], fn, boost=boost)
+
+    def tt(out, oa, in0, in1, op, ins, n=0, f=1.0, dur=None, boost=0.0):
+        return task("V", vc(n, f) if dur is None else dur, ins, [out], lambda: [g.vector.tensor_tensor(oa, in0, in1, op)], boost=boost)
+
+    def tcopy(out, oa, in0, ins, n=0, f=1.0, dur=None):
+        return task("V", vc(n, f) if dur is None else dur, ins, [out], lambda: [g.vector.tensor_copy(oa, in0)])
+
+    def act(out, oa, in0, func, ins, n=0, dur=None, bias=0.0, scale=1.0, acc=None, boost=0.0):
+        return task("S", vc(n) if dur is None else dur, ins, [out] + ([acc] if acc else []),
+                    lambda: [g.scalar.activation(oa, in0, func, bias=bias, scale=scale, accum_out=ap(acc) if acc else None)], boost=boost)
+
+    def iota(out, pat, base, cm, flag=True):
+        task("G", 0.13 + 2 * out["n"] * CY, [], [out], lambda: [g.iota(ap(out), pat, base, cm, allow_small_or_imprecise_dtypes=flag)])
+
+    def mms(out, ins, lst, f32=1, boost=0.0, after=None):
+        def fn():
+            r = []
+            for o, l, x, a, b, n in lst:
+                m = g.tensor.matmul(o, l, x, a, b)
+                if b:
+                    r.append(m)
+            return r or [m]
+        i = task("P", (0.03 + sum(max(64, m[5]) for m in lst) * COST["pe"] * f32) * COST["f"], ins, [out], fn, boost=boost)
+        if after:
+            for w, _ in after["wr"][:-1]:
+                soft(i, w)
+        return i
+
+    def load(out, oa, src, dur):
+        i = task("Y", 0.1, [], [out], lambda: [g.sync.dma_start(oa, src)], "d", ndma[0])
+        out["wr"] = [(w, dur if w == i else lg) for w, lg in out["wr"]]
+        ndma[0] += 1
+
+    def store(dst, oa, ins):
+        task("Y", 0.1, ins, [], lambda: [g.sync.dma_start(dst, oa)], "d", ndma[0])
+        ndma[0] += 1
+
+    def engines(a, b):
+        return topo.engines(a, b)[:8]
+
+    def send(src, sa, moves, boost=0.0):
+        got, out, n = [], [], len(moves)
+        trs = []
+        for m, (dst, da, d) in enumerate(moves):
+            to, fr = T.cores[(rank + d) % NR], T.cores[(rank - d) % NR]
+            name = "r%d" % nrem[0]
+            nrem[0] += 1
+            rid, pid, _ = topo.addr(to)
+            es = engines(core, to)
+            es = es[m * len(es) // n:(m + 1) * len(es) // n]
+            trs.append((rid, pid, sum(1 << e for e in es), name, da))
+            got.append((name, len(engines(fr, core)) // n))
+            out.append(len(es))
+
+        def fn():
+            if n == 1:
+                rid, pid, mask, name, da = trs[0]
+                g.remote_dma(da, sa, T.sem[name], T.sem.left, pid, rid, mask)
+            else:
+                g.remote_dma_fused([RemoteDMATransfer(dst_ids=[DstId(rid=rid, pnc=pid)], dma_engine_mask=mask, remote_sem=T.sem[name], src=sa, dst=da)
+                                    for rid, pid, mask, name, da in trs], local_sem=T.sem.left)
+            return []
+        i = task("G", COST["issue"], [src], [], fn, "r", (got, sum(out)), boost)
+        for m, (dst, da, d) in enumerate(moves):
+            dst["wr"].append(((i, m), COST["hop"] + src["n"] * 512 / 60000.0))
+        return i
+
+    gni, nbi, thi = tile("i32", GW), tile("i32", GW), tile("i32", 1)
+    XB = tile("bf", XW + L)
+    X, ext = mk(XB["b"], XB["lo"], XW, True), mk(XB["b"], XB["lo"] + XW, L, True)
+    a = tile("bf", L)
+    load(thi, ap(thi), T.th[:], 1.8)
+    gh = [mk(gni["b"], gni["lo"] + 768 * j, 768) for j in range(2)]
+    for j in range(2):
+        load(gh[j], ap(gh[j]), T.gn[:, 768 * j:768 * j + 768], 2.3 + 0.5 * j)
+    load(nbi, ap(nbi), T.nb[:], 3.8)
+    load(X, ap(X), T.x[:], 4.8)
+    load(a, ap(a), T.a0[:], 4.8)
+    for i in range(1, len(tasks)):
+        soft(i, i - 1)
+
+    def col(ins, src, s1, op0, s2=None, op1=None, n=1, pool="f32", f=1.0):
+        t = tile(pool, n)
+        ts(t, ap(t), src, s1, op0, s2, op1, ins, n, f)
+        return t
+
+    def acol(src, scale, bias):
+        t = tile("f32", src["n"])
+        act(t, ap(t), ap(src), AF.Identity, [src], src["n"], scale=scale, bias=bias)
+        return t
+    ip, ckr, ci = tile("i32", 1), tile("i32", 16), tile("i32", C)
+    im, kpat = tile("f32", 144), tile("bf", 16 * CW)
+    mgf, msf, ii0 = tile("f32", 128), tile("f32", 128), tile("f32", 12)
+    iota(ip, [[0, 1]], 0, 1, False)
+    iota(im, [[1, 144]], 0, 0)
+    iota(kpat, [[0, CW], [1, 16]], 0, 0)
+    iota(mgf, [[1, 8], [0, 16]], 0, 0)
+    iota(ii0, [[16, 12]], 0, 0)
+    iota(ckr, [[-1, 16]], 16, 1, False)
+    iota(ci, [[1, C]], 0, 0, False)
+    iota(msf, [[0, 8], [1, 16]], 0, 0)
+    si = col([ip], ap(ip), 15, AL.bitwise_and, pool="i32")
+    gi = col([ip], ap(ip), 4, AL.arith_shift_right, pool="i32")
+    scol = col([si], ap(si), 0.0, AL.add)
+    zc = col([gi], ap(gi), 16.0, AL.mult, 15.0, AL.add)
+    gcol = col([gi], ap(gi), 0.0, AL.add)
+    pcol = col([ip], ap(ip), 0.0, AL.add)
+    oh0 = col([scol], ap(scol), 0.0, AL.is_equal)
+    k16 = col([scol], ap(scol), 16.0, AL.add)
+    rm3 = col([scol], ap(scol), 3.0, AL.is_ge)
+    mask0 = col([kpat, scol], ap(kpat), ap(scol), AL.is_equal, n=16 * CW, pool="bf", f=0.5)
+    Zh = col([im, zc], ap(im), ap(zc), AL.is_equal, n=144, pool="hf")
+    Zb = col([im, zc], ap(im), ap(zc), AL.is_equal, n=144, pool="bf")
+    Zk = col([Zh, k16], ap(Zh), ap(k16), AL.mult, n=144, pool="hf", f=0.5)
+    Idb = col([im, pcol], ap(im, 0, 128), ap(pcol), AL.is_equal, n=128, pool="bf")
+    Im = col([Idb], ap(Idb), -1.0, AL.mult, n=128, pool="bf", f=0.5)
+    Blk = col([mgf, gcol], ap(mgf), ap(gcol), AL.is_equal, n=128, pool="bf")
+    lt = col([im, pcol], ap(im, 0, 128), ap(pcol), AL.is_gt, n=128, pool="bf")
+    Tri = tile("bf", 128)
+    tt(Tri, ap(Tri), ap(lt), ap(Blk), AL.mult, [lt, Blk], 128, 2)
+    RS = col([im, oh0], ap(im, 0, 128), 0.0, AL.mult, ap(oh0), AL.add, n=128)
+    Idh = col([im, pcol], ap(im, 0, 128), ap(pcol), AL.is_equal, n=128, pool="hf")
+    Lt = []
+    for t in range(ST):
+        eq = col([msf], ap(msf), float(t), AL.is_equal, n=128, pool="bf")
+        Lt.append(tile("hf", 128))
+        tt(Lt[t], ap(Lt[t]), ap(eq), ap(Blk), AL.mult, [eq, Blk], 128, 2)
+    cki = col([ckr], ap(ckr), 15, AL.bitwise_and, n=16, pool="i32")
+    ck = col([cki], ap(cki), 0.0, AL.add, n=16)
+    cidx = tile("u16", C)
+    tcopy(cidx, ap(cidx), ap(ci), [ci], C)
+    ii = col([ii0, scol], ap(ii0), ap(scol), AL.add, n=12)
+    hU0, I2, xi = acol(ii, 8.0, -1536.0), acol(ii, 1.0, 1536.0), acol(ii, 16.0, 0.0)
+    i48, i144, one = acol(ii, 1.0, 48.0), acol(ii, -1.0, 144.0), acol(ii, 0.0, 1.0)
+    ones = tile("bf", L)
+    act(ones, ap(ones), ap(kpat, 0, L), AF.Identity, [kpat], L, scale=0.0, bias=1.0)
+    thf = col([thi], ap(thi), 0.0, AL.add)
+    own_nb = ap(nbi, 0, GW, 8)
+    El0 = tile("u16", L)
+    tcopy(El0, ap(El0), own_nb, [nbi], L)
+    NBh0 = col([nbi], own_nb, -1536.0, AL.add, n=L)
+    G = tile("f32", GW)
+    for j in range(2):
+        ts(G, ap(G, 768 * j, 768 * j + 768), ap(gh[j]), -1536.0, AL.add, None, None, [gh[j]], 768)
+    G["mut"] = True
+    NBf = tile("f32", GW)
+    for j in range(4):
+        ts(NBf, ap(NBf, 384 * j, 384 * j + 384), ap(nbi, 384 * j, 384 * j + 384), -1536.0, AL.add, None, None, [nbi], 384)
+    own = tile("f32", 48 + L)
+    act(own, ap(own, 48, 48 + L), ap(G, 0, GW, 8), AF.Copy, [G], L)
+
+    def Z(z, k):
+        return ap(z, 15 - k, 143 - k)
+
+    lim = thf
+    for gen in range(GENS):
+        mo, mother = tile("hf", L), tile("hf", L)
+        imo = ts(mo, ap(mo), ap(own, 48, 48 + L), ap(rm3), AL.mult, None, None, [own, rm3], L, boost=-30)
+        send(mo, ap(mo), [(mother, ap(mother), 2)], boost=-30)
+        hp = None
+        vs, fs = [], []
+        for t in range(ST):
+            last = t == ST - 1
+            nM = tile("hf", L)
+            if t == 0:
+                NBh, El, mask = NBh0, El0, mask0
+                inM = ts(nM, ap(nM), ap(G, 0, GW, 8), ap(oh0), AL.mult, None, None, [G, oh0], L)
+                hU, hUa, pw1 = hU0, ap(hU0), one
+            else:
+                PM = tile("bf", L)
+                tt(PM, ap(PM), ap(hp, 0, C).indirect(ap(cidx)), ap(mask0, 0, L), AL.mult, [hp, cidx, mask0], dur=gc_(L))
+                pr = ps(1)
+                mms(pr, [PM, Blk], [(ap(pr, 0, L), ap(Blk), ap(PM), True, True, L)])
+                prb = tile("bf", L)
+                act(prb, ap(prb), ap(pr, 0, L), AF.Copy, [pr], L)
+                hl = tile("u16", C)
+                ts(hl, ap(hl), ap(hp, C, 2 * C), 1536.0, AL.add, None, None, [hp], C, boost=50)
+                NBh, El = tile("f32", L), tile("u16", L)
+                act(NBh, ap(NBh), ap(NBf).indirect(ap(hl)), AF.Copy, [NBf, hl], dur=gc_(L), boost=50)
+                ts(El, ap(El), ap(NBh), 1536.0, AL.add, None, None, [NBh], L, boost=50)
+                mask = ring("bf", 16 * L, "mask")
+                for k in range(16 - SM, 16):
+                    ab = ring("bf", L, ("ab", k))
+                    act(ab, ap(ab), ap(prb), AF.Abs, [prb, ck], L, scale=-1.0, bias=ap(ck, k, k + 1))
+                    act(mask, ap(mask, k, 16 * L, 16), ap(ab), AF.Relu, [ab], L, scale=-1.0, bias=1.0)
+                for k in range(16 - SM):
+                    ts(mask, ap(mask, k, 16 * L, 16), ap(prb), ap(ck, k, k + 1), AL.is_equal, None, None, [prb, ck], L, 0.5)
+                inM = tt(nM, ap(nM), ap(G).indirect(ap(hl)), ap(mask, 0, 16 * L, 16), AL.mult, [G, hl, mask], dur=gc_(L))
+                hU, hUa, pw1 = hp, ap(hp, C, 2 * C), tile("f32", C)
+                act(pw1, ap(pw1), ap(hp, 0, C), AF.Identity, [hp], C, bias=1.0)
+            V, Vj, iG, iW = ring("bf", 16 * L, "V"), [], [], []
+            Wp = ps(0)
+            for j in range(EC):
+                Gg, c0, c1 = ring("hf", 16 * CW, ("Gg", j)), j * CW, j * CW + CW
+                m0 = 0 if t == 0 else 16 * c0
+                iG.append(tt(Gg, ap(Gg), ap(G).indirect(ap(El, c0, c1)), ap(mask, m0, m0 + 16 * CW), AL.mult, [G, El, mask], dur=gc_(16 * CW)))
+                iWm = mms(Wp, [Gg, Zh], [(ap(Wp, c0, c1), Z(Zh, k), ap(Gg, k, 16 * CW, 16), k == 0, k == 15, CW) for k in range(16)])
+                Wl = tile("u16", CW)
+                iW.append(ts(Wl, ap(Wl), ap(Wp, c0, c1), 1536.0, AL.add, None, None, [Wp], CW, boost=50))
+                Vv = mk(V["b"], V["lo"] + 16 * c0, 16 * CW, False, V["pre"])
+                if VG[j] == "V":
+                    tcopy(Vv, ap(Vv), ap(X).indirect(ap(Wl)), [X, Wl], dur=gc_(16 * CW))
+                else:
+                    act(Vv, ap(Vv), ap(X).indirect(ap(Wl)), AF.Copy, [X, Wl], dur=gc_(16 * CW))
+                V["wr"] += Vv["wr"]
+                Vj.append(Vv)
+                if j == 0:
+                    npz, dq = ps(1), ps(7)
+                    mms(npz, [nM, Zh], [(ap(npz, 0, C), Z(Zh, r), ap(nM, r, L, 16), r == 0, r == 15, C) for r in range(16)])
+                    nl, df = tile("u16", C), tile("bf", L)
+                    inl = ts(nl, ap(nl), ap(npz, 0, C), 1536.0, AL.add, None, None, [npz], C, boost=50)
+                    act(df, ap(df), ap(X).indirect(ap(nl)), AF.Copy, [X, nl], dur=gc_(L), boost=50)
+                    mms(dq, [df, a, Idb, Im], [(ap(dq, 0, L), ap(Idb), ap(df), True, False, L), (ap(dq, 0, L), ap(Im), ap(a), False, True, L)], boost=50)
+                    act(ext, ap(ext), ap(dq, 0, L), AF.Abs, [dq], L, boost=50)
+            seq = [iG[0], inM, iW[0], iG[1], inl, iW[1], iG[2], iW[2], iG[3], iW[3]]
+            if t == 0:
+                soft(imo, iG[0])
+            for u, v in zip(seq, seq[1:]):
+                soft(v, u)
+            FI, Q, ok = tile("hf", L), tile("hf", 2 * L), tile("bf", L)
+            for y in range(NC):
+                i0, i1 = y * W, y * W + W
+                Dp = ps(2 + y)
+                D = ap(Dp, 0, W)
+                Te = ap(ext, i0, i1)
+                vin = [Vj[j] for j in range(EC) if i0 <= j * CW < i1]
+                for q in range(16 // KG):
+                    Y, lst, dl = ps(4 + (y * 4 + q) % 3), [], []
+                    ya = ring("bf", KG * W, ("ya", y, q))
+                    for kk in range(KG):
+                        k = q * KG + kk
+                        o, v = ap(Y, kk * W, kk * W + W), ap(V, 16 * i0 + k, 16 * i1, 16)
+                        lst += [(o, ap(Idb), v, True, False, W), (o, ap(Idb), Te, False, True, W)]
+                        dl.append((D, Z(Zb, k), ap(ya, kk * W, kk * W + W), k == 0, k == 15, W))
+                    mms(Y, vin + [Idb, ext], lst)
+                    act(ya, ap(ya), ap(Y, 0, KG * W), AF.Abs, [Y], KG * W, bias=-255.0)
+                    soft(mms(Dp, [ya, Zb], dl, after=Dp, boost=20), iWm)
+                ts(ok, ap(ok, i0, i1), D, ap(lim), AL.is_le, None, None, [Dp, lim], W, boost=20)
+                oky = mk(ok["b"], ok["lo"] + i0, W)
+                oky["wr"] = ok["wr"][-1:]
+                Cp = ps(2 + y)
+                mms(Cp, [oky, Tri], [(ap(Cp, 0, W), ap(Tri), ap(oky), True, True, W)], boost=20)
+                tt(FI, ap(FI, i0, i1), ap(Cp, 0, W), ap(oky), AL.is_lt, [Cp, oky], W, boost=20)
+                FIy = mk(FI["b"], FI["lo"] + i0, W)
+                FIy["wr"] = FI["wr"][-1:]
+                tt(Q, ap(Q, i0, i1), ap(FIy), ap(NBh, i0, i1), AL.mult, [FIy, NBh], W, 2)
+                tt(Q, ap(Q, L + i0, L + i1), ap(Wp, i0, i1), ap(FIy), AL.mult, [FIy, Wp], W)
+            cp = ps(1)
+            mms(cp, [FI, Zk], [(ap(cp, 0, C), Z(Zk, r), ap(FI, r, L, 16), r == 0, r == 15, C) for r in range(16)])
+            x1, x2, nf = tile("i32", C), tile("i32", C), tile("f32", C)
+            icode = tt(x1, ap(x1), ap(cp, 0, C), ap(pw1, 0, C), AL.add, [cp, pw1], C)
+            ts(x2, ap(x2), ap(x1), 15, AL.bitwise_and, None, None, [x1], C)
+            soft(ts(nf, ap(nf), ap(cp, 0, C), 16.0, AL.is_lt, None, None, [cp], C), icode)
+            Qp, Qe = ps(7), ps(3)
+            for Qx, o in ((Qp, 0), (Qe, L)):
+                if Qx is Qe or not last:
+                    Qs = mk(Q["b"], Q["lo"] + o, L)
+                    Qs["wr"] = Q["wr"][o // L::2]
+                    mms(Qx, [Qs, Zh], [(ap(Qx, 0, C), Z(Zh, r), ap(Qs, r, L, 16), r == 0, r == 15, C) for r in range(16)])
+            if not last:
+                Uh, ho, hp = tile("f32", C), tile("f32", 2 * C), tile("f32", 2 * C)
+                tcopy(ho, ap(ho, 0, C), ap(x2), [x2], C)
+                tt(Uh, ap(Uh), ap(nf), hUa, AL.mult, [nf, hU], C)
+                tt(ho, ap(ho, C, 2 * C), ap(Qp, 0, C), ap(Uh), AL.add, [Qp, Uh], C)
+                send(ho, ap(ho), [(hp, ap(hp), 1)])
+            Ue, Re, Ll = tile("f32", C), tile("f32", C), tile("u16", C)
+            tt(Ue, ap(Ue), ap(nf), ap(I2), AL.mult, [nf, I2], C)
+            tt(Re, ap(Re), ap(Qe, 0, C), ap(Ue), AL.add, [Qe, Ue], C)
+            iL = ts(Ll, ap(Ll), ap(Re), 1536.0, AL.add, None, None, [Re], C)
+            an, a2 = tile("bf", L), tile("bf", L)
+            act(an, ap(an), ap(XB).indirect(ap(Ll)), AF.Copy, [X, ext, Ll], dur=gc_(L))
+            ian = send(an, ap(an), [(a2, ap(a2), 1 if not last else -2)])
+            cn = ps(4)
+            mms(cn, [ok, Blk], [(ap(cn, 0, L), ap(Blk), ap(ok), True, True, L)], boost=40 if last else 0)
+            fl, acc, P4 = tile("bf", L), tile("f32", 1), tile("hf", L)
+            act(fl, ap(fl), ap(cn, 0, L), AF.Relu, [cn], L, scale=-1.0, bias=1.0, acc=acc)
+            iP4 = tt(P4, ap(P4), ap(fl), ap(nM), AL.mult, [fl, nM], L, 2)
+            if not last:
+                soft(iP4, iL)
+                vn, vi, fi = tile("hf", L), tile("hf", L), tile("bf", L)
+                tt(vn, ap(vn), ap(P4), ap(Q, L, 2 * L), AL.add, [P4, Q], L, 2)
+                soft(send(fl, ap(fl), [(fi, ap(fi), 2 - t)]), ian)
+                send(vn, ap(vn), [(vi, ap(vi), 2 - t)])
+                vs.append([(vi, 0)])
+                fs.append(fi)
+            else:
+                vs.append([(P4, 0), (Q, L)])
+                fs.append(fl)
+            pf, pl = tile("f32", C), tile("u16", C)
+            tt(pf, ap(pf), ap(x2), ap(xi), AL.add, [x2, xi], C)
+            tcopy(pl, ap(pl), ap(pf), [pf], C)
+
+            def put(pl=pl, an=an):
+                return [g.vector.tensor_copy(ap(X).indirect(ap(pl)), ap(an))]
+            iput = task("V", gc_(L, "scatter"), [pl, an], [X], put)
+            if not (gen == GENS - 1 and last):
+                Ap = ps(0)
+                mms(Ap, [acc, RS], [(ap(Ap, 0, 1), ap(RS), ap(acc), True, True, 1)], 4)
+                A1, A2, lim = tile("i32", 1), tile("i32", 1), tile("f32", 1)
+                soft(tcopy(A1, ap(A1), ap(Ap, 0, 1), [Ap], 1), iL)
+                ts(A2, ap(A2), ap(A1), 63, AL.bitwise_and, None, None, [A1], 1)
+                ts(lim, ap(lim), ap(A2), ap(thf), AL.add, None, None, [A2, thf], 1)
+            a = a2
+        Ep = ps(5)
+        mms(Ep, fs + [Idb], [(ap(Ep, 0, L), ap(Idb), ap(fs[t]), t == 0, t == ST - 1, L) for t in range(ST)], boost=40)
+        oh, cum = tile("bf", L), tile("bf", L)
+        ts(oh, ap(oh), ap(Ep, 0, L), ap(scol), AL.is_equal, None, None, [Ep, scol], L, boost=40)
+
+        def scan(oh=oh, cum=cum):
+            return [g.vector.tensor_tensor_scan(ap(cum), ap(ones), ap(oh), 0.0, AL.mult, AL.add)]
+        task("V", vc(L, 0.5), [oh, ones], [cum], scan, boost=40)
+        bp = ps(5)
+        mms(bp, [cum, Tri], [(ap(bp, 0, 1), ap(Tri), ap(cum, L - 1, L), True, True, 1)], boost=40)
+        q1, q2 = tile("bf", L), tile("bf", L)
+        tt(q1, ap(q1), ap(oh), ap(cum), AL.mult, [oh, cum], L, 2, boost=40)
+        iq2 = ts(q2, ap(q2), ap(oh), ap(bp, 0, 1), AL.mult, None, None, [oh, bp], L, 0.5, boost=40)
+        soft(iP4, iq2)
+        soft(icode, iP4)
+        op_ = ps(7)
+        for q in (q1, q2):
+            mms(op_, [q, Zb], [(ap(op_, 0, 12), Z(Zb, r), ap(q, r, L, 16), r == 0 and q is q1, r == 15 and q is q2, 12) for r in range(16)], boost=40, after=op_)
+        po = tile("u16", 12)
+        ts(po, ap(po), ap(op_, 0, 12), -1.0, AL.add, None, None, [op_], 12)
+        dp, lst = ps(6), [(ap(Idh), ap(mother))]
+        for t in range(ST):
+            lst += [(ap(Lt[t]), ap(v, o, o + L)) for v, o in vs[t]]
+        lst = [(ap(dp, 0, L), l, r, j == 0, j == len(lst) - 1, L) for j, (l, r) in enumerate(lst)]
+        mms(dp, [mother, Idh] + Lt + [v for w in vs for v, _ in w], lst)
+        dau, srt = tile("f32", L), tile("f32", L)
+        act(dau, ap(dau), ap(dp, 0, L), AF.Copy, [dp], L)
+
+        def scat(srt=srt, po=po, dau=dau):
+            return [g.vector.tensor_copy(ap(srt).indirect(ap(po)), ap(dau))]
+        y1, y2, y3, y4 = tile("f32", 12), tile("f32", 12), tile("f32", 12), tile("f32", 12)
+        ts(y1, ap(y1), ap(op_, 0, 12), 145.0, AL.is_ge, None, None, [op_], 12)
+        tt(y2, ap(y2), ap(i144), ap(op_, 0, 12), AL.subtract, [i144, op_], 12)
+        tt(y3, ap(y3), ap(y1), ap(y2), AL.mult, [y1, y2], 12)
+        iy4 = tt(y4, ap(y4), ap(y3), ap(i48), AL.add, [y3, i48], 12)
+        Lm, Ln, prev = tile("f32", 12), tile("u16", 12), tile("f32", 48)
+        send(y4, ap(y4), [(Lm, ap(Lm), -2)])
+        isc = task("V", gc_(L, "scatter"), [po, dau], [srt], scat)
+        soft(isc, iy4)
+        soft(iput, isc)
+        best = mk(srt["b"], srt["lo"], 48)
+        best["wr"] = srt["wr"]
+        soft(ian, send(best, ap(best), [(own, ap(own, 0, 48), -2), (prev, ap(prev), -1)]))
+        tcopy(Ln, ap(Ln), ap(Lm), [Lm], 12)
+        own2 = mk(own["b"], own["lo"], own["n"])
+        own2["wr"] = list(own["wr"])
+        tcopy(own2, ap(own, 1, 48, 2), ap(prev, 1, 48, 2), [own, prev], 24)
+        new = tile("f32", 48 + L)
+        tcopy(new, ap(new, 48, 48 + L), ap(own).indirect(ap(Ln)), [own2, Ln], dur=gc_(L))
+        if gen < GENS - 1:
+            tcopy(G, ap(G, 0, GW, 8), ap(new, 48, 48 + L), [new], L)
+        own = new
+    yo, ao, so = tile("f32", L), tile("f32", L), tile("f32", L)
+    act(yo, ap(yo), ap(own, 48, 48 + L), AF.Copy, [own], L, bias=1536.0)
+    store(T.yg[:], ap(yo), [yo])
+    act(ao, ap(ao), ap(a), AF.Copy, [a], L)
+    store(T.ya[:], ap(ao), [ao])
+    sp = ps(0)
+    mms(sp, [X, Idb], [(ap(sp, 0, L), ap(Idb), ap(X, s, XW, 16), s == 0, s == 15, L) for s in range(16)])
+    act(so, ap(so), ap(sp, 0, L), AF.Copy, [sp], L)
+    store(T.ys[:], ap(so), [so])
+    emit(g, T, tasks)
+
+
+def tid(d):
+    return d[0] if isinstance(d, tuple) else d
+
+
+def order(tasks):
+    n = len(tasks)
+    succ, left = [[] for _ in range(n)], [0] * n
+    for i, t in enumerate(tasks):
+        for d, lag in t["deps"].items():
+            succ[tid(d)].append((i, lag))
+        left[i] = len(t["deps"])
+    need, topo_order = list(left), [i for i in range(n) if not left[i]]
+    for i in topo_order:
+        for j, _ in succ[i]:
+            need[j] -= 1
+            if not need[j]:
+                topo_order.append(j)
+    assert len(topo_order) == n
+    prio = [0.0] * n
+    for i in reversed(topo_order):
+        prio[i] = tasks[i]["dur"] + max([prio[j] + COST["sem"] + lag for j, lag in succ[i]], default=0.0)
+    free, fin, out = {}, [0.0] * n, []
+    avail = {i: 0.0 for i in range(n) if not left[i]}
+    while avail:
+        st, _, i = min((max(r, free.get(tasks[i]["q"], 0.0)), -prio[i] - tasks[i]["boost"], i) for i, r in avail.items())
+        del avail[i]
+        fin[i] = free[tasks[i]["q"]] = st + tasks[i]["dur"]
+        out.append(i)
+        for j, _ in succ[i]:
+            left[j] -= 1
+            if not left[j]:
+                avail[j] = max(fin[tid(d)] + lag + COST["sem"] for d, lag in tasks[j]["deps"].items())
+    return out
+
+
+def emit(g, T, tasks):
+    eng = {"V": g.vector, "S": g.scalar, "P": g.tensor, "G": g, "Y": g.sync}
+    sem_of = {"V": "sV", "S": "sS", "P": "sP", "G": "sG"}
+    count = {s: 0 for s in sem_of.values()}
+    known, done = {q: {} for q in eng}, {}
+    sent, ends = 0, []
+    for i in order(tasks):
+        t = tasks[i]
+        q = t["q"]
+        k, need = known[q], {}
+        for d in t["deps"]:
+            if d in t["soft"]:
+                continue
+            s, v, kn = done[d]
+            if k.get(s, 0) < v and need.get(s, (0, None))[0] < v:
+                need[s] = (v, kn)
+        for s in sorted(need, key=lambda s: -len(need[s][1])):
+            v, kn = need[s]
+            if k.get(s, 0) >= v or any(o != s and need[o][1].get(s, 0) >= v and k.get(o, 0) < need[o][0] for o in need):
+                continue
+            eng[q].wait_ge(T.sem[s], v)
+            for b, w in kn.items():
+                k[b] = max(k.get(b, 0), w)
+            k[s] = max(v, k.get(s, 0))
+        for s, (v, kn) in need.items():
+            if k.get(s, 0) < v:
+                eng[q].wait_ge(T.sem[s], v)
+                k[s] = v
+        ins = t["fn"]()
+        if t["kind"] == "c":
+            s = sem_of[q]
+            for m in ins:
+                m.then_inc(T.sem[s], 1)
+            count[s] += len(ins)
+            done[i] = (s, count[s], dict(k))
+        elif t["kind"] == "d":
+            s = "d%d" % t["x"]
+            ins[0].then_inc(T.sem[s], 16)
+            done[i] = (s, 16, dict(k))
+            ends.append((s, 16))
+        else:
+            got, out = t["x"]
+            sent += out
+            for m, (name, c) in enumerate(got):
+                done[(i, m)] = (name, c, {})
+                ends.append((name, c))
+    for s, v in ends + [("left", sent)] + list(count.items()):
+        if known["Y"].get(s, 0) < v:
+            g.sync.wait_ge(T.sem[s], v)

@@ -5,46 +5,43 @@ AL, AF = AluOpType, ActivationFunctionType
 NR, L, ST, GENS = 8, 192, 3, 2
 GW, XW = 1536, 3072
 C = 12
-EC, CW = 4, 48
-NC, W, KG = 2, 96, 4
-SM = 4
-VG = "SSSV"
-POOL = {"f32": ("float32", 11000), "bf": ("bfloat16", 28000), "hf": ("float16", 15000), "u16": ("uint16", 4600), "i32": ("int32", 3600)}
+CFG = {"halves": [(0, 96, (32, 32, 32)), (96, 96, (32, 32, 32))],
+       "rec": {0: "SSSSSV", 1: "SSSSSS", 2: "SSSSSS"},
+       "kg": 4, "passes": 4}
+PLAN = {"step": 14.0, "half": 5.5, "end": 6.0, "lists": (0, 0), "names": (1.35, 0.95), "records": (2.4, 0.95), "sums": (6.5, 0.4),
+        "first": (8.5, 0), "put": (11.0, 0), "info": (11.5, 0)}
+POOL = {"f32": ("float32", 7000), "bf": ("bfloat16", 48000), "hf": ("float16", 30000), "u16": ("uint16", 6000), "i32": ("int32", 3600)}
 SIZE = {"f32": 4, "bf": 2, "hf": 2, "u16": 2, "i32": 4}
 SCRATCH = {"p_" + k: ("sbuf", [128, v[1]], v[0]) for k, v in POOL.items()}
 SCRATCH.update({"bank%d" % b: ("psum", [128, 512], "float32") for b in range(8)})
-SEMAPHORES = ["sV", "sS", "sP", "sG", "left"] + ["d%d" % i for i in range(10)] + ["r%d" % i for i in range(40)]
+SEMAPHORES = ["sV", "sS", "sP", "sG", "left"] + ["d%d" % i for i in range(16)] + ["r%d" % i for i in range(60)]
 CY = 0.00083
-COST = {"f": 1.25, "gather": 1.56, "scatter": 3.5, "issue": 0.9, "hop": 2.2, "sem": 0.06, "pe": 0.00042}
+COST = {"f": 1.25, "fix": 0.0, "gather": 1.56, "scatter": 3.5, "issue": 0.9, "hop": 1.9, "sem": 0.12, "own": 0.0, "pe": 0.00042}
+NOTE, ORDER = [""], []
 
 
 def rank_program(g, core, T, topo):
     rank = T.rank_of(core)
     if rank is None:
         return
-    tasks, used, rings = [], {k: 0 for k in POOL}, {}
-    bank_use = [dict() for _ in range(8)]
-    ndma, nrem = [0], [0]
+    tasks, used = [], {k: 0 for k in POOL}
+    bank_use = [{"q": None, "now": [], "before": []} for _ in range(8)]
+    ndma, nrem, lab, turn = [0], [0], [""], [0.0]
 
-    def mk(b, lo, n, mut=False, pre=()):
-        return {"b": b, "lo": lo, "n": n, "wr": [], "rd": [], "mut": mut, "pre": pre}
+    def mk(b, lo, n, mut=False):
+        return {"b": b, "lo": lo, "n": n, "wr": [], "rd": [], "mut": mut}
 
     def tile(pool, n, mut=False):
         lo, al = used[pool], 32 // SIZE[pool]
         used[pool] = (lo + n + al - 1) // al * al
-        assert used[pool] <= POOL[pool][1]
+        assert used[pool] <= POOL[pool][1], pool
         return mk("p_" + pool, lo, n, mut)
 
-    def ring(pool, n, key):
-        if key not in rings:
-            rings[key] = tile(pool, n)
-        else:
-            o = rings[key]
-            rings[key] = mk(o["b"], o["lo"], n, False, [i for i, _ in o["wr"]] + o["rd"])
-        return rings[key]
+    def part(t, a, n):
+        return mk(t["b"], t["lo"] + a, n)
 
-    def ps(bank):
-        t = mk("bank%d" % bank, 0, 512)
+    def ps(bank, lo=0, n=512):
+        t = mk("bank%d" % bank, lo, n)
         t["bank"] = bank
         return t
 
@@ -59,8 +56,6 @@ def rank_program(g, core, T, topo):
             for w, lag in t["wr"]:
                 deps[w] = max(deps.get(w, 0), lag)
         for t in outs:
-            for w in t["pre"]:
-                deps.setdefault(w, 0)
             if t["mut"]:
                 for w, lag in t["wr"]:
                     deps[w] = max(deps.get(w, 0), lag)
@@ -69,15 +64,13 @@ def rank_program(g, core, T, topo):
         for t in list(ins) + list(outs):
             if "bank" in t:
                 bu = bank_use[t["bank"]]
-                for q2 in list(bu):
-                    if q2 != q:
-                        for j in bu[q2]:
-                            deps.setdefault(j, 0)
-                        bu[q2] = []
-                if i not in bu.setdefault(q, []):
-                    bu[q].append(i)
+                if bu["q"] != q:
+                    bu.update(q=q, now=[], before=bu["now"])
+                for j in bu["before"]:
+                    deps.setdefault(j, 0)
+                bu["now"].append(i)
         deps.pop(i, None)
-        tasks.append({"q": q, "dur": dur, "deps": deps, "fn": fn, "kind": kind, "x": extra, "soft": set(), "boost": boost})
+        tasks.append({"q": q, "dur": dur, "deps": deps, "fn": fn, "kind": kind, "x": extra, "soft": set(), "turn": turn[0] - boost, "lab": lab[0]})
         for t in outs:
             if t["mut"]:
                 t["wr"], t["rd"] = [], []
@@ -92,380 +85,412 @@ def rank_program(g, core, T, topo):
             tasks[i]["soft"].add(j)
 
     def vc(n, f=1.0):
-        return (0.05 + max(64, n * f) * CY) * COST["f"]
+        return (COST["fix"] + max(64, n * f) * CY) * COST["f"]
 
     def gc_(n, k="gather"):
         return (0.06 + n * COST[k] * CY) * COST["f"]
 
-    def ts(out, oa, in0, s1, op0, s2, op1, ins, n, f=1.0, boost=0.0):
+    def ts(out, oa, in0, s1, op0, s2, op1, ins, n, f=1.0, boost=0.0, dur=None):
         def fn():
             if op1 is None:
                 return [g.vector.tensor_scalar(oa, in0, s1, None, op0)]
             return [g.vector.tensor_scalar(oa, in0, s1, s2, op0, op1)]
-        return task("V", vc(n, f), ins, [out], fn, boost=boost)
+        return task("V", vc(n, f) if dur is None else dur, ins, [out], fn, boost=boost)
 
     def tt(out, oa, in0, in1, op, ins, n=0, f=1.0, dur=None, boost=0.0):
         return task("V", vc(n, f) if dur is None else dur, ins, [out], lambda: [g.vector.tensor_tensor(oa, in0, in1, op)], boost=boost)
 
-    def tcopy(out, oa, in0, ins, n=0, f=1.0, dur=None):
-        return task("V", vc(n, f) if dur is None else dur, ins, [out], lambda: [g.vector.tensor_copy(oa, in0)])
+    def tcopy(out, oa, in0, ins, n=0, f=1.0, dur=None, boost=0.0):
+        return task("V", vc(n, f) if dur is None else dur, ins, [out], lambda: [g.vector.tensor_copy(oa, in0)], boost=boost)
 
     def act(out, oa, in0, func, ins, n=0, dur=None, bias=0.0, scale=1.0, acc=None, boost=0.0):
-        return task("S", vc(n) if dur is None else dur, ins, [out] + ([acc] if acc else []),
+        return task("S", (vc(n) if dur is None else dur) + (0.02 if acc else 0), ins, [out] + ([acc] if acc else []),
                     lambda: [g.scalar.activation(oa, in0, func, bias=bias, scale=scale, accum_out=ap(acc) if acc else None)], boost=boost)
 
     def iota(out, pat, base, cm, flag=True):
-        task("G", 0.13 + 2 * out["n"] * CY, [], [out], lambda: [g.iota(ap(out), pat, base, cm, allow_small_or_imprecise_dtypes=flag)])
+        task("G", 0.16 + 2.5 * out["n"] * CY, [], [out], lambda: [g.iota(ap(out), pat, base, cm, allow_small_or_imprecise_dtypes=flag)])
 
-    def mms(out, ins, lst, f32=1, boost=0.0, after=None):
+    def mms(outs, ins, groups, n, boost=0.0, after=None, ends=(True, True)):
         def fn():
             r = []
-            for o, l, x, a, b, n in lst:
-                m = g.tensor.matmul(o, l, x, a, b)
-                if b:
-                    r.append(m)
-            return r or [m]
-        i = task("P", (0.03 + sum(max(64, m[5]) for m in lst) * COST["pe"] * f32) * COST["f"], ins, [out], fn, boost=boost)
+            for gr in groups:
+                for j, (o, l, x) in enumerate(gr):
+                    m = g.tensor.matmul(o, l, x, ends[0] and j == 0, ends[1] and j == len(gr) - 1)
+                r.append(m)
+            return r
+        i = task("P", (0.04 + n * COST["pe"]) * COST["f"], ins, outs, fn, boost=boost)
         if after:
             for w, _ in after["wr"][:-1]:
                 soft(i, w)
         return i
 
-    def load(out, oa, src, dur):
-        i = task("Y", 0.1, [], [out], lambda: [g.sync.dma_start(oa, src)], "d", ndma[0])
+    def load(out, oa, src, dur, q="Y"):
+        i = task(q, 0.05, [], [out], lambda: [(g.sync if q == "Y" else g.scalar).dma_start(oa, src)], "d", ndma[0], boost=1000)
         out["wr"] = [(w, dur if w == i else lg) for w, lg in out["wr"]]
         ndma[0] += 1
+        return i
 
     def store(dst, oa, ins):
-        task("Y", 0.1, ins, [], lambda: [g.sync.dma_start(dst, oa)], "d", ndma[0])
+        task("Y", 2.0, ins, [], lambda: [g.sync.dma_start(dst, oa)], "d", ndma[0])
         ndma[0] += 1
 
     def engines(a, b):
         return topo.engines(a, b)[:8]
 
-    def send(src, sa, moves, boost=0.0):
-        got, out, n = [], [], len(moves)
-        trs = []
-        for m, (dst, da, d) in enumerate(moves):
+    def send(moves, boost=0.0):
+        got, out, n, trs = [], [], len(moves), []
+        for m, (src, sa, dst, da, d) in enumerate(moves):
             to, fr = T.cores[(rank + d) % NR], T.cores[(rank - d) % NR]
             name = "r%d" % nrem[0]
             nrem[0] += 1
             rid, pid, _ = topo.addr(to)
             es = engines(core, to)
             es = es[m * len(es) // n:(m + 1) * len(es) // n]
-            trs.append((rid, pid, sum(1 << e for e in es), name, da))
+            trs.append((rid, pid, sum(1 << e for e in es), name, sa, da))
             got.append((name, len(engines(fr, core)) // n))
             out.append(len(es))
 
         def fn():
             if n == 1:
-                rid, pid, mask, name, da = trs[0]
+                rid, pid, mask, name, sa, da = trs[0]
                 g.remote_dma(da, sa, T.sem[name], T.sem.left, pid, rid, mask)
             else:
                 g.remote_dma_fused([RemoteDMATransfer(dst_ids=[DstId(rid=rid, pnc=pid)], dma_engine_mask=mask, remote_sem=T.sem[name], src=sa, dst=da)
-                                    for rid, pid, mask, name, da in trs], local_sem=T.sem.left)
+                                    for rid, pid, mask, name, sa, da in trs], local_sem=T.sem.left)
             return []
-        i = task("G", COST["issue"], [src], [], fn, "r", (got, sum(out)), boost)
-        for m, (dst, da, d) in enumerate(moves):
-            dst["wr"].append(((i, m), COST["hop"] + src["n"] * 512 / 60000.0))
+        i = task("G", COST["issue"], [m[0] for m in moves], [], fn, "r", (got, sum(out)), boost)
+        for m, (src, sa, dst, da, d) in enumerate(moves):
+            dst["wr"].append(((i, m), COST["hop"] + n * dst["n"] * SIZE[dst["b"][2:]] * 128 / 60000.0))
         return i
 
+    HV, KG = CFG["halves"], CFG["kg"]
     gni, nbi, thi = tile("i32", GW), tile("i32", GW), tile("i32", 1)
-    XB = tile("bf", XW + L)
-    X, ext = mk(XB["b"], XB["lo"], XW, True), mk(XB["b"], XB["lo"] + XW, L, True)
-    a = tile("bf", L)
-    load(thi, ap(thi), T.th[:], 1.8)
-    gh = [mk(gni["b"], gni["lo"] + 768 * j, 768) for j in range(2)]
-    for j in range(2):
-        load(gh[j], ap(gh[j]), T.gn[:, 768 * j:768 * j + 768], 2.3 + 0.5 * j)
-    load(nbi, ap(nbi), T.nb[:], 3.8)
-    load(X, ap(X), T.x[:], 4.8)
-    load(a, ap(a), T.a0[:], 4.8)
-    for i in range(1, len(tasks)):
-        soft(i, i - 1)
+    X, a0 = tile("bf", XW, True), tile("bf", L)
+    NG = 4
+    gh = [part(gni, GW // NG * j, GW // NG) for j in range(NG)]
+    nh = [part(nbi, 8 * i0, 8 * W) for i0, W, _ in HV]
+    seq = [load(gh[j], ap(gh[j]), T.gn[:, GW // NG * j:GW // NG * (j + 1)], 2.2 + 0.6 * j) for j in range(NG)]
+    seq.append(load(nh[0], ap(nh[0]), T.nb[:, 0:nh[0]["n"]], 5.2))
+    seq.append(load(X, ap(X), T.x[:], 7.6))
+    seq.append(load(nh[1], ap(nh[1]), T.nb[:, nh[0]["n"]:GW], 8.8))
+    for u, v in zip(seq, seq[1:]):
+        soft(v, u)
+    load(thi, ap(thi), T.th[:], 2.0, "S")
+    load(a0, ap(a0), T.a0[:], 2.2, "S")
+
+    lab[0] = "const"
 
     def col(ins, src, s1, op0, s2=None, op1=None, n=1, pool="f32", f=1.0):
         t = tile(pool, n)
         ts(t, ap(t), src, s1, op0, s2, op1, ins, n, f)
         return t
 
-    def acol(src, scale, bias):
-        t = tile("f32", src["n"])
-        act(t, ap(t), ap(src), AF.Identity, [src], src["n"], scale=scale, bias=bias)
+    def acol(src, scale, bias=0.0, pool="bf", a=0, n=None, out=None, o=0):
+        n = src["n"] if n is None else n
+        t = out or tile(pool, n)
+        cols = [c for c in (scale, bias) if isinstance(c, dict)]
+        act(t, ap(t, o, o + n), ap(src, a, a + n), AF.Identity, [src] + cols, n,
+            scale=ap(scale) if isinstance(scale, dict) else scale, bias=ap(bias) if isinstance(bias, dict) else bias)
         return t
-    ip, ckr, ci = tile("i32", 1), tile("i32", 16), tile("i32", C)
-    im, kpat = tile("f32", 144), tile("bf", 16 * CW)
-    mgf, msf, ii0 = tile("f32", 128), tile("f32", 128), tile("f32", 12)
+    PW = max(max(p) for _, _, p in HV)
+    ip, ckr, pni = tile("i32", 1), tile("i32", 16), tile("i32", 128)
+    im, kpat, mgf, ii0, il = tile("f32", 144), tile("bf", 16 * PW), tile("f32", 128), tile("f32", C), tile("bf", L)
     iota(ip, [[0, 1]], 0, 1, False)
     iota(im, [[1, 144]], 0, 0)
-    iota(kpat, [[0, CW], [1, 16]], 0, 0)
     iota(mgf, [[1, 8], [0, 16]], 0, 0)
-    iota(ii0, [[16, 12]], 0, 0)
+    iota(kpat, [[0, PW], [1, 16]], 0, 0)
+    iota(ii0, [[16, C]], 0, 0)
+    iota(il, [[1, L]], 0, 0)
+    iota(pni, [[0, 8], [1, 16]], 1, 1, False)
     iota(ckr, [[-1, 16]], 16, 1, False)
-    iota(ci, [[1, C]], 0, 0, False)
-    iota(msf, [[0, 8], [1, 16]], 0, 0)
+    for j in range(len(tasks) - 7, len(tasks)):
+        soft(j, j - 1)
     si = col([ip], ap(ip), 15, AL.bitwise_and, pool="i32")
     gi = col([ip], ap(ip), 4, AL.arith_shift_right, pool="i32")
     scol = col([si], ap(si), 0.0, AL.add)
     zc = col([gi], ap(gi), 16.0, AL.mult, 15.0, AL.add)
     gcol = col([gi], ap(gi), 0.0, AL.add)
     pcol = col([ip], ap(ip), 0.0, AL.add)
-    oh0 = col([scol], ap(scol), 0.0, AL.is_equal)
-    k16 = col([scol], ap(scol), 16.0, AL.add)
+    row = {r: col([scol], ap(scol), float(r), AL.is_equal) for r in (0, 3, 4)}
     rm3 = col([scol], ap(scol), 3.0, AL.is_ge)
-    mask0 = col([kpat, scol], ap(kpat), ap(scol), AL.is_equal, n=16 * CW, pool="bf", f=0.5)
-    Zh = col([im, zc], ap(im), ap(zc), AL.is_equal, n=144, pool="hf")
+    r01 = col([scol], ap(scol), 2.0, AL.is_lt)
+    mask0 = col([kpat, scol], ap(kpat), ap(scol), AL.is_equal, n=16 * PW, pool="bf", f=0.5)
     Zb = col([im, zc], ap(im), ap(zc), AL.is_equal, n=144, pool="bf")
-    Zk = col([Zh, k16], ap(Zh), ap(k16), AL.mult, n=144, pool="hf", f=0.5)
     Idb = col([im, pcol], ap(im, 0, 128), ap(pcol), AL.is_equal, n=128, pool="bf")
-    Im = col([Idb], ap(Idb), -1.0, AL.mult, n=128, pool="bf", f=0.5)
     Blk = col([mgf, gcol], ap(mgf), ap(gcol), AL.is_equal, n=128, pool="bf")
     lt = col([im, pcol], ap(im, 0, 128), ap(pcol), AL.is_gt, n=128, pool="bf")
-    Tri = tile("bf", 128)
+    Tri, M1, M2, PNm = tile("bf", 128), tile("bf", 128), tile("bf", 128), tile("bf", 128)
+    Zn, Im, I16n, I512, I15 = acol(Zb, -1.0), acol(Idb, -1.0), acol(Idb, -16.0), acol(Idb, 512.0), acol(Idb, 15.0)
     tt(Tri, ap(Tri), ap(lt), ap(Blk), AL.mult, [lt, Blk], 128, 2)
-    RS = col([im, oh0], ap(im, 0, 128), 0.0, AL.mult, ap(oh0), AL.add, n=128)
-    Idh = col([im, pcol], ap(im, 0, 128), ap(pcol), AL.is_equal, n=128, pool="hf")
-    Lt = []
-    for t in range(ST):
-        eq = col([msf], ap(msf), float(t), AL.is_equal, n=128, pool="bf")
-        Lt.append(tile("hf", 128))
-        tt(Lt[t], ap(Lt[t]), ap(eq), ap(Blk), AL.mult, [eq, Blk], 128, 2)
+    tt(M1, ap(M1), ap(Tri), ap(I16n), AL.add, [Tri, I16n], 128, 2)
+    tt(M2, ap(M2), ap(M1), ap(Zb, 15, 143), AL.add, [M1, Zb], 128, 2)
+    M3 = acol(M1, 1024.0)
+    pn2 = col([pni], ap(pni), 15, AL.bitwise_and, n=128, pool="i32")
+    tt(PNm, ap(PNm), ap(pn2), ap(Blk), AL.mult, [pn2, Blk], 128, 2)
+    th1 = acol(scol, 1.0, 16.0, "f32")
+    n0 = acol(row[0], -16.0, 0.0, "f32")
+    th2 = acol(th1, 1.0, n0, "f32")
+    e3 = acol(scol, 1.0, -3.0, "f32")
+    r4n = acol(row[4], -1.0, 0.0, "f32")
+    R3, R4n, K4, K01, Bn = acol(Blk, row[3]), acol(Blk, r4n), acol(Idb, row[4]), acol(Idb, r01), acol(Blk, -1.0)
+    ones = acol(il, 0.0, 1.0)
+    neg1 = acol(scol, 0.0, -1.0)
+    oh0 = acol(ones, row[0], n=128)
+    i8 = acol(il, 8.0)
     cki = col([ckr], ap(ckr), 15, AL.bitwise_and, n=16, pool="i32")
-    ck = col([cki], ap(cki), 0.0, AL.add, n=16)
-    cidx = tile("u16", C)
-    tcopy(cidx, ap(cidx), ap(ci), [ci], C)
-    ii = col([ii0, scol], ap(ii0), ap(scol), AL.add, n=12)
-    hU0, I2, xi = acol(ii, 8.0, -1536.0), acol(ii, 1.0, 1536.0), acol(ii, 16.0, 0.0)
-    i48, i144, one = acol(ii, 1.0, 48.0), acol(ii, -1.0, 144.0), acol(ii, 0.0, 1.0)
-    ones = tile("bf", L)
-    act(ones, ap(ones), ap(kpat, 0, L), AF.Identity, [kpat], L, scale=0.0, bias=1.0)
-    thf = col([thi], ap(thi), 0.0, AL.add)
-    own_nb = ap(nbi, 0, GW, 8)
-    El0 = tile("u16", L)
-    tcopy(El0, ap(El0), own_nb, [nbi], L)
-    NBh0 = col([nbi], own_nb, -1536.0, AL.add, n=L)
+    ck = col([cki], ap(cki), 0.0, AL.add, n=16, pool="bf")
+    ii = col([ii0, scol], ap(ii0), ap(scol), AL.add, n=C)
+    nth = col([thi], ap(thi), -1.0, AL.mult, -0.5, AL.add)
+    b3, dfl = {}, {}
+    for i0, W, _ in HV:
+        cw, c0, pad = W // 16, i0 // 16, -(W // 16) % 8
+        if W not in b3:
+            b3[W] = acol(scol, -1023.0, 2.0 * W - 16384.0, "f32")
+        for t in range(2):
+            d = dfl[i0, t] = tile("bf", pad + 3 * cw)
+            acol(ones, 0.0, n=pad + cw, out=d)
+            if t == 0:
+                d = dict(d, mut=True)
+                acol(ii, 8.0, a=c0, n=cw, out=d, o=pad)
+                dfl[i0, t] = d = dict(d, mut=False)
+            acol(ii, 16.0, a=c0, n=cw, out=d, o=pad + cw)
+            acol(ii, 1.0, -float(i0), a=c0, n=cw, out=d, o=pad + 2 * cw)
+    lab[0] = "conv"
     G = tile("f32", GW)
-    for j in range(2):
-        ts(G, ap(G, 768 * j, 768 * j + 768), ap(gh[j]), -1536.0, AL.add, None, None, [gh[j]], 768)
+    for j in range(NG):
+        ts(G, ap(G, GW // NG * j, GW // NG * (j + 1)), ap(gh[j]), -1536.0, AL.add, None, None, [gh[j]], GW // NG, boost=100)
     G["mut"] = True
-    NBf = tile("f32", GW)
-    for j in range(4):
-        ts(NBf, ap(NBf, 384 * j, 384 * j + 384), ap(nbi, 384 * j, 384 * j + 384), -1536.0, AL.add, None, None, [nbi], 384)
-    own = tile("f32", 48 + L)
-    act(own, ap(own, 48, 48 + L), ap(G, 0, GW, 8), AF.Copy, [G], L)
+    El0, NB0 = [], []
+    for h, (i0, W, _) in enumerate(HV):
+        El0.append(tile("u16", W))
+        tcopy(El0[h], ap(El0[h]), ap(nh[h], 0, 8 * W, 8), [nh[h]], W, boost=100)
+        NB0.append(tile("hf", W))
+        tcopy(NB0[h], ap(NB0[h]), ap(nh[h], 0, 8 * W, 8), [nh[h]], W)
+
+    def when(gen, t, h, what, j=0):
+        at, step = PLAN[what]
+        turn[0] = (gen * ST + t + 1) * PLAN["step"] + gen * PLAN["end"] + h * PLAN["half"] + at + j * step
 
     def Z(z, k):
         return ap(z, 15 - k, 143 - k)
 
-    lim = thf
+    BW, BD, BY, BM = (0, 1), (2, 3), (4, 5, 6), 7
+    ny = [0]
+    masks, yas = [tile("bf", 17 * W) for _, W, _ in HV], [tile("bf", 16 * W) for _, W, _ in HV]
+    lim = nth
+    a = [part(a0, i0, W) for i0, W, _ in HV]
+    for p in a:
+        p["wr"] = a0["wr"]
     for gen in range(GENS):
-        mo, mother = tile("hf", L), tile("hf", L)
-        imo = ts(mo, ap(mo), ap(own, 48, 48 + L), ap(rm3), AL.mult, None, None, [own, rm3], L, boost=-30)
-        send(mo, ap(mo), [(mother, ap(mother), 2)], boost=-30)
-        hp = None
-        vs, fs = [], []
+        lab[0] = "g%d mother" % gen
+        when(gen, 0, 0, "sums")
+        mo, mother, win = tile("hf", L), tile("hf", L), tile("f32", L + 48)
+        own, come = part(win, 0, L), part(win, L, 48)
+        ts(mo, ap(mo), ap(G, 0, GW, 8), ap(rm3), AL.mult, None, None, [G, rm3], L, boost=-30)
+        send([(mo, ap(mo), mother, ap(mother), 2)], boost=-30)
+        act(own, ap(own), ap(G, 0, GW, 8), AF.Copy, [G], L, boost=-30)
+        R, info = [None] * len(HV), [None] * len(HV)
+        oh, cum, dau = tile("bf", L), tile("bf", L), tile("f32", L)
         for t in range(ST):
-            last = t == ST - 1
-            nM = tile("hf", L)
-            if t == 0:
-                NBh, El, mask = NBh0, El0, mask0
-                inM = ts(nM, ap(nM), ap(G, 0, GW, 8), ap(oh0), AL.mult, None, None, [G, oh0], L)
-                hU, hUa, pw1 = hU0, ap(hU0), one
-            else:
-                PM = tile("bf", L)
-                tt(PM, ap(PM), ap(hp, 0, C).indirect(ap(cidx)), ap(mask0, 0, L), AL.mult, [hp, cidx, mask0], dur=gc_(L))
-                pr = ps(1)
-                mms(pr, [PM, Blk], [(ap(pr, 0, L), ap(Blk), ap(PM), True, True, L)])
-                prb = tile("bf", L)
-                act(prb, ap(prb), ap(pr, 0, L), AF.Copy, [pr], L)
-                hl = tile("u16", C)
-                ts(hl, ap(hl), ap(hp, C, 2 * C), 1536.0, AL.add, None, None, [hp], C, boost=50)
-                NBh, El = tile("f32", L), tile("u16", L)
-                act(NBh, ap(NBh), ap(NBf).indirect(ap(hl)), AF.Copy, [NBf, hl], dur=gc_(L), boost=50)
-                ts(El, ap(El), ap(NBh), 1536.0, AL.add, None, None, [NBh], L, boost=50)
-                mask = ring("bf", 16 * L, "mask")
-                for k in range(16 - SM, 16):
-                    ab = ring("bf", L, ("ab", k))
-                    act(ab, ap(ab), ap(prb), AF.Abs, [prb, ck], L, scale=-1.0, bias=ap(ck, k, k + 1))
-                    act(mask, ap(mask, k, 16 * L, 16), ap(ab), AF.Relu, [ab], L, scale=-1.0, bias=1.0)
-                for k in range(16 - SM):
-                    ts(mask, ap(mask, k, 16 * L, 16), ap(prb), ap(ck, k, k + 1), AL.is_equal, None, None, [prb, ck], L, 0.5)
-                inM = tt(nM, ap(nM), ap(G).indirect(ap(hl)), ap(mask, 0, 16 * L, 16), AL.mult, [G, hl, mask], dur=gc_(L))
-                hU, hUa, pw1 = hp, ap(hp, C, 2 * C), tile("f32", C)
-                act(pw1, ap(pw1), ap(hp, 0, C), AF.Identity, [hp], C, bias=1.0)
-            V, Vj, iG, iW = ring("bf", 16 * L, "V"), [], [], []
-            Wp = ps(0)
-            for j in range(EC):
-                Gg, c0, c1 = ring("hf", 16 * CW, ("Gg", j)), j * CW, j * CW + CW
-                m0 = 0 if t == 0 else 16 * c0
-                iG.append(tt(Gg, ap(Gg), ap(G).indirect(ap(El, c0, c1)), ap(mask, m0, m0 + 16 * CW), AL.mult, [G, El, mask], dur=gc_(16 * CW)))
-                iWm = mms(Wp, [Gg, Zh], [(ap(Wp, c0, c1), Z(Zh, k), ap(Gg, k, 16 * CW, 16), k == 0, k == 15, CW) for k in range(16)])
-                Wl = tile("u16", CW)
-                iW.append(ts(Wl, ap(Wl), ap(Wp, c0, c1), 1536.0, AL.add, None, None, [Wp], CW, boost=50))
-                Vv = mk(V["b"], V["lo"] + 16 * c0, 16 * CW, False, V["pre"])
-                if VG[j] == "V":
-                    tcopy(Vv, ap(Vv), ap(X).indirect(ap(Wl)), [X, Wl], dur=gc_(16 * CW))
+            last, st = t == ST - 1, []
+            for h, (i0, W, pieces) in enumerate(HV):
+                lab[0] = "g%d t%d h%d front" % (gen, t, h)
+                when(gen, t, h, "lists")
+                cw, pad = W // 16, -(W // 16) % 8
+                Gg, Wl, Tb = tile("hf", 17 * W), tile("u16", cw + W), tile("bf", 18 * W)
+                Wp, nM, Tt, recs = ps(BW[h], 0, cw + W), part(Gg, 0, W), part(Tb, 0, W), []
+                s = {"Gg": Gg, "Tb": Tb, "Wp": Wp, "nM": nM, "T": Tt, "recs": recs, "R": R[h]}
+                if t == 0:
+                    ts(nM, ap(nM), ap(G, 8 * i0, 8 * (i0 + W), 8), ap(row[0]), AL.mult, None, None, [G, row[0]], W)
+                    s["oh"], s["nb"] = oh0, NB0[h]
                 else:
-                    act(Vv, ap(Vv), ap(X).indirect(ap(Wl)), AF.Copy, [X, Wl], dur=gc_(16 * CW))
-                V["wr"] += Vv["wr"]
-                Vj.append(Vv)
-                if j == 0:
-                    npz, dq = ps(1), ps(7)
-                    mms(npz, [nM, Zh], [(ap(npz, 0, C), Z(Zh, r), ap(nM, r, L, 16), r == 0, r == 15, C) for r in range(16)])
-                    nl, df = tile("u16", C), tile("bf", L)
-                    inl = ts(nl, ap(nl), ap(npz, 0, C), 1536.0, AL.add, None, None, [npz], C, boost=50)
-                    act(df, ap(df), ap(X).indirect(ap(nl)), AF.Copy, [X, nl], dur=gc_(L), boost=50)
-                    mms(dq, [df, a, Idb, Im], [(ap(dq, 0, L), ap(Idb), ap(df), True, False, L), (ap(dq, 0, L), ap(Im), ap(a), False, True, L)], boost=50)
-                    act(ext, ap(ext), ap(dq, 0, L), AF.Abs, [dq], L, boost=50)
-            seq = [iG[0], inM, iW[0], iG[1], inl, iW[1], iG[2], iW[2], iG[3], iW[3]]
-            if t == 0:
-                soft(imo, iG[0])
-            for u, v in zip(seq, seq[1:]):
-                soft(v, u)
-            FI, Q, ok = tile("hf", L), tile("hf", 2 * L), tile("bf", L)
-            for y in range(NC):
-                i0, i1 = y * W, y * W + W
-                Dp = ps(2 + y)
-                D = ap(Dp, 0, W)
-                Te = ap(ext, i0, i1)
-                vin = [Vj[j] for j in range(EC) if i0 <= j * CW < i1]
+                    Rm, o = R[h], W + pad
+                    El = mk(Rm["b"], Rm["lo"] + o + cw, W)
+                    tcopy(El, ap(El), ap(nbi).indirect(ap(Rm, o, o + cw)), nh + [Rm], dur=gc_(W))
+                    mask = part(masks[h], 0, 17 * W)
+                    s["oh"] = part(mask, 0, W)
+                    ts(s["oh"], ap(mask, 0, W), ap(Rm, 0, W), ap(ck, 0, 1), AL.is_equal, None, None, [Rm, ck], W, 0.5)
+                    for k in range(16):
+                        ts(mask, ap(mask, W + k, 17 * W, 16), ap(Rm, 0, W), ap(ck, k, k + 1), AL.is_equal, None, None, [Rm, ck], W, 0.5)
+                    if not last:
+                        when(gen, t, h, "sums")
+                        s["nb"], s["hw"] = tile("hf", W), tile("hf", cw)
+                        tcopy(s["nb"], ap(s["nb"]), ap(El), [El], W, 0.5)
+                        tcopy(s["hw"], ap(s["hw"]), ap(Rm, o, o + cw), [Rm], cw)
+                s0 = 0
+                for j, pw in enumerate(pieces):
+                    e0, e1 = (0 if j == 0 else W + 16 * s0), W + 16 * (s0 + pw)
+                    l0, l1 = e0 // 16, e1 // 16
+                    Gp = part(Gg, e0, e1 - e0)
+                    when(gen, t, h, "names", j)
+                    if t == 0:
+                        tt(Gp, ap(Gg, W + 16 * s0, e1), ap(G).indirect(ap(El0[h], s0, s0 + pw)), ap(mask0, 0, 16 * pw), AL.mult, [G, El0[h], mask0], dur=gc_(16 * pw))
+                    else:
+                        tt(Gp, ap(Gp), ap(G).indirect(ap(Rm, o + l0, o + l1)), ap(mask, e0, e1), AL.mult, [G, El, mask, s["oh"]], dur=gc_(e1 - e0))
+                        if j == 0:
+                            nM["wr"] = Gp["wr"]
+                    Wq = ps(BW[h], l0, l1 - l0)
+                    when(gen, t, h, "records", j)
+                    mms([Wq, Wp], [Gp, nM, Zb], [[(ap(Wq), Z(Zb, k), ap(Gp, k, e1 - e0, 16)) for k in range(16)]], 16 * max(64, l1 - l0))
+                    Wj, rec = part(Wl, l0, l1 - l0), part(Tb, W + e0, e1 - e0)
+                    ts(Wj, ap(Wj), ap(Wq), 1536.0, AL.add, None, None, [Wq], l1 - l0)
+                    if CFG["rec"][t][sum(len(x[2]) for x in HV[:h]) + j] == "V":
+                        tcopy(rec, ap(rec), ap(X).indirect(ap(Wj)), [X, Wj], dur=gc_(e1 - e0))
+                    else:
+                        act(rec, ap(rec), ap(X).indirect(ap(Wj)), AF.Copy, [X, Wj], dur=gc_(e1 - e0))
+                    recs.append(rec)
+                    if j == 0:
+                        dq = ps(BD[h], 0, W)
+                        mms([dq], [rec, a[h], Idb, Im], [[(ap(dq), ap(Idb), ap(rec, 0, W)), (ap(dq), ap(Im), ap(a[h]))]], 2 * W)
+                        act(Tt, ap(Tt), ap(dq), AF.Abs, [dq], W)
+                    s0 += pw
+                st.append(s)
+            cnt = ps(BM, 128, L)
+            for h, (i0, W, pieces) in enumerate(HV):
+                lab[0] = "g%d t%d h%d mid" % (gen, t, h)
+                when(gen, t, h, "sums")
+                s = st[h]
+                cw, pad = W // 16, -(W // 16) % 8
+                Tb, Tt, recs, Wp, nM = s["Tb"], s["T"], s["recs"], s["Wp"], s["nM"]
+                val = ps(BW[h], 256, 2 * W)
+                grp, ins = [[(ap(val, W, 2 * W), ap(PNm), ap(s["oh"], 0, W))]], [PNm, s["oh"]]
+                if not last:
+                    old = (ap(Im), ap(i8, i0, i0 + W)) if t == 0 else (ap(R4n), ap(info[h]))
+                    grp.append([(ap(val, 0, W), ap(Idb), ap(s["nb"])), (ap(val, 0, W),) + old])
+                    ins += [Idb, s["nb"], Im, i8] + ([R4n, info[h]] if t else [])
+                mms([val], ins, grp, 3 * W)
+                D = ps(BD[h], 0, W)
                 for q in range(16 // KG):
-                    Y, lst, dl = ps(4 + (y * 4 + q) % 3), [], []
-                    ya = ring("bf", KG * W, ("ya", y, q))
-                    for kk in range(KG):
-                        k = q * KG + kk
-                        o, v = ap(Y, kk * W, kk * W + W), ap(V, 16 * i0 + k, 16 * i1, 16)
-                        lst += [(o, ap(Idb), v, True, False, W), (o, ap(Idb), Te, False, True, W)]
-                        dl.append((D, Z(Zb, k), ap(ya, kk * W, kk * W + W), k == 0, k == 15, W))
-                    mms(Y, vin + [Idb, ext], lst)
-                    act(ya, ap(ya), ap(Y, 0, KG * W), AF.Abs, [Y], KG * W, bias=-255.0)
-                    soft(mms(Dp, [ya, Zb], dl, after=Dp, boost=20), iWm)
-                ts(ok, ap(ok, i0, i1), D, ap(lim), AL.is_le, None, None, [Dp, lim], W, boost=20)
-                oky = mk(ok["b"], ok["lo"] + i0, W)
-                oky["wr"] = ok["wr"][-1:]
-                Cp = ps(2 + y)
-                mms(Cp, [oky, Tri], [(ap(Cp, 0, W), ap(Tri), ap(oky), True, True, W)], boost=20)
-                tt(FI, ap(FI, i0, i1), ap(Cp, 0, W), ap(oky), AL.is_lt, [Cp, oky], W, boost=20)
-                FIy = mk(FI["b"], FI["lo"] + i0, W)
-                FIy["wr"] = FI["wr"][-1:]
-                tt(Q, ap(Q, i0, i1), ap(FIy), ap(NBh, i0, i1), AL.mult, [FIy, NBh], W, 2)
-                tt(Q, ap(Q, L + i0, L + i1), ap(Wp, i0, i1), ap(FIy), AL.mult, [FIy, Wp], W)
-            cp = ps(1)
-            mms(cp, [FI, Zk], [(ap(cp, 0, C), Z(Zk, r), ap(FI, r, L, 16), r == 0, r == 15, C) for r in range(16)])
-            x1, x2, nf = tile("i32", C), tile("i32", C), tile("f32", C)
-            icode = tt(x1, ap(x1), ap(cp, 0, C), ap(pw1, 0, C), AL.add, [cp, pw1], C)
-            ts(x2, ap(x2), ap(x1), 15, AL.bitwise_and, None, None, [x1], C)
-            soft(ts(nf, ap(nf), ap(cp, 0, C), 16.0, AL.is_lt, None, None, [cp], C), icode)
-            Qp, Qe = ps(7), ps(3)
-            for Qx, o in ((Qp, 0), (Qe, L)):
-                if Qx is Qe or not last:
-                    Qs = mk(Q["b"], Q["lo"] + o, L)
-                    Qs["wr"] = Q["wr"][o // L::2]
-                    mms(Qx, [Qs, Zh], [(ap(Qx, 0, C), Z(Zh, r), ap(Qs, r, L, 16), r == 0, r == 15, C) for r in range(16)])
-            if not last:
-                Uh, ho, hp = tile("f32", C), tile("f32", 2 * C), tile("f32", 2 * C)
-                tcopy(ho, ap(ho, 0, C), ap(x2), [x2], C)
-                tt(Uh, ap(Uh), ap(nf), hUa, AL.mult, [nf, hU], C)
-                tt(ho, ap(ho, C, 2 * C), ap(Qp, 0, C), ap(Uh), AL.add, [Qp, Uh], C)
-                send(ho, ap(ho), [(hp, ap(hp), 1)])
-            Ue, Re, Ll = tile("f32", C), tile("f32", C), tile("u16", C)
-            tt(Ue, ap(Ue), ap(nf), ap(I2), AL.mult, [nf, I2], C)
-            tt(Re, ap(Re), ap(Qe, 0, C), ap(Ue), AL.add, [Qe, Ue], C)
-            iL = ts(Ll, ap(Ll), ap(Re), 1536.0, AL.add, None, None, [Re], C)
-            an, a2 = tile("bf", L), tile("bf", L)
-            act(an, ap(an), ap(XB).indirect(ap(Ll)), AF.Copy, [X, ext, Ll], dur=gc_(L))
-            ian = send(an, ap(an), [(a2, ap(a2), 1 if not last else -2)])
-            cn = ps(4)
-            mms(cn, [ok, Blk], [(ap(cn, 0, L), ap(Blk), ap(ok), True, True, L)], boost=40 if last else 0)
-            fl, acc, P4 = tile("bf", L), tile("f32", 1), tile("hf", L)
-            act(fl, ap(fl), ap(cn, 0, L), AF.Relu, [cn], L, scale=-1.0, bias=1.0, acc=acc)
-            iP4 = tt(P4, ap(P4), ap(fl), ap(nM), AL.mult, [fl, nM], L, 2)
-            if not last:
-                soft(iP4, iL)
-                vn, vi, fi = tile("hf", L), tile("hf", L), tile("bf", L)
-                tt(vn, ap(vn), ap(P4), ap(Q, L, 2 * L), AL.add, [P4, Q], L, 2)
-                soft(send(fl, ap(fl), [(fi, ap(fi), 2 - t)]), ian)
-                send(vn, ap(vn), [(vi, ap(vi), 2 - t)])
-                vs.append([(vi, 0)])
-                fs.append(fi)
-            else:
-                vs.append([(P4, 0), (Q, L)])
-                fs.append(fl)
-            pf, pl = tile("f32", C), tile("u16", C)
-            tt(pf, ap(pf), ap(x2), ap(xi), AL.add, [x2, xi], C)
-            tcopy(pl, ap(pl), ap(pf), [pf], C)
+                    Y, ya = ps(BY[ny[0] % len(BY)], 0, KG * W), part(yas[h], q * KG * W, KG * W)
+                    ny[0] += 1
+                    when(gen, t, h, "sums", q)
+                    ks = range(q * KG, q * KG + KG)
+                    mms([Y], recs + [Idb, Tt], [[(ap(Y, (k % KG) * W, (k % KG + 1) * W), ap(Idb), x) for x in (ap(Tb, 2 * W + k, 18 * W, 16), ap(Tt))] for k in ks], 2 * KG * W)
+                    act(ya, ap(ya), ap(Y), AF.Abs, [Y], KG * W, bias=-255.0)
+                    mms([D], [ya, Zb], [[(ap(D), Z(Zb, k), ap(ya, (k % KG) * W, (k % KG + 1) * W)) for k in ks]], KG * W, after=D, ends=(q == 0, q == 16 // KG - 1))
+                lab[0] = "g%d t%d h%d tail" % (gen, t, h)
+                sg = tile("bf", W)
+                when(gen, t, h, "first")
+                act(sg, ap(sg), ap(D), AF.Sign, [D, lim], W, bias=ap(lim))
+                x = ps(BD[h], W, 3 * W)
+                mms([x], [sg, M1, M2, M3, I15, il], [[(ap(x, 0, W), ap(M1), ap(sg))], [(ap(x, W, 2 * W), ap(M2), ap(sg))],
+                                                    [(ap(x, 2 * W, 3 * W), ap(M3), ap(sg)), (ap(x, 2 * W, 3 * W), ap(I15), ap(il, 0, W))]], 4 * W)
+                FF, Q = tile("bf", 2 * W), tile("hf", 3 * W)
+                FI, F2, Qv, Ql = part(FF, 0, W), part(FF, W, W), part(Q, 0, 2 * W), part(Q, 2 * W, W)
+                bo = 20 if last and h == len(HV) - 1 else 0
+                ts(FI, ap(FI), ap(x, 0, W), ap(th1), AL.is_ge, None, None, [x, th1], W, boost=bo)
+                ts(F2, ap(F2), ap(x, W, 2 * W), ap(th2), AL.is_ge, None, None, [x, th2], W)
+                q0 = W if last else 0
+                tt(Qv, ap(Q, q0, 2 * W), ap(val, q0, 2 * W), ap(FF, q0, 2 * W), AL.mult, [val, FI, F2], 2 * W - q0)
+                ts(Ql, ap(Ql), ap(x, 2 * W, 3 * W), ap(b3[W]), AL.add, 0.0, AL.max, [x, b3[W]], W)
+                n, w0 = W + pad + 3 * cw, W + pad
+                Op, O, d = ps(BD[h], 0, n), tile("u16", n), dfl[i0, min(t, 1)]
+                c0 = cw if last else 0
+                grp = [] if last else [[(ap(Op, 0, W), ap(Blk), ap(Q, W, 2 * W))]]
+                gr = [(ap(Op, W, n), ap(Idb), ap(d))] + ([(ap(Op, w0, w0 + cw), ap(Idb), ap(s["hw"]))] if t == 1 else [])
+                gr += [(ap(Op, w0 + c0, n), Z(Zb, r), ap(Q, q0 + r, 3 * W, 16)) for r in range(16)]
+                mms([Op], [Qv, Ql, Zb, Blk, Idb, d] + ([s["hw"]] if t == 1 else []), grp + [gr], 18 * 64 + W)
+                o0 = w0 + cw if last else 0
+                tcopy(O, ap(O, o0, n), ap(Op, o0, n), [Op], n - o0)
+                if not last:
+                    R[h] = tile("u16", w0 + cw + W)
+                    R[h]["n"] = w0 + cw
+                    im1 = send([(O, ap(O, 0, w0 + cw), R[h], ap(R[h]), 1)])
+                an, a2 = tile("bf", W), tile("bf", W)
+                when(gen, t, h, "put")
+                act(an, ap(an), ap(Tb).indirect(ap(O, w0 + 2 * cw, n)), AF.Copy, recs + [Tt, O], dur=gc_(W))
 
-            def put(pl=pl, an=an):
-                return [g.vector.tensor_copy(ap(X).indirect(ap(pl)), ap(an))]
-            iput = task("V", gc_(L, "scatter"), [pl, an], [X], put)
-            if not (gen == GENS - 1 and last):
-                Ap = ps(0)
-                mms(Ap, [acc, RS], [(ap(Ap, 0, 1), ap(RS), ap(acc), True, True, 1)], 4)
-                A1, A2, lim = tile("i32", 1), tile("i32", 1), tile("f32", 1)
-                soft(tcopy(A1, ap(A1), ap(Ap, 0, 1), [Ap], 1), iL)
+                def put(O=O, an=an, u=w0 + cw, v=w0 + 2 * cw):
+                    return [g.vector.tensor_copy(ap(X).indirect(ap(O, u, v)), ap(an))]
+                s["put"] = task("V", gc_(W, "scatter"), [O, an], [X], put)
+                lab[0] = "g%d t%d h%d info" % (gen, t, h)
+                when(gen, t, h, "first" if last else "info")
+                if last:
+                    Ep = ps(BW[h], 256, W)
+                    mms([Ep], [info[h], FI, R3, Bn], [[(ap(Ep), ap(R3), ap(info[h])), (ap(Ep), ap(Bn), ap(FI))]], 2 * W, boost=bo)
+                    ohh, cm = part(oh, i0, W), part(cum, i0, W)
+                    ts(ohh, ap(ohh), ap(Ep), ap(e3), AL.is_equal, None, None, [Ep, e3], W, boost=bo)
+                    before = st[h - 1]["cum"] if h else None
+
+                    def scan(ohh=ohh, cm=cm, W=W, before=before):
+                        return [g.vector.tensor_tensor_scan(ap(cm), ap(ones, 0, W), ap(ohh), ap(before, before["n"] - 1) if before else 0.0, AL.mult, AL.add)]
+                    task("V", vc(W, 0.5), [ohh, ones] + ([before] if before else []), [cm], scan, boost=bo)
+                    s["cum"], s["ohh"] = cm, ohh
+                fo, ch = ps(BM, 0, W), ps(BM, 128 + i0, W)
+                more = not (gen == GENS - 1 and last)
+                mms([fo, ch, cnt], [FI, Blk, ones], [[(ap(fo), ap(Blk), ap(FI))]] + ([[(ap(ch), ap(ones, 0, 128), ap(FI))]] if more else []), 2 * W)
+                Qe, Qn = tile("hf", W), tile("hf", W)
+                tt(Qe, ap(Qe), ap(Wp, cw, cw + W), ap(FI), AL.mult, [Wp, FI], W)
+                tt(Qn, ap(Qn), ap(fo), ap(nM), AL.mult, [fo, nM], W)
+                ip_ = ps(BM, 320 + i0, W)
+                gr = [(Z(Zb, t), ap(Qe)), (Z(Zb, t), ap(nM)), (Z(Zn, t), ap(Qn))]
+                ins = [Qe, Qn, nM, Zb, Zn]
+                if t == 0:
+                    gr += [(Z(Zn, 3), ap(FI)), (Z(Zb, 4), ap(Q, 0, W)), (ap(K4), ap(i8, i0, i0 + W))]
+                    ins += [FI, Qv, K4, i8]
+                elif not last:
+                    gr += [(Z(Zn, 3), ap(FI)), (ap(Idb), ap(info[h]))]
+                    ins += [FI, Idb, info[h]]
+                else:
+                    gr += [(ap(K01), ap(info[h])), (ap(Idb), ap(mother, i0, i0 + W))]
+                    ins += [K01, Idb, info[h], mother]
+                mms([ip_], ins, [[(ap(ip_),) + u for u in gr]], len(gr) * W)
+                if last:
+                    act(dau, ap(dau, i0, i0 + W), ap(ip_), AF.Copy, [ip_], W)
+                    s["send"] = send([(an, ap(an), a2, ap(a2), -2)], boost=-5)
+                else:
+                    io, info[h] = tile("hf", W), tile("hf", W)
+                    tcopy(io, ap(io), ap(ip_), [ip_], W)
+                    soft(send([(an, ap(an), a2, ap(a2), 1), (io, ap(io), info[h], ap(info[h]), 1)]), im1)
+                a[h] = a2
+            if more:
+                lab[0] = "g%d t%d lim" % (gen, t)
+                junk, acc, A1, A2, lim = tile("bf", L), tile("f32", 1), tile("i32", 1), tile("i32", 1), tile("f32", 1)
+                act(junk, ap(junk), ap(cnt), AF.Identity, [cnt], L, scale=-1.0, bias=8.0, acc=acc, dur=vc(L) + 0.14)
+                tcopy(A1, ap(A1), ap(acc), [acc], 1)
                 ts(A2, ap(A2), ap(A1), 63, AL.bitwise_and, None, None, [A1], 1)
-                ts(lim, ap(lim), ap(A2), ap(thf), AL.add, None, None, [A2, thf], 1)
-            a = a2
-        Ep = ps(5)
-        mms(Ep, fs + [Idb], [(ap(Ep, 0, L), ap(Idb), ap(fs[t]), t == 0, t == ST - 1, L) for t in range(ST)], boost=40)
-        oh, cum = tile("bf", L), tile("bf", L)
-        ts(oh, ap(oh), ap(Ep, 0, L), ap(scol), AL.is_equal, None, None, [Ep, scol], L, boost=40)
-
-        def scan(oh=oh, cum=cum):
-            return [g.vector.tensor_tensor_scan(ap(cum), ap(ones), ap(oh), 0.0, AL.mult, AL.add)]
-        task("V", vc(L, 0.5), [oh, ones], [cum], scan, boost=40)
-        bp = ps(5)
-        mms(bp, [cum, Tri], [(ap(bp, 0, 1), ap(Tri), ap(cum, L - 1, L), True, True, 1)], boost=40)
-        q1, q2 = tile("bf", L), tile("bf", L)
-        tt(q1, ap(q1), ap(oh), ap(cum), AL.mult, [oh, cum], L, 2, boost=40)
-        iq2 = ts(q2, ap(q2), ap(oh), ap(bp, 0, 1), AL.mult, None, None, [oh, bp], L, 0.5, boost=40)
-        soft(iP4, iq2)
-        soft(icode, iP4)
-        op_ = ps(7)
-        for q in (q1, q2):
-            mms(op_, [q, Zb], [(ap(op_, 0, 12), Z(Zb, r), ap(q, r, L, 16), r == 0 and q is q1, r == 15 and q is q2, 12) for r in range(16)], boost=40, after=op_)
-        po = tile("u16", 12)
-        ts(po, ap(po), ap(op_, 0, 12), -1.0, AL.add, None, None, [op_], 12)
-        dp, lst = ps(6), [(ap(Idh), ap(mother))]
-        for t in range(ST):
-            lst += [(ap(Lt[t]), ap(v, o, o + L)) for v, o in vs[t]]
-        lst = [(ap(dp, 0, L), l, r, j == 0, j == len(lst) - 1, L) for j, (l, r) in enumerate(lst)]
-        mms(dp, [mother, Idh] + Lt + [v for w in vs for v, _ in w], lst)
-        dau, srt = tile("f32", L), tile("f32", L)
-        act(dau, ap(dau), ap(dp, 0, L), AF.Copy, [dp], L)
+                ts(lim, ap(lim), ap(A2), -1.0, AL.mult, ap(nth), AL.add, [A2, nth], 1)
+        lab[0] = "g%d order" % gen
+        xo, hs = ps(BY[ny[0] % len(BY)], 0, L + 1), [u[k] for u in st for k in ("cum", "ohh")]
+        mms([xo], hs + [Idb, I512, Tri, neg1], [[(ap(xo, L), ap(Tri), ap(cum, L - 1)), (ap(xo, L), ap(I512), ap(neg1))],
+                                                [(ap(xo, 0, L), ap(Idb), ap(cum)), (ap(xo, 0, L), ap(I512), ap(oh))]], 2 * L + 128, boost=20)
+        q1 = tile("bf", L)
+        ts(q1, ap(q1), ap(xo, 0, L), ap(xo, L), AL.add, 0.0, AL.max, [xo], L, boost=20)
+        op_ = ps(BY[(ny[0] + 1) % len(BY)], 0, C)
+        ny[0] += 2
+        mms([op_], [q1, Zb], [[(ap(op_), Z(Zb, r), ap(q1, r, L, 16)) for r in range(16)]], 1024, boost=20)
+        po, pm, srt, prev = tile("u16", C), tile("u16", C), tile("f32", L), tile("f32", 48)
+        ts(po, ap(po), ap(op_), -1.0, AL.mult, float(L), AL.add, [op_], C, boost=20)
+        ipo = send([(po, ap(po), pm, ap(pm), -2)], boost=20)
 
         def scat(srt=srt, po=po, dau=dau):
             return [g.vector.tensor_copy(ap(srt).indirect(ap(po)), ap(dau))]
-        y1, y2, y3, y4 = tile("f32", 12), tile("f32", 12), tile("f32", 12), tile("f32", 12)
-        ts(y1, ap(y1), ap(op_, 0, 12), 145.0, AL.is_ge, None, None, [op_], 12)
-        tt(y2, ap(y2), ap(i144), ap(op_, 0, 12), AL.subtract, [i144, op_], 12)
-        tt(y3, ap(y3), ap(y1), ap(y2), AL.mult, [y1, y2], 12)
-        iy4 = tt(y4, ap(y4), ap(y3), ap(i48), AL.add, [y3, i48], 12)
-        Lm, Ln, prev = tile("f32", 12), tile("u16", 12), tile("f32", 48)
-        send(y4, ap(y4), [(Lm, ap(Lm), -2)])
-        isc = task("V", gc_(L, "scatter"), [po, dau], [srt], scat)
-        soft(isc, iy4)
-        soft(iput, isc)
-        best = mk(srt["b"], srt["lo"], 48)
-        best["wr"] = srt["wr"]
-        soft(ian, send(best, ap(best), [(own, ap(own, 0, 48), -2), (prev, ap(prev), -1)]))
-        tcopy(Ln, ap(Ln), ap(Lm), [Lm], 12)
-        own2 = mk(own["b"], own["lo"], own["n"])
-        own2["wr"] = list(own["wr"])
-        tcopy(own2, ap(own, 1, 48, 2), ap(prev, 1, 48, 2), [own, prev], 24)
-        new = tile("f32", 48 + L)
-        tcopy(new, ap(new, 48, 48 + L), ap(own).indirect(ap(Ln)), [own2, Ln], dur=gc_(L))
+        isc = task("V", gc_(L, "scatter"), [po, dau], [srt], scat, boost=20)
+        ibest = send([(srt, ap(srt, L - 48, L), come, ap(come), -2), (srt, ap(srt, L - 48, L), prev, ap(prev), -1)], boost=20)
+        soft(ibest, ipo)
+        soft(st[-1]["send"], ibest)
+        soft(st[-1]["put"], isc)
+        lab[0] = "g%d home" % gen
+        y1 = col([pm], ap(pm), -1.0, AL.mult, 239.0, AL.add, n=C)
+        y2 = col([pm], ap(pm), -256.0, AL.mult, 48.0 * 256, AL.add, n=C)
+        y3, y4, Ln = tile("f32", C), tile("f32", C), tile("u16", C)
+        tt(y3, ap(y3), ap(y1), ap(y2), AL.min, [y1, y2], C)
+        tt(y4, ap(y4), ap(y3), ap(ii), AL.max, [y3, ii], C)
+        tcopy(Ln, ap(Ln), ap(y4), [y4], C)
+        merged = part(win, L, 48)
+        tcopy(merged, ap(come, 0, 48, 2), ap(prev, 0, 48, 2), [come, prev], 24)
         if gen < GENS - 1:
-            tcopy(G, ap(G, 0, GW, 8), ap(new, 48, 48 + L), [new], L)
-        own = new
+            tcopy(G, ap(G, 0, GW, 8), ap(win).indirect(ap(Ln)), [own, merged, Ln], dur=gc_(L))
+    lab[0] = "out"
     yo, ao, so = tile("f32", L), tile("f32", L), tile("f32", L)
-    act(yo, ap(yo), ap(own, 48, 48 + L), AF.Copy, [own], L, bias=1536.0)
+    ts(yo, ap(yo), ap(win).indirect(ap(Ln)), 1536.0, AL.add, None, None, [own, merged, Ln], L, dur=gc_(L))
     store(T.yg[:], ap(yo), [yo])
-    act(ao, ap(ao), ap(a), AF.Copy, [a], L)
+    for h, (i0, W, _) in enumerate(HV):
+        act(ao, ap(ao, i0, i0 + W), ap(a[h]), AF.Copy, [a[h]], W)
     store(T.ya[:], ap(ao), [ao])
-    sp = ps(0)
-    mms(sp, [X, Idb], [(ap(sp, 0, L), ap(Idb), ap(X, s, XW, 16), s == 0, s == 15, L) for s in range(16)])
-    act(so, ap(so), ap(sp, 0, L), AF.Copy, [sp], L)
+    sp = ps(BW[0], 0, L)
+    mms([sp], [X, Idb], [[(ap(sp), ap(Idb), ap(X, s, XW, 16)) for s in range(16)]], 16 * L)
+    act(so, ap(so), ap(sp), AF.Copy, [sp], L)
     store(T.ys[:], ap(so), [so])
     emit(g, T, tasks)
 
@@ -476,33 +501,51 @@ def tid(d):
 
 def order(tasks):
     n = len(tasks)
-    succ, left = [[] for _ in range(n)], [0] * n
+    pred, succ = [[] for _ in range(n)], [[] for _ in range(n)]
     for i, t in enumerate(tasks):
         for d, lag in t["deps"].items():
+            lag += COST["sem"] if tasks[tid(d)]["q"] != t["q"] else COST["own"] * (d not in t["soft"])
+            pred[i].append((tid(d), lag))
             succ[tid(d)].append((i, lag))
-        left[i] = len(t["deps"])
-    need, topo_order = list(left), [i for i in range(n) if not left[i]]
-    for i in topo_order:
+    dur = [0.05 if t["kind"] == "d" else t["dur"] for t in tasks]
+    tail = [t["dur"] - u for t, u in zip(tasks, dur)]
+
+    def place(before, after, key, first):
+        left, end, busy = [len(p) for p in before], [0.0] * n, {}
+        ready = sorted((key[i], i) for i in range(n) if not left[i])
+        while ready:
+            _, i = ready.pop(0)
+            st, line, at = max([end[j] + lag for j, lag in before[i]] + [first[i]]), busy.setdefault(tasks[i]["q"], []), 0
+            while at < len(line) and line[at][0] < st + dur[i] - 1e-9:
+                st, at = max(st, line[at][1]), at + 1
+            line.insert(at, (st, st + dur[i]))
+            end[i] = st + dur[i]
+            new = []
+            for j, _ in after[i]:
+                left[j] -= 1
+                if not left[j]:
+                    new.append((key[j], j))
+            if new:
+                ready = sorted(ready + new)
+        return end
+    line, need = [], [len(p) for p in pred]
+    line += [i for i in range(n) if not need[i]]
+    for i in line:
         for j, _ in succ[i]:
             need[j] -= 1
             if not need[j]:
-                topo_order.append(j)
-    assert len(topo_order) == n
-    prio = [0.0] * n
-    for i in reversed(topo_order):
-        prio[i] = tasks[i]["dur"] + max([prio[j] + COST["sem"] + lag for j, lag in succ[i]], default=0.0)
-    free, fin, out = {}, [0.0] * n, []
-    avail = {i: 0.0 for i in range(n) if not left[i]}
-    while avail:
-        st, _, i = min((max(r, free.get(tasks[i]["q"], 0.0)), -prio[i] - tasks[i]["boost"], i) for i, r in avail.items())
-        del avail[i]
-        fin[i] = free[tasks[i]["q"]] = st + tasks[i]["dur"]
-        out.append(i)
-        for j, _ in succ[i]:
-            left[j] -= 1
-            if not left[j]:
-                avail[j] = max(fin[tid(d)] + lag + COST["sem"] for d, lag in tasks[j]["deps"].items())
-    return out
+                line.append(j)
+    assert len(line) == n
+    key = [t["turn"] for t in tasks]
+    best = None
+    for _ in range(CFG["passes"]):
+        end = place(pred, succ, key, [0.0] * n)
+        span = max(e + u for e, u in zip(end, tail))
+        if best is None or span < best[0]:
+            best = (span, end)
+        key = [-e for e in place(succ, pred, [-e - u for e, u in zip(end, tail)], tail)]
+    rank = {i: j for j, i in enumerate(line)}
+    return sorted(range(n), key=lambda i: (best[1][i] - dur[i], rank[i]))
 
 
 def emit(g, T, tasks):
@@ -511,8 +554,11 @@ def emit(g, T, tasks):
     count = {s: 0 for s in sem_of.values()}
     known, done = {q: {} for q in eng}, {}
     sent, ends = 0, []
-    for i in order(tasks):
+    if not ORDER:
+        ORDER.extend(order(tasks))
+    for i in ORDER:
         t = tasks[i]
+        NOTE[0] = t["lab"]
         q = t["q"]
         k, need = known[q], {}
         for d in t["deps"]:

@@ -1,3 +1,4 @@
+import numpy as np
 from concourse.bass import DstId, RemoteDMATransfer
 from concourse.mybir import AluOpType, ActivationFunctionType
 
@@ -6,17 +7,20 @@ NR, L, ST, GENS = 8, 192, 3, 2
 GW, XW = 1536, 3072
 C = 12
 CFG = {"halves": [(0, 96, (32, 32, 32)), (96, 96, (32, 32, 32))],
-       "rec": {0: "SSSSSV", 1: "SSSSSS", 2: "SSSSSS"},
-       "kg": 4, "passes": 4}
-PLAN = {"step": 14.0, "half": 5.5, "end": 6.0, "lists": (0, 0), "names": (1.35, 0.95), "records": (2.4, 0.95), "sums": (6.5, 0.4),
-        "first": (8.5, 0), "put": (11.0, 0), "info": (11.5, 0)}
+       "rec": (("SSS", "SVV"), ("SSS", "SSV"), ("SSS", "SSV")),
+       "kg": 4, "pre": 3, "pcut": 2, "xat": 2, "pq": "VV", "aq": "SS", "passes": 1500, "seed": 1}
+PLAN = {"mask": (-3.4, 0), "hosts": (-2.3, 0), "names": (-2.3, 1.0), "rows": (-1.0, 1.5), "list": (-0.2, 1.0), "records": (0.2, 0.5), "T": (1.1, 0),
+        "old": (2.0, 0), "val": (2.7, 0), "pre": (2.0, 0), "add": (3.0, 0.3), "abs": (3.4, 0.4), "sum": (3.9, 0.4), "sign": (5.4, 0), "err": (5.5, 0),
+        "first": (5.8, 0), "pick": (5.8, 0), "place": (6.1, 0), "wrap": (6.8, 0), "lists": (7.0, 0), "new": (7.3, 0), "put": (7.5, 0), "name": (6.9, 0),
+        "rows out": (7.9, 0), "count": (8.4, 0), "limit": (9.6, 0), "order": (5.9, 0), "home": (13.0, 0), "mother": (2.5, 0),
+        "start": ((6.0, 11.8), (19.8, 26.6), (34.6, 40.2)), "generation": 48}
 POOL = {"f32": ("float32", 7000), "bf": ("bfloat16", 48000), "hf": ("float16", 30000), "u16": ("uint16", 6000), "i32": ("int32", 3600)}
 SIZE = {"f32": 4, "bf": 2, "hf": 2, "u16": 2, "i32": 4}
 SCRATCH = {"p_" + k: ("sbuf", [128, v[1]], v[0]) for k, v in POOL.items()}
 SCRATCH.update({"bank%d" % b: ("psum", [128, 512], "float32") for b in range(8)})
-SEMAPHORES = ["sV", "sS", "sP", "sG", "left"] + ["d%d" % i for i in range(16)] + ["r%d" % i for i in range(60)]
+SEMAPHORES = ["sV", "sS", "sP", "sG", "left"] + ["d%d" % i for i in range(20)] + ["r%d" % i for i in range(60)]
 CY = 0.00083
-COST = {"f": 1.25, "fix": 0.0, "gather": 1.56, "scatter": 3.5, "issue": 0.9, "hop": 1.9, "sem": 0.12, "own": 0.0, "pe": 0.00042}
+COST = {"f": 1.25, "gather": 1.56, "scatter": 3.5, "issue": 0.9, "hop": 2.2, "spread": (-0.8, 1.0), "sem": 0.08, "pe": 0.00042}
 NOTE, ORDER = [""], []
 
 
@@ -26,7 +30,7 @@ def rank_program(g, core, T, topo):
         return
     tasks, used = [], {k: 0 for k in POOL}
     bank_use = [{"q": None, "now": [], "before": []} for _ in range(8)]
-    ndma, nrem, lab, turn = [0], [0], [""], [0.0]
+    ndma, nrem, lab, turn = [0], [0], [""], [None]
 
     def mk(b, lo, n, mut=False):
         return {"b": b, "lo": lo, "n": n, "wr": [], "rd": [], "mut": mut}
@@ -50,7 +54,7 @@ def rank_program(g, core, T, topo):
         buf = T[t["b"]]
         return buf[:, t["lo"] + a:t["lo"] + b] if st == 1 else buf[:, t["lo"] + a:t["lo"] + b:st]
 
-    def task(q, dur, ins, outs, fn, kind="c", extra=None, boost=0.0):
+    def task(q, dur, ins, outs, fn, kind="c", extra=None, at=0.0):
         i, deps = len(tasks), {}
         for t in ins:
             for w, lag in t["wr"]:
@@ -70,7 +74,8 @@ def rank_program(g, core, T, topo):
                     deps.setdefault(j, 0)
                 bu["now"].append(i)
         deps.pop(i, None)
-        tasks.append({"q": q, "dur": dur, "deps": deps, "fn": fn, "kind": kind, "x": extra, "soft": set(), "turn": turn[0] - boost, "lab": lab[0]})
+        tasks.append({"q": q, "dur": dur, "deps": deps, "fn": fn, "kind": kind, "x": extra, "soft": set(),
+                      "turn": turn[0], "at": at or 0.07 * (i - 16), "lab": lab[0]})
         for t in outs:
             if t["mut"]:
                 t["wr"], t["rd"] = [], []
@@ -84,33 +89,39 @@ def rank_program(g, core, T, topo):
             tasks[i]["deps"][j] = 0
             tasks[i]["soft"].add(j)
 
+    def when(gen, t, h, what, j=0):
+        turn[0] = (gen, t, h, what, j)
+
     def vc(n, f=1.0):
-        return (COST["fix"] + max(64, n * f) * CY) * COST["f"]
+        return max(64, n * f) * CY * COST["f"]
 
     def gc_(n, k="gather"):
         return (0.06 + n * COST[k] * CY) * COST["f"]
 
-    def ts(out, oa, in0, s1, op0, s2, op1, ins, n, f=1.0, boost=0.0, dur=None):
+    def ts(out, oa, in0, s1, op0, s2, op1, ins, n, f=1.0, at=0.0, dur=None):
         def fn():
             if op1 is None:
                 return [g.vector.tensor_scalar(oa, in0, s1, None, op0)]
             return [g.vector.tensor_scalar(oa, in0, s1, s2, op0, op1)]
-        return task("V", vc(n, f) if dur is None else dur, ins, [out], fn, boost=boost)
+        return task("V", vc(n, f) if dur is None else dur, ins, [out], fn, at=at)
 
-    def tt(out, oa, in0, in1, op, ins, n=0, f=1.0, dur=None, boost=0.0):
-        return task("V", vc(n, f) if dur is None else dur, ins, [out], lambda: [g.vector.tensor_tensor(oa, in0, in1, op)], boost=boost)
+    def tt(out, oa, in0, in1, op, ins, n=0, f=1.0, dur=None):
+        return task("V", vc(n, f) if dur is None else dur, ins, [out], lambda: [g.vector.tensor_tensor(oa, in0, in1, op)])
 
-    def tcopy(out, oa, in0, ins, n=0, f=1.0, dur=None, boost=0.0):
-        return task("V", vc(n, f) if dur is None else dur, ins, [out], lambda: [g.vector.tensor_copy(oa, in0)], boost=boost)
+    def tcopy(out, oa, in0, ins, n=0, f=1.0, dur=None):
+        return task("V", vc(n, f) if dur is None else dur, ins, [out], lambda: [g.vector.tensor_copy(oa, in0)])
 
-    def act(out, oa, in0, func, ins, n=0, dur=None, bias=0.0, scale=1.0, acc=None, boost=0.0):
-        return task("S", (vc(n) if dur is None else dur) + (0.02 if acc else 0), ins, [out] + ([acc] if acc else []),
-                    lambda: [g.scalar.activation(oa, in0, func, bias=bias, scale=scale, accum_out=ap(acc) if acc else None)], boost=boost)
+    def act(out, oa, in0, func, ins, n=0, dur=None, bias=0.0, scale=1.0, acc=None):
+        return task("S", vc(n) if dur is None else dur, ins, [out] + ([acc] if acc else []),
+                    lambda: [g.scalar.activation(oa, in0, func, bias=bias, scale=scale, accum_out=ap(acc) if acc else None)])
+
+    def copy(q, out, oa, in0, ins, n=0, dur=None):
+        return tcopy(out, oa, in0, ins, n, dur=dur) if q == "V" else act(out, oa, in0, AF.Copy, ins, n, dur=dur)
 
     def iota(out, pat, base, cm, flag=True):
         task("G", 0.16 + 2.5 * out["n"] * CY, [], [out], lambda: [g.iota(ap(out), pat, base, cm, allow_small_or_imprecise_dtypes=flag)])
 
-    def mms(outs, ins, groups, n, boost=0.0, after=None, ends=(True, True)):
+    def mms(outs, ins, groups, n, after=None, ends=(True, True)):
         def fn():
             r = []
             for gr in groups:
@@ -118,14 +129,14 @@ def rank_program(g, core, T, topo):
                     m = g.tensor.matmul(o, l, x, ends[0] and j == 0, ends[1] and j == len(gr) - 1)
                 r.append(m)
             return r
-        i = task("P", (0.04 + n * COST["pe"]) * COST["f"], ins, outs, fn, boost=boost)
+        i = task("P", (0.02 + n * COST["pe"]) * COST["f"], ins, outs, fn)
         if after:
             for w, _ in after["wr"][:-1]:
                 soft(i, w)
         return i
 
     def load(out, oa, src, dur, q="Y"):
-        i = task(q, 0.05, [], [out], lambda: [(g.sync if q == "Y" else g.scalar).dma_start(oa, src)], "d", ndma[0], boost=1000)
+        i = task(q, 0.05, [], [out], lambda: [(g.sync if q == "Y" else g.scalar).dma_start(oa, src)], "d", ndma[0], at=-5.0)
         out["wr"] = [(w, dur if w == i else lg) for w, lg in out["wr"]]
         ndma[0] += 1
         return i
@@ -137,7 +148,7 @@ def rank_program(g, core, T, topo):
     def engines(a, b):
         return topo.engines(a, b)[:8]
 
-    def send(moves, boost=0.0):
+    def send(moves):
         got, out, n, trs = [], [], len(moves), []
         for m, (src, sa, dst, da, d) in enumerate(moves):
             to, fr = T.cores[(rank + d) % NR], T.cores[(rank - d) % NR]
@@ -158,7 +169,7 @@ def rank_program(g, core, T, topo):
                 g.remote_dma_fused([RemoteDMATransfer(dst_ids=[DstId(rid=rid, pnc=pid)], dma_engine_mask=mask, remote_sem=T.sem[name], src=sa, dst=da)
                                     for rid, pid, mask, name, sa, da in trs], local_sem=T.sem.left)
             return []
-        i = task("G", COST["issue"], [m[0] for m in moves], [], fn, "r", (got, sum(out)), boost)
+        i = task("G", COST["issue"] + (1.5 if nrem[0] == 1 else 0), [m[0] for m in moves], [], fn, "r", (got, sum(out)))
         for m, (src, sa, dst, da, d) in enumerate(moves):
             dst["wr"].append(((i, m), COST["hop"] + n * dst["n"] * SIZE[dst["b"][2:]] * 128 / 60000.0))
         return i
@@ -168,11 +179,17 @@ def rank_program(g, core, T, topo):
     X, a0 = tile("bf", XW, True), tile("bf", L)
     NG = 4
     gh = [part(gni, GW // NG * j, GW // NG) for j in range(NG)]
-    nh = [part(nbi, 8 * i0, 8 * W) for i0, W, _ in HV]
-    seq = [load(gh[j], ap(gh[j]), T.gn[:, GW // NG * j:GW // NG * (j + 1)], 2.2 + 0.6 * j) for j in range(NG)]
-    seq.append(load(nh[0], ap(nh[0]), T.nb[:, 0:nh[0]["n"]], 5.2))
-    seq.append(load(X, ap(X), T.x[:], 7.6))
-    seq.append(load(nh[1], ap(nh[1]), T.nb[:, nh[0]["n"]:GW], 8.8))
+    seq = [load(gh[j], ap(gh[j]), T.gn[:, GW // NG * j:GW // NG * (j + 1)], 2.4 + 0.45 * j) for j in range(NG)]
+    nh, at = [], 3.6
+    for i0, W, pieces in HV:
+        for pw in pieces if i0 == 0 else (W,):
+            if len(nh) == CFG["xat"]:
+                at += 2.0
+                seq.append(load(X, ap(X), T.x[:], at))
+            at += pw / 96.0
+            nh.append(part(nbi, 8 * i0, 8 * pw))
+            seq.append(load(nh[-1], ap(nh[-1]), T.nb[:, 8 * i0:8 * (i0 + pw)], at))
+            i0 += pw
     for u, v in zip(seq, seq[1:]):
         soft(v, u)
     load(thi, ap(thi), T.th[:], 2.0, "S")
@@ -209,17 +226,19 @@ def rank_program(g, core, T, topo):
     gi = col([ip], ap(ip), 4, AL.arith_shift_right, pool="i32")
     scol = col([si], ap(si), 0.0, AL.add)
     zc = col([gi], ap(gi), 16.0, AL.mult, 15.0, AL.add)
+    row = {0: col([scol], ap(scol), 0.0, AL.is_equal)}
+    Zb = col([im, zc], ap(im), ap(zc), AL.is_equal, n=144, pool="bf")
     gcol = col([gi], ap(gi), 0.0, AL.add)
     pcol = col([ip], ap(ip), 0.0, AL.add)
-    row = {r: col([scol], ap(scol), float(r), AL.is_equal) for r in (0, 3, 4)}
+    row.update({r: col([scol], ap(scol), float(r), AL.is_equal) for r in (3, 4)})
     rm3 = col([scol], ap(scol), 3.0, AL.is_ge)
     r01 = col([scol], ap(scol), 2.0, AL.is_lt)
-    mask0 = col([kpat, scol], ap(kpat), ap(scol), AL.is_equal, n=16 * PW, pool="bf", f=0.5)
-    Zb = col([im, zc], ap(im), ap(zc), AL.is_equal, n=144, pool="bf")
-    Idb = col([im, pcol], ap(im, 0, 128), ap(pcol), AL.is_equal, n=128, pool="bf")
+    Idw = col([im, pcol], ap(im), ap(pcol), AL.is_equal, n=144, pool="bf")
+    Idb = dict(Idw, n=128)
     Blk = col([mgf, gcol], ap(mgf), ap(gcol), AL.is_equal, n=128, pool="bf")
     lt = col([im, pcol], ap(im, 0, 128), ap(pcol), AL.is_gt, n=128, pool="bf")
-    Tri, M1, M2, PNm = tile("bf", 128), tile("bf", 128), tile("bf", 128), tile("bf", 128)
+    mask0 = col([kpat, scol], ap(kpat), ap(scol), AL.is_equal, n=16 * PW, pool="bf", f=0.5)
+    Tri, M1, M2, PNm, Dm = tile("bf", 128), tile("bf", 128), tile("bf", 128), tile("bf", 128), tile("bf", 128)
     Zn, Im, I16n, I512, I15 = acol(Zb, -1.0), acol(Idb, -1.0), acol(Idb, -16.0), acol(Idb, 512.0), acol(Idb, 15.0)
     tt(Tri, ap(Tri), ap(lt), ap(Blk), AL.mult, [lt, Blk], 128, 2)
     tt(M1, ap(M1), ap(Tri), ap(I16n), AL.add, [Tri, I16n], 128, 2)
@@ -228,13 +247,13 @@ def rank_program(g, core, T, topo):
     pn2 = col([pni], ap(pni), 15, AL.bitwise_and, n=128, pool="i32")
     tt(PNm, ap(PNm), ap(pn2), ap(Blk), AL.mult, [pn2, Blk], 128, 2)
     th1 = acol(scol, 1.0, 16.0, "f32")
-    n0 = acol(row[0], -16.0, 0.0, "f32")
-    th2 = acol(th1, 1.0, n0, "f32")
-    e3 = acol(scol, 1.0, -3.0, "f32")
-    r4n = acol(row[4], -1.0, 0.0, "f32")
-    R3, R4n, K4, K01, Bn = acol(Blk, row[3]), acol(Blk, r4n), acol(Idb, row[4]), acol(Idb, r01), acol(Blk, -1.0)
+    th2 = acol(th1, 1.0, acol(row[0], -16.0, 0.0, "f32"), "f32")
+    e3 = acol(scol, 32.0, -80.0, "f32")
+    tt(Dm, ap(Dm), ap(Idw, 0, 128), ap(Idw, 1, 129), AL.subtract, [Idw], 128, 2)
+    D512, c320 = acol(Dm, 512.0), acol(scol, 0.0, -0.625)
+    R3, R4n = acol(Blk, acol(row[3], 32.0, 0.0, "f32")), acol(Blk, acol(row[4], -1.0, 0.0, "f32"))
+    K4, K01 = acol(Idb, row[4]), acol(Idb, r01)
     ones = acol(il, 0.0, 1.0)
-    neg1 = acol(scol, 0.0, -1.0)
     oh0 = acol(ones, row[0], n=128)
     i8 = acol(il, 8.0)
     cki = col([ckr], ap(ckr), 15, AL.bitwise_and, n=16, pool="i32")
@@ -243,33 +262,30 @@ def rank_program(g, core, T, topo):
     nth = col([thi], ap(thi), -1.0, AL.mult, -0.5, AL.add)
     b3, dfl = {}, {}
     for i0, W, _ in HV:
-        cw, c0, pad = W // 16, i0 // 16, -(W // 16) % 8
+        cw, c0 = W // 16, i0 // 16
         if W not in b3:
             b3[W] = acol(scol, -1023.0, 2.0 * W - 16384.0, "f32")
         for t in range(2):
-            d = dfl[i0, t] = tile("bf", pad + 3 * cw)
-            acol(ones, 0.0, n=pad + cw, out=d)
-            if t == 0:
-                d = dict(d, mut=True)
-                acol(ii, 8.0, a=c0, n=cw, out=d, o=pad)
-                dfl[i0, t] = d = dict(d, mut=False)
-            acol(ii, 16.0, a=c0, n=cw, out=d, o=pad + cw)
-            acol(ii, 1.0, -float(i0), a=c0, n=cw, out=d, o=pad + 2 * cw)
+            d = dfl[i0, t] = tile("bf", 3 * cw)
+            acol(ii, 8.0 * (1 - t), a=c0, n=cw, out=d)
+            acol(ii, 16.0, a=c0, n=cw, out=d, o=cw)
+            acol(ii, 1.0, -float(i0), a=c0, n=cw, out=d, o=2 * cw)
     lab[0] = "conv"
     G = tile("f32", GW)
     for j in range(NG):
-        ts(G, ap(G, GW // NG * j, GW // NG * (j + 1)), ap(gh[j]), -1536.0, AL.add, None, None, [gh[j]], GW // NG, boost=100)
+        ts(G, ap(G, GW // NG * j, GW // NG * (j + 1)), ap(gh[j]), -1536.0, AL.add, None, None, [gh[j]], GW // NG, at=2.2 + 0.5 * j)
     G["mut"] = True
     El0, NB0 = [], []
-    for h, (i0, W, _) in enumerate(HV):
-        El0.append(tile("u16", W))
-        tcopy(El0[h], ap(El0[h]), ap(nh[h], 0, 8 * W, 8), [nh[h]], W, boost=100)
+    for h, (i0, W, pieces) in enumerate(HV):
+        El0.append([])
+        when(0, 0, h, "hosts")
+        for j, pw in enumerate(pieces):
+            El0[h].append(tile("u16", pw))
+            o = 8 * (i0 + sum(pieces[:j]))
+            tcopy(El0[h][j], ap(El0[h][j]), ap(nbi, o, o + 8 * pw, 8), [nh[j] if h == 0 else nh[-1]], pw)
         NB0.append(tile("hf", W))
-        tcopy(NB0[h], ap(NB0[h]), ap(nh[h], 0, 8 * W, 8), [nh[h]], W)
-
-    def when(gen, t, h, what, j=0):
-        at, step = PLAN[what]
-        turn[0] = (gen * ST + t + 1) * PLAN["step"] + gen * PLAN["end"] + h * PLAN["half"] + at + j * step
+        when(0, 0, h, "old")
+        tcopy(NB0[h], ap(NB0[h]), ap(nbi, 8 * i0, 8 * (i0 + W), 8), nh, W)
 
     def Z(z, k):
         return ap(z, 15 - k, 143 - k)
@@ -283,40 +299,42 @@ def rank_program(g, core, T, topo):
         p["wr"] = a0["wr"]
     for gen in range(GENS):
         lab[0] = "g%d mother" % gen
-        when(gen, 0, 0, "sums")
+        when(gen, 0, 0, "mother")
         mo, mother, win = tile("hf", L), tile("hf", L), tile("f32", L + 48)
         own, come = part(win, 0, L), part(win, L, 48)
-        ts(mo, ap(mo), ap(G, 0, GW, 8), ap(rm3), AL.mult, None, None, [G, rm3], L, boost=-30)
-        send([(mo, ap(mo), mother, ap(mother), 2)], boost=-30)
-        act(own, ap(own), ap(G, 0, GW, 8), AF.Copy, [G], L, boost=-30)
+        ts(mo, ap(mo), ap(G, 0, GW, 8), ap(rm3), AL.mult, None, None, [G, rm3], L)
+        send([(mo, ap(mo), mother, ap(mother), 2)])
+        act(own, ap(own), ap(G, 0, GW, 8), AF.Copy, [G], L)
         R, info = [None] * len(HV), [None] * len(HV)
         oh, cum, dau = tile("bf", L), tile("bf", L), tile("f32", L)
         for t in range(ST):
             last, st = t == ST - 1, []
             for h, (i0, W, pieces) in enumerate(HV):
                 lab[0] = "g%d t%d h%d front" % (gen, t, h)
-                when(gen, t, h, "lists")
-                cw, pad = W // 16, -(W // 16) % 8
+                cw = W // 16
                 Gg, Wl, Tb = tile("hf", 17 * W), tile("u16", cw + W), tile("bf", 18 * W)
                 Wp, nM, Tt, recs = ps(BW[h], 0, cw + W), part(Gg, 0, W), part(Tb, 0, W), []
-                s = {"Gg": Gg, "Tb": Tb, "Wp": Wp, "nM": nM, "T": Tt, "recs": recs, "R": R[h]}
+                s = {"Tb": Tb, "Wp": Wp, "nM": nM, "T": Tt, "recs": recs}
                 if t == 0:
+                    when(gen, t, h, "hosts")
                     ts(nM, ap(nM), ap(G, 8 * i0, 8 * (i0 + W), 8), ap(row[0]), AL.mult, None, None, [G, row[0]], W)
                     s["oh"], s["nb"] = oh0, NB0[h]
                 else:
-                    Rm, o = R[h], W + pad
-                    El = mk(Rm["b"], Rm["lo"] + o + cw, W)
-                    tcopy(El, ap(El), ap(nbi).indirect(ap(Rm, o, o + cw)), nh + [Rm], dur=gc_(W))
+                    Rp, Rm = R[h]
+                    when(gen, t, h, "mask")
                     mask = part(masks[h], 0, 17 * W)
                     s["oh"] = part(mask, 0, W)
-                    ts(s["oh"], ap(mask, 0, W), ap(Rm, 0, W), ap(ck, 0, 1), AL.is_equal, None, None, [Rm, ck], W, 0.5)
+                    ts(s["oh"], ap(mask, 0, W), ap(Rp), ap(ck, 0, 1), AL.is_equal, None, None, [Rp, ck], W, 0.5)
                     for k in range(16):
-                        ts(mask, ap(mask, W + k, 17 * W, 16), ap(Rm, 0, W), ap(ck, k, k + 1), AL.is_equal, None, None, [Rm, ck], W, 0.5)
+                        ts(mask, ap(mask, W + k, 17 * W, 16), ap(Rp), ap(ck, k, k + 1), AL.is_equal, None, None, [Rp, ck], W, 0.5)
+                    when(gen, t, h, "hosts")
+                    El = mk(Rm["b"], Rm["lo"] + cw, W)
+                    tcopy(El, ap(El), ap(nbi).indirect(ap(Rm)), nh + [Rm], dur=gc_(W))
                     if not last:
-                        when(gen, t, h, "sums")
+                        when(gen, t, h, "old")
                         s["nb"], s["hw"] = tile("hf", W), tile("hf", cw)
                         tcopy(s["nb"], ap(s["nb"]), ap(El), [El], W, 0.5)
-                        tcopy(s["hw"], ap(s["hw"]), ap(Rm, o, o + cw), [Rm], cw)
+                        tcopy(s["hw"], ap(s["hw"]), ap(Rm), [Rm], cw)
                 s0 = 0
                 for j, pw in enumerate(pieces):
                     e0, e1 = (0 if j == 0 else W + 16 * s0), W + 16 * (s0 + pw)
@@ -324,22 +342,24 @@ def rank_program(g, core, T, topo):
                     Gp = part(Gg, e0, e1 - e0)
                     when(gen, t, h, "names", j)
                     if t == 0:
-                        tt(Gp, ap(Gg, W + 16 * s0, e1), ap(G).indirect(ap(El0[h], s0, s0 + pw)), ap(mask0, 0, 16 * pw), AL.mult, [G, El0[h], mask0], dur=gc_(16 * pw))
+                        tt(Gp, ap(Gg, W + 16 * s0, e1), ap(G).indirect(ap(El0[h][j])), ap(mask0, 0, 16 * pw), AL.mult, [G, El0[h][j], mask0], dur=gc_(16 * pw))
                     else:
-                        tt(Gp, ap(Gp), ap(G).indirect(ap(Rm, o + l0, o + l1)), ap(mask, e0, e1), AL.mult, [G, El, mask, s["oh"]], dur=gc_(e1 - e0))
+                        tt(Gp, ap(Gp), ap(G).indirect(ap(Rm, l0, l1)), ap(mask, e0, e1), AL.mult, [G, El, mask, s["oh"]], dur=gc_(e1 - e0))
                         if j == 0:
                             nM["wr"] = Gp["wr"]
-                    Wq = ps(BW[h], l0, l1 - l0)
-                    when(gen, t, h, "records", j)
-                    mms([Wq, Wp], [Gp, nM, Zb], [[(ap(Wq), Z(Zb, k), ap(Gp, k, e1 - e0, 16)) for k in range(16)]], 16 * max(64, l1 - l0))
+                    Wq, pc = ps(BW[h], l0, l1 - l0), CFG["pcut"]
+                    when(gen, t, h, "rows", j)
+                    for c in range(pc):
+                        mms([Wq, Wp], [Gp, nM, Zb], [[(ap(Wq), Z(Zb, k), ap(Gp, k, e1 - e0, 16)) for k in range(16 * c // pc, 16 * (c + 1) // pc)]],
+                            16 // pc * max(64, l1 - l0), after=Wq, ends=(c == 0, c == pc - 1))
                     Wj, rec = part(Wl, l0, l1 - l0), part(Tb, W + e0, e1 - e0)
+                    when(gen, t, h, "list", j)
                     ts(Wj, ap(Wj), ap(Wq), 1536.0, AL.add, None, None, [Wq], l1 - l0)
-                    if CFG["rec"][t][sum(len(x[2]) for x in HV[:h]) + j] == "V":
-                        tcopy(rec, ap(rec), ap(X).indirect(ap(Wj)), [X, Wj], dur=gc_(e1 - e0))
-                    else:
-                        act(rec, ap(rec), ap(X).indirect(ap(Wj)), AF.Copy, [X, Wj], dur=gc_(e1 - e0))
+                    when(gen, t, h, "records", j)
+                    copy(CFG["rec"][t][h][j], rec, ap(rec), ap(X).indirect(ap(Wj)), [X, Wj], dur=gc_(e1 - e0))
                     recs.append(rec)
                     if j == 0:
+                        when(gen, t, h, "T")
                         dq = ps(BD[h], 0, W)
                         mms([dq], [rec, a[h], Idb, Im], [[(ap(dq), ap(Idb), ap(rec, 0, W)), (ap(dq), ap(Im), ap(a[h]))]], 2 * W)
                         act(Tt, ap(Tt), ap(dq), AF.Abs, [dq], W)
@@ -348,74 +368,96 @@ def rank_program(g, core, T, topo):
             cnt = ps(BM, 128, L)
             for h, (i0, W, pieces) in enumerate(HV):
                 lab[0] = "g%d t%d h%d mid" % (gen, t, h)
-                when(gen, t, h, "sums")
                 s = st[h]
-                cw, pad = W // 16, -(W // 16) % 8
+                cw = W // 16
                 Tb, Tt, recs, Wp, nM = s["Tb"], s["T"], s["recs"], s["Wp"], s["nM"]
-                val = ps(BW[h], 256, 2 * W)
+                when(gen, t, h, "val")
+                val, x3 = ps(BW[h], 144, 2 * W), ps(BW[h], 144 + 2 * W, W)
                 grp, ins = [[(ap(val, W, 2 * W), ap(PNm), ap(s["oh"], 0, W))]], [PNm, s["oh"]]
                 if not last:
                     old = (ap(Im), ap(i8, i0, i0 + W)) if t == 0 else (ap(R4n), ap(info[h]))
                     grp.append([(ap(val, 0, W), ap(Idb), ap(s["nb"])), (ap(val, 0, W),) + old])
                     ins += [Idb, s["nb"], Im, i8] + ([R4n, info[h]] if t else [])
                 mms([val], ins, grp, 3 * W)
-                D = ps(BD[h], 0, W)
+                D, Ys = ps(BD[h], 0, W), []
                 for q in range(16 // KG):
-                    Y, ya = ps(BY[ny[0] % len(BY)], 0, KG * W), part(yas[h], q * KG * W, KG * W)
+                    Ys.append(ps(BY[ny[0] % len(BY)], 0, KG * W))
                     ny[0] += 1
-                    when(gen, t, h, "sums", q)
-                    ks = range(q * KG, q * KG + KG)
-                    mms([Y], recs + [Idb, Tt], [[(ap(Y, (k % KG) * W, (k % KG + 1) * W), ap(Idb), x) for x in (ap(Tb, 2 * W + k, 18 * W, 16), ap(Tt))] for k in ks], 2 * KG * W)
+                    if q < CFG["pre"]:
+                        when(gen, t, h, "pre", q)
+                        mms([Ys[q]], [Idb, Tt], [[(ap(Ys[q], k * W, k * W + W), ap(Idb), ap(Tt)) for k in range(KG)]], KG * W, ends=(True, False))
+                for q, Y in enumerate(Ys):
+                    ya = part(yas[h], q * KG * W, KG * W)
+                    when(gen, t, h, "add", q)
+                    vs = [(ap(Y, k * W, k * W + W), ap(Idb), ap(Tb, 2 * W + q * KG + k, 18 * W, 16)) for k in range(KG)]
+                    if q < CFG["pre"]:
+                        mms([Y], recs + [Idb], [vs], KG * W, after=Y, ends=(False, True))
+                    else:
+                        mms([Y], recs + [Idb, Tt], [[v, (v[0], ap(Idb), ap(Tt))] for v in vs], 2 * KG * W)
+                    when(gen, t, h, "abs", q)
                     act(ya, ap(ya), ap(Y), AF.Abs, [Y], KG * W, bias=-255.0)
-                    mms([D], [ya, Zb], [[(ap(D), Z(Zb, k), ap(ya, (k % KG) * W, (k % KG + 1) * W)) for k in ks]], KG * W, after=D, ends=(q == 0, q == 16 // KG - 1))
+                    when(gen, t, h, "sum", q)
+                    mms([D], [ya, Zb], [[(ap(D), Z(Zb, q * KG + k), ap(ya, k * W, k * W + W)) for k in range(KG)]], KG * W, after=D, ends=(q == 0, q == 16 // KG - 1))
                 lab[0] = "g%d t%d h%d tail" % (gen, t, h)
                 sg = tile("bf", W)
-                when(gen, t, h, "first")
+                when(gen, t, h, "sign")
                 act(sg, ap(sg), ap(D), AF.Sign, [D, lim], W, bias=ap(lim))
-                x = ps(BD[h], W, 3 * W)
-                mms([x], [sg, M1, M2, M3, I15, il], [[(ap(x, 0, W), ap(M1), ap(sg))], [(ap(x, W, 2 * W), ap(M2), ap(sg))],
-                                                    [(ap(x, 2 * W, 3 * W), ap(M3), ap(sg)), (ap(x, 2 * W, 3 * W), ap(I15), ap(il, 0, W))]], 4 * W)
-                FF, Q = tile("bf", 2 * W), tile("hf", 3 * W)
-                FI, F2, Qv, Ql = part(FF, 0, W), part(FF, W, W), part(Q, 0, 2 * W), part(Q, 2 * W, W)
-                bo = 20 if last and h == len(HV) - 1 else 0
-                ts(FI, ap(FI), ap(x, 0, W), ap(th1), AL.is_ge, None, None, [x, th1], W, boost=bo)
-                ts(F2, ap(F2), ap(x, W, 2 * W), ap(th2), AL.is_ge, None, None, [x, th2], W)
-                q0 = W if last else 0
-                tt(Qv, ap(Q, q0, 2 * W), ap(val, q0, 2 * W), ap(FF, q0, 2 * W), AL.mult, [val, FI, F2], 2 * W - q0)
-                ts(Ql, ap(Ql), ap(x, 2 * W, 3 * W), ap(b3[W]), AL.add, 0.0, AL.max, [x, b3[W]], W)
-                n, w0 = W + pad + 3 * cw, W + pad
-                Op, O, d = ps(BD[h], 0, n), tile("u16", n), dfl[i0, min(t, 1)]
-                c0 = cw if last else 0
-                grp = [] if last else [[(ap(Op, 0, W), ap(Blk), ap(Q, W, 2 * W))]]
-                gr = [(ap(Op, W, n), ap(Idb), ap(d))] + ([(ap(Op, w0, w0 + cw), ap(Idb), ap(s["hw"]))] if t == 1 else [])
-                gr += [(ap(Op, w0 + c0, n), Z(Zb, r), ap(Q, q0 + r, 3 * W, 16)) for r in range(16)]
-                mms([Op], [Qv, Ql, Zb, Blk, Idb, d] + ([s["hw"]] if t == 1 else []), grp + [gr], 18 * 64 + W)
-                o0 = w0 + cw if last else 0
-                tcopy(O, ap(O, o0, n), ap(Op, o0, n), [Op], n - o0)
-                if not last:
-                    R[h] = tile("u16", w0 + cw + W)
-                    R[h]["n"] = w0 + cw
-                    im1 = send([(O, ap(O, 0, w0 + cw), R[h], ap(R[h]), 1)])
-                an, a2 = tile("bf", W), tile("bf", W)
-                when(gen, t, h, "put")
-                act(an, ap(an), ap(Tb).indirect(ap(O, w0 + 2 * cw, n)), AF.Copy, recs + [Tt, O], dur=gc_(W))
-
-                def put(O=O, an=an, u=w0 + cw, v=w0 + 2 * cw):
-                    return [g.vector.tensor_copy(ap(X).indirect(ap(O, u, v)), ap(an))]
-                s["put"] = task("V", gc_(W, "scatter"), [O, an], [X], put)
-                lab[0] = "g%d t%d h%d info" % (gen, t, h)
-                when(gen, t, h, "first" if last else "info")
                 if last:
-                    Ep = ps(BW[h], 256, W)
-                    mms([Ep], [info[h], FI, R3, Bn], [[(ap(Ep), ap(R3), ap(info[h])), (ap(Ep), ap(Bn), ap(FI))]], 2 * W, boost=bo)
+                    when(gen, t, h, "err")
+                    Ep = ps(BW[h], 144, W)
+                    mms([Ep], [info[h], sg, R3, Blk], [[(ap(Ep), ap(R3), ap(info[h])), (ap(Ep), ap(Blk), ap(sg))]], 2 * W)
                     ohh, cm = part(oh, i0, W), part(cum, i0, W)
-                    ts(ohh, ap(ohh), ap(Ep), ap(e3), AL.is_equal, None, None, [Ep, e3], W, boost=bo)
+                    ts(ohh, ap(ohh), ap(Ep), ap(e3), AL.is_ge, None, None, [Ep, e3], W)
                     before = st[h - 1]["cum"] if h else None
 
                     def scan(ohh=ohh, cm=cm, W=W, before=before):
                         return [g.vector.tensor_tensor_scan(ap(cm), ap(ones, 0, W), ap(ohh), ap(before, before["n"] - 1) if before else 0.0, AL.mult, AL.add)]
-                    task("V", vc(W, 0.5), [ohh, ones] + ([before] if before else []), [cm], scan, boost=bo)
+                    task("V", vc(W, 0.5), [ohh, ones] + ([before] if before else []), [cm], scan)
                     s["cum"], s["ohh"] = cm, ohh
+                when(gen, t, h, "first")
+                x = ps(BD[h], W, 2 * W)
+                mms([x], [sg, M1, M2], [[(ap(x, W, 2 * W), ap(M2), ap(sg))], [(ap(x, 0, W), ap(M1), ap(sg))]], 2 * W)
+                mms([x3], [sg, M3, I15, il], [[(ap(x3), ap(M3), ap(sg)), (ap(x3), ap(I15), ap(il, 0, W))]], 2 * W)
+                FI, F2, Q = tile("bf", W), tile("bf", W), tile("hf", 3 * W)
+                Qh, Qp, Ql = part(Q, 0, W), part(Q, W, W), part(Q, 2 * W, W)
+                ts(F2, ap(F2), ap(x, W, 2 * W), ap(th2), AL.is_ge, None, None, [x, th2], W)
+                tt(Qp, ap(Qp), ap(val, W, 2 * W), ap(F2), AL.mult, [val, F2], W)
+                if not last:
+                    pp, pb = ps(BM, 0, W), tile("bf", W)
+                    mms([pp], [Blk, Qp], [[(ap(pp), ap(Blk), ap(Qp))]], W)
+                when(gen, t, h, "pick")
+                ts(FI, ap(FI), ap(x, 0, W), ap(th1), AL.is_ge, None, None, [x, th1], W)
+                if not last:
+                    tt(Qh, ap(Qh), ap(val, 0, W), ap(FI), AL.mult, [val, FI], W)
+                ts(Ql, ap(Ql), ap(x3), ap(b3[W]), AL.add, 0.0, AL.max, [x3, b3[W]], W)
+                if not last:
+                    when(gen, t, h, "place")
+                    copy(CFG["pq"][h], pb, ap(pb), ap(pp), [pp], W)
+                    Rp, Rm = tile("bf", W), tile("u16", cw + W)
+                    Rm["n"] = cw
+                    R[h] = (Rp, Rm)
+                    im0 = send([(pb, ap(pb), Rp, ap(Rp), 1)])
+                when(gen, t, h, "wrap")
+                n, c0 = 3 * cw, cw if last else 0
+                Op, O, d = ps(BD[h], 0, n), tile("u16", n), dfl[i0, min(t, 1)]
+                gr = [(ap(Op), ap(Idb), ap(d))] + ([(ap(Op, 0, cw), ap(Idb), ap(s["hw"]))] if t == 1 else [])
+                gr += [(ap(Op, c0, n), Z(Zb, r), ap(Q, 16 * c0 + r, 3 * W, 16)) for r in range(16)]
+                mms([Op], [Qh, Qp, Ql, Zb, Idb, d] + ([s["hw"]] if t == 1 else []), [gr], 18 * 64)
+                when(gen, t, h, "lists")
+                tcopy(O, ap(O, c0, n), ap(Op, c0, n), [Op], n - c0)
+                if not last:
+                    im1 = send([(O, ap(O, 0, cw), Rm, ap(Rm), 1)])
+                    soft(im1, im0)
+                an, a2 = tile("bf", W), tile("bf", W)
+                when(gen, t, h, "new")
+                copy(CFG["aq"][h], an, ap(an), ap(Tb).indirect(ap(O, 2 * cw, n)), recs + [Tt, O], dur=gc_(W))
+                when(gen, t, h, "put")
+
+                def put(O=O, an=an, u=cw, v=2 * cw):
+                    return [g.vector.tensor_copy(ap(X).indirect(ap(O, u, v)), ap(an))]
+                task("V", gc_(W, "scatter"), [O, an], [X], put)
+                lab[0] = "g%d t%d h%d info" % (gen, t, h)
+                when(gen, t, h, "name")
                 fo, ch = ps(BM, 0, W), ps(BM, 128 + i0, W)
                 more = not (gen == GENS - 1 and last)
                 mms([fo, ch, cnt], [FI, Blk, ones], [[(ap(fo), ap(Blk), ap(FI))]] + ([[(ap(ch), ap(ones, 0, 128), ap(FI))]] if more else []), 2 * W)
@@ -426,18 +468,19 @@ def rank_program(g, core, T, topo):
                 gr = [(Z(Zb, t), ap(Qe)), (Z(Zb, t), ap(nM)), (Z(Zn, t), ap(Qn))]
                 ins = [Qe, Qn, nM, Zb, Zn]
                 if t == 0:
-                    gr += [(Z(Zn, 3), ap(FI)), (Z(Zb, 4), ap(Q, 0, W)), (ap(K4), ap(i8, i0, i0 + W))]
-                    ins += [FI, Qv, K4, i8]
+                    gr += [(Z(Zn, 3), ap(FI)), (Z(Zb, 4), ap(Qh)), (ap(K4), ap(i8, i0, i0 + W))]
+                    ins += [FI, Qh, K4, i8]
                 elif not last:
                     gr += [(Z(Zn, 3), ap(FI)), (ap(Idb), ap(info[h]))]
                     ins += [FI, Idb, info[h]]
                 else:
                     gr += [(ap(K01), ap(info[h])), (ap(Idb), ap(mother, i0, i0 + W))]
                     ins += [K01, Idb, info[h], mother]
+                when(gen, t, h, "rows out")
                 mms([ip_], ins, [[(ap(ip_),) + u for u in gr]], len(gr) * W)
                 if last:
                     act(dau, ap(dau, i0, i0 + W), ap(ip_), AF.Copy, [ip_], W)
-                    s["send"] = send([(an, ap(an), a2, ap(a2), -2)], boost=-5)
+                    send([(an, ap(an), a2, ap(a2), -2)])
                 else:
                     io, info[h] = tile("hf", W), tile("hf", W)
                     tcopy(io, ap(io), ap(ip_), [ip_], W)
@@ -445,32 +488,33 @@ def rank_program(g, core, T, topo):
                 a[h] = a2
             if more:
                 lab[0] = "g%d t%d lim" % (gen, t)
+                when(gen, t, h, "count")
                 junk, acc, A1, A2, lim = tile("bf", L), tile("f32", 1), tile("i32", 1), tile("i32", 1), tile("f32", 1)
                 act(junk, ap(junk), ap(cnt), AF.Identity, [cnt], L, scale=-1.0, bias=8.0, acc=acc, dur=vc(L) + 0.14)
+                when(gen, t, h, "limit")
                 tcopy(A1, ap(A1), ap(acc), [acc], 1)
                 ts(A2, ap(A2), ap(A1), 63, AL.bitwise_and, None, None, [A1], 1)
                 ts(lim, ap(lim), ap(A2), -1.0, AL.mult, ap(nth), AL.add, [A2, nth], 1)
         lab[0] = "g%d order" % gen
+        when(gen, t, h, "order")
         xo, hs = ps(BY[ny[0] % len(BY)], 0, L + 1), [u[k] for u in st for k in ("cum", "ohh")]
-        mms([xo], hs + [Idb, I512, Tri, neg1], [[(ap(xo, L), ap(Tri), ap(cum, L - 1)), (ap(xo, L), ap(I512), ap(neg1))],
-                                                [(ap(xo, 0, L), ap(Idb), ap(cum)), (ap(xo, 0, L), ap(I512), ap(oh))]], 2 * L + 128, boost=20)
+        mms([xo], hs + [Im, I512, Dm, D512, c320], [[(ap(xo, L), ap(Im), ap(cum, L - 1)), (ap(xo, L), ap(I512), ap(c320))],
+                                                    [(ap(xo, 0, L), ap(Dm), ap(cum)), (ap(xo, 0, L), ap(D512), ap(oh))]], 2 * L + 128)
         q1 = tile("bf", L)
-        ts(q1, ap(q1), ap(xo, 0, L), ap(xo, L), AL.add, 0.0, AL.max, [xo], L, boost=20)
+        ts(q1, ap(q1), ap(xo, 0, L), ap(xo, L), AL.add, 0.0, AL.max, [xo], L)
         op_ = ps(BY[(ny[0] + 1) % len(BY)], 0, C)
         ny[0] += 2
-        mms([op_], [q1, Zb], [[(ap(op_), Z(Zb, r), ap(q1, r, L, 16)) for r in range(16)]], 1024, boost=20)
+        mms([op_], [q1, Zb], [[(ap(op_), Z(Zb, r), ap(q1, r, L, 16)) for r in range(16)]], 1024)
         po, pm, srt, prev = tile("u16", C), tile("u16", C), tile("f32", L), tile("f32", 48)
-        ts(po, ap(po), ap(op_), -1.0, AL.mult, float(L), AL.add, [op_], C, boost=20)
-        ipo = send([(po, ap(po), pm, ap(pm), -2)], boost=20)
+        ts(po, ap(po), ap(op_), -1.0, AL.mult, float(L), AL.add, [op_], C)
+        send([(po, ap(po), pm, ap(pm), -2)])
 
         def scat(srt=srt, po=po, dau=dau):
             return [g.vector.tensor_copy(ap(srt).indirect(ap(po)), ap(dau))]
-        isc = task("V", gc_(L, "scatter"), [po, dau], [srt], scat, boost=20)
-        ibest = send([(srt, ap(srt, L - 48, L), come, ap(come), -2), (srt, ap(srt, L - 48, L), prev, ap(prev), -1)], boost=20)
-        soft(ibest, ipo)
-        soft(st[-1]["send"], ibest)
-        soft(st[-1]["put"], isc)
+        task("V", gc_(L, "scatter"), [po, dau], [srt], scat)
+        send([(srt, ap(srt, L - 48, L), come, ap(come), -2), (srt, ap(srt, L - 48, L), prev, ap(prev), -1)])
         lab[0] = "g%d home" % gen
+        when(gen, t, h, "home")
         y1 = col([pm], ap(pm), -1.0, AL.mult, 239.0, AL.add, n=C)
         y2 = col([pm], ap(pm), -256.0, AL.mult, 48.0 * 256, AL.add, n=C)
         y3, y4, Ln = tile("f32", C), tile("f32", C), tile("u16", C)
@@ -499,35 +543,29 @@ def tid(d):
     return d[0] if isinstance(d, tuple) else d
 
 
+def turn_of(t):
+    if t["turn"] is None:
+        return t["at"]
+    gen, step, h, what, j = t["turn"]
+    return gen * PLAN["generation"] + PLAN["start"][step][h] + PLAN[what][0] + j * PLAN[what][1]
+
+
 def order(tasks):
     n = len(tasks)
-    pred, succ = [[] for _ in range(n)], [[] for _ in range(n)]
-    for i, t in enumerate(tasks):
-        for d, lag in t["deps"].items():
-            lag += COST["sem"] if tasks[tid(d)]["q"] != t["q"] else COST["own"] * (d not in t["soft"])
-            pred[i].append((tid(d), lag))
-            succ[tid(d)].append((i, lag))
+    q = [t["q"] for t in tasks]
     dur = [0.05 if t["kind"] == "d" else t["dur"] for t in tasks]
-    tail = [t["dur"] - u for t, u in zip(tasks, dur)]
+    tail, none = [t["dur"] - u for t, u in zip(tasks, dur)], [0.0] * n
 
-    def place(before, after, key, first):
-        left, end, busy = [len(p) for p in before], [0.0] * n, {}
-        ready = sorted((key[i], i) for i in range(n) if not left[i])
-        while ready:
-            _, i = ready.pop(0)
-            st, line, at = max([end[j] + lag for j, lag in before[i]] + [first[i]]), busy.setdefault(tasks[i]["q"], []), 0
-            while at < len(line) and line[at][0] < st + dur[i] - 1e-9:
-                st, at = max(st, line[at][1]), at + 1
-            line.insert(at, (st, st + dur[i]))
-            end[i] = st + dur[i]
-            new = []
-            for j, _ in after[i]:
-                left[j] -= 1
-                if not left[j]:
-                    new.append((key[j], j))
-            if new:
-                ready = sorted(ready + new)
-        return end
+    def links(hop):
+        pred, succ = [[] for _ in range(n)], [[] for _ in range(n)]
+        for i, t in enumerate(tasks):
+            for d, lag in t["deps"].items():
+                lag += (COST["sem"] if q[tid(d)] != q[i] else 0.0) + (hop if isinstance(d, tuple) else 0.0)
+                pred[i].append((tid(d), lag))
+                succ[tid(d)].append((i, lag))
+        return pred, succ
+    pred, succ = links(0.0)
+    others = [links(hop)[0] for hop in COST["spread"]]
     line, need = [], [len(p) for p in pred]
     line += [i for i in range(n) if not need[i]]
     for i in line:
@@ -536,16 +574,56 @@ def order(tasks):
             if not need[j]:
                 line.append(j)
     assert len(line) == n
-    key = [t["turn"] for t in tasks]
-    best = None
+
+    def place(before, walk, key, first):
+        key = list(key)
+        for i in walk:
+            for j, _ in before[i]:
+                if key[j] >= key[i]:
+                    key[i] = key[j] + 1e-6
+        end, busy = [0.0] * n, {x: [] for x in q}
+        for i in sorted(walk, key=lambda j: key[j]):
+            st, slots = first[i], busy[q[i]]
+            for j, lag in before[i]:
+                if end[j] + lag > st:
+                    st = end[j] + lag
+            at = len(slots)
+            while at and slots[at - 1][1] > st:
+                at -= 1
+            while at < len(slots) and slots[at][0] < st + dur[i] - 1e-9:
+                st, at = max(st, slots[at][1]), at + 1
+            slots.insert(at, (st, st + dur[i]))
+            end[i] = st + dur[i]
+        return end
+
+    def length(issue, before):
+        end, free = [0.0] * n, {x: 0.0 for x in q}
+        for i in issue:
+            st = free[q[i]]
+            for j, lag in before[i]:
+                if end[j] + lag > st:
+                    st = end[j] + lag
+            end[i] = free[q[i]] = st + dur[i]
+        return max(e + u for e, u in zip(end, tail))
+
+    def closed(key):
+        end = place(pred, line, key, none)
+        back = place(succ, line[::-1], [-e - u for e, u in zip(end, tail)], tail)
+        end = min(end, place(pred, line, [-e for e in back], none), key=lambda x: max(e + u for e, u in zip(x, tail)))
+        start = [e - u for e, u in zip(end, dur)]
+        issue = sorted(line, key=lambda i: start[i])
+        return 2 * max(e + u for e, u in zip(end, tail)) + sum(length(issue, p) for p in others), start, issue
+    best = now = closed([turn_of(t) for t in tasks])
+    rng = np.random.default_rng(CFG["seed"])
     for _ in range(CFG["passes"]):
-        end = place(pred, succ, key, [0.0] * n)
-        span = max(e + u for e, u in zip(end, tail))
-        if best is None or span < best[0]:
-            best = (span, end)
-        key = [-e for e in place(succ, pred, [-e - u for e, u in zip(end, tail)], tail)]
-    rank = {i: j for j, i in enumerate(line)}
-    return sorted(range(n), key=lambda i: (best[1][i] - dur[i], rank[i]))
+        size, lo, wide = rng.random(3).tolist()
+        lo *= max(now[1])
+        new = closed([u + size * x if lo < u < lo + 5 + 20 * wide else u for u, x in zip(now[1], rng.normal(size=n).tolist())])
+        if new[0] <= now[0] + 0.3:
+            now = new
+        if new[0] < best[0]:
+            best = new
+    return best[2]
 
 
 def emit(g, T, tasks):

@@ -7,21 +7,26 @@ NR, L, ST, GENS = 8, 192, 3, 2
 GW, XW = 1536, 3072
 C = 12
 CFG = {"halves": [(0, 96, (32, 32, 32)), (96, 96, (32, 32, 32))],
-       "rec": (("SSS", "SVV"), ("SSS", "SSV"), ("SSS", "SSV")),
-       "kg": 4, "pre": 3, "pcut": 2, "xat": 2, "pq": "VV", "aq": "SS", "passes": 1500, "seed": 1}
-PLAN = {"mask": (-3.4, 0), "hosts": (-2.3, 0), "names": (-2.3, 1.0), "rows": (-1.0, 1.5), "list": (-0.2, 1.0), "records": (0.2, 0.5), "T": (1.1, 0),
+       "rec": (("SSV", "SVV"), ("SSS", "SSV"), ("SSS", "SSV")),
+       "ks": (4, 5, 5, 2), "own": 0.04, "pcut": 1, "wide": True,
+       "lags": (4.0, 4.5, 5.0, 5.5), "passes": 500, "rounds": 3, "again": 2, "more": 400, "moves": 9000, "seed": 4, "flip": 0.15, "swap": 0.6, "slack": 0.4, "heat": 0.2}
+PLAN = {"mask": (-3.4, 0.6), "hosts": (-2.3, 0), "names": (-2.3, 1.0), "rows": (-1.0, 1.5), "list": (-0.2, 1.0), "records": (0.2, 0.5), "T": (1.1, 0),
         "old": (2.0, 0), "val": (2.7, 0), "pre": (2.0, 0), "add": (3.0, 0.3), "abs": (3.4, 0.4), "sum": (3.9, 0.4), "sign": (5.4, 0), "err": (5.5, 0),
         "first": (5.8, 0), "pick": (5.8, 0), "place": (6.1, 0), "wrap": (6.8, 0), "lists": (7.0, 0), "new": (7.3, 0), "put": (7.5, 0), "name": (6.9, 0),
         "rows out": (7.9, 0), "count": (8.4, 0), "limit": (9.6, 0), "order": (5.9, 0), "home": (13.0, 0), "mother": (2.5, 0),
-        "start": ((6.0, 11.8), (19.8, 26.6), (34.6, 40.2)), "generation": 48}
-POOL = {"f32": ("float32", 7000), "bf": ("bfloat16", 48000), "hf": ("float16", 30000), "u16": ("uint16", 6000), "i32": ("int32", 3600)}
+        "start": (6, 19, 33), "generation": 48}
+POOL = {"f32": ("float32", 6000), "bf": ("bfloat16", 56000), "hf": ("float16", 33600), "u16": ("uint16", 6000), "i32": ("int32", 3600)}
 SIZE = {"f32": 4, "bf": 2, "hf": 2, "u16": 2, "i32": 4}
 SCRATCH = {"p_" + k: ("sbuf", [128, v[1]], v[0]) for k, v in POOL.items()}
 SCRATCH.update({"bank%d" % b: ("psum", [128, 512], "float32") for b in range(8)})
+SCRATCH.update({"turns": ("sbuf", [128, 16, 8, 16], "bfloat16"), "ring": ("sbuf", [128, 8, 32], "bfloat16"), "twice": ("sbuf", [128, 8, 32], "float32")})
 SEMAPHORES = ["sV", "sS", "sP", "sG", "left"] + ["d%d" % i for i in range(20)] + ["r%d" % i for i in range(60)]
 CY = 0.00083
-COST = {"f": 1.25, "gather": 1.56, "scatter": 3.5, "issue": 0.9, "hop": 2.2, "spread": (-0.8, 1.0), "sem": 0.08, "pe": 0.00042}
-NOTE, ORDER = [""], []
+COSTS = [{"f": 1.25, "fix": 0.01, "min": 64, "gather": 1.56, "scatter": 3.5, "pe": 0.00034, "issue": 0.9, "hop": 2.3, "row": 0.04, "sem": 0.08},
+         {"f": 1.1, "fix": 0.03, "min": 64, "gather": 1.3, "scatter": 2.5, "pe": 0.00038, "issue": 0.8, "hop": 2.2, "row": 0.01, "sem": 0.25},
+         {"f": 1.5, "fix": 0.01, "min": 64, "gather": 2.0, "scatter": 5.0, "pe": 0.00042, "issue": 1.2, "hop": 3.0, "row": 0.04, "sem": 0.12},
+         {"f": 1.3, "fix": 0.02, "min": 64, "gather": 1.7, "scatter": 4.0, "pe": 0.00036, "issue": 1.1, "hop": 3.0, "row": 0.1, "sem": 0.1}]
+NOTE, ORDER, QUEUE = [""], [], []
 
 
 def rank_program(g, core, T, topo):
@@ -30,7 +35,7 @@ def rank_program(g, core, T, topo):
         return
     tasks, used = [], {k: 0 for k in POOL}
     bank_use = [{"q": None, "now": [], "before": []} for _ in range(8)]
-    ndma, nrem, lab, turn = [0], [0], [""], [None]
+    ndma, nrem, lab, turn, wide = [0], [0], [""], [None], [False]
 
     def mk(b, lo, n, mut=False):
         return {"b": b, "lo": lo, "n": n, "wr": [], "rd": [], "mut": mut}
@@ -54,7 +59,7 @@ def rank_program(g, core, T, topo):
         buf = T[t["b"]]
         return buf[:, t["lo"] + a:t["lo"] + b] if st == 1 else buf[:, t["lo"] + a:t["lo"] + b:st]
 
-    def task(q, dur, ins, outs, fn, kind="c", extra=None, at=0.0):
+    def task(q, dur, ins, outs, fn, kind="c", extra=None, at=0.0, either=False):
         i, deps = len(tasks), {}
         for t in ins:
             for w, lag in t["wr"]:
@@ -68,14 +73,14 @@ def rank_program(g, core, T, topo):
         for t in list(ins) + list(outs):
             if "bank" in t:
                 bu = bank_use[t["bank"]]
-                if bu["q"] != q:
-                    bu.update(q=q, now=[], before=bu["now"])
+                if bu["q"] != q or either:
+                    bu.update(q=i if either else q, now=[], before=bu["now"])
                 for j in bu["before"]:
                     deps.setdefault(j, 0)
                 bu["now"].append(i)
         deps.pop(i, None)
-        tasks.append({"q": q, "dur": dur, "deps": deps, "fn": fn, "kind": kind, "x": extra, "soft": set(),
-                      "turn": turn[0], "at": at or 0.07 * (i - 16), "lab": lab[0]})
+        tasks.append({"q": q, "dur": (dur + np.zeros(len(COSTS))).tolist(), "deps": deps, "fn": fn, "kind": kind, "x": extra, "soft": set(),
+                      "turn": turn[0], "at": at or 0.07 * (i - 16), "lab": lab[0], "either": either})
         for t in outs:
             if t["mut"]:
                 t["wr"], t["rd"] = [], []
@@ -93,10 +98,10 @@ def rank_program(g, core, T, topo):
         turn[0] = (gen, t, h, what, j)
 
     def vc(n, f=1.0):
-        return max(64, n * f) * CY * COST["f"]
+        return np.array([(c["fix"] + max(c["min"], n * f) * CY) * c["f"] for c in COSTS])
 
     def gc_(n, k="gather"):
-        return (0.06 + n * COST[k] * CY) * COST["f"]
+        return np.array([(0.06 + n * c[k] * CY) * c["f"] for c in COSTS])
 
     def ts(out, oa, in0, s1, op0, s2, op1, ins, n, f=1.0, at=0.0, dur=None):
         def fn():
@@ -116,10 +121,16 @@ def rank_program(g, core, T, topo):
                     lambda: [g.scalar.activation(oa, in0, func, bias=bias, scale=scale, accum_out=ap(acc) if acc else None)])
 
     def copy(q, out, oa, in0, ins, n=0, dur=None):
-        return tcopy(out, oa, in0, ins, n, dur=dur) if q == "V" else act(out, oa, in0, AF.Copy, ins, n, dur=dur)
+        def fn():
+            return [g.vector.tensor_copy(oa, in0) if QUEUE[i] == "V" else g.scalar.activation(oa, in0, AF.Copy)]
+        i = task(q, vc(n) if dur is None else dur, ins, [out], fn, either=True)
+        return i
 
     def iota(out, pat, base, cm, flag=True):
         task("G", 0.16 + 2.5 * out["n"] * CY, [], [out], lambda: [g.iota(ap(out), pat, base, cm, allow_small_or_imprecise_dtypes=flag)])
+
+    def keep(out, src, op, fill, base):
+        task("G", 0.5, [src], [out], lambda: [g.affine_select(ap(out), ap(src), [[1, 128]], op, fill, base, -1)])
 
     def mms(outs, ins, groups, n, after=None, ends=(True, True)):
         def fn():
@@ -129,7 +140,7 @@ def rank_program(g, core, T, topo):
                     m = g.tensor.matmul(o, l, x, ends[0] and j == 0, ends[1] and j == len(gr) - 1)
                 r.append(m)
             return r
-        i = task("P", (0.02 + n * COST["pe"]) * COST["f"], ins, outs, fn)
+        i = task("P", np.array([(0.02 + n * c["pe"]) * c["f"] for c in COSTS]), ins, outs, fn)
         if after:
             for w, _ in after["wr"][:-1]:
                 soft(i, w)
@@ -145,20 +156,23 @@ def rank_program(g, core, T, topo):
         task("Y", 2.0, ins, [], lambda: [g.sync.dma_start(dst, oa)], "d", ndma[0])
         ndma[0] += 1
 
-    def engines(a, b):
-        return topo.engines(a, b)[:8]
+    far = [e for e in range(32) if all(e in topo.engines(u, v) for u in T.cores for v in T.cores if u != v)]
+
+    def engines(r, m, moves):
+        ways = [topo.engines(T.cores[r], T.cores[(r + u[4]) % NR]) if wide[0] else far for u in moves]
+        if len(set(len(w) for w in ways)) > 1:
+            return far if ways[m] == far else [e for e in ways[m] if e not in far]
+        return ways[m][m * len(ways[m]) // len(moves):(m + 1) * len(ways[m]) // len(moves)]
 
     def send(moves):
         got, out, n, trs = [], [], len(moves), []
         for m, (src, sa, dst, da, d) in enumerate(moves):
-            to, fr = T.cores[(rank + d) % NR], T.cores[(rank - d) % NR]
             name = "r%d" % nrem[0]
             nrem[0] += 1
-            rid, pid, _ = topo.addr(to)
-            es = engines(core, to)
-            es = es[m * len(es) // n:(m + 1) * len(es) // n]
+            rid, pid, _ = topo.addr(T.cores[(rank + d) % NR])
+            es = engines(rank, m, moves)
             trs.append((rid, pid, sum(1 << e for e in es), name, sa, da))
-            got.append((name, len(engines(fr, core)) // n))
+            got.append((name, len(engines((rank - d) % NR, m, moves))))
             out.append(len(es))
 
         def fn():
@@ -169,31 +183,25 @@ def rank_program(g, core, T, topo):
                 g.remote_dma_fused([RemoteDMATransfer(dst_ids=[DstId(rid=rid, pnc=pid)], dma_engine_mask=mask, remote_sem=T.sem[name], src=sa, dst=da)
                                     for rid, pid, mask, name, sa, da in trs], local_sem=T.sem.left)
             return []
-        i = task("G", COST["issue"] + (1.5 if nrem[0] == 1 else 0), [m[0] for m in moves], [], fn, "r", (got, sum(out)))
+        i = task("G", np.array([c["issue"] for c in COSTS]) + (3.5 if nrem[0] == 1 else 0), [m[0] for m in moves], [], fn, "r", (got, sum(out)))
+        dst = moves[0][2]
+        w = task("W", np.array([16 * n * c["row"] for c in COSTS]) + n * dst["n"] * SIZE[dst["b"][2:]] * 128 / 90000.0, [], [], None, "w")
+        tasks[w]["deps"][i, 0] = 0.0
         for m, (src, sa, dst, da, d) in enumerate(moves):
-            dst["wr"].append(((i, m), COST["hop"] + n * dst["n"] * SIZE[dst["b"][2:]] * 128 / 60000.0))
+            dst["wr"] += [((i, m), 0.0), ((w, 0), 0.0)]
         return i
 
-    HV, KG = CFG["halves"], CFG["kg"]
+    HV = CFG["halves"]
     gni, nbi, thi = tile("i32", GW), tile("i32", GW), tile("i32", 1)
     X, a0 = tile("bf", XW, True), tile("bf", L)
-    NG = 4
+    NG = 2
     gh = [part(gni, GW // NG * j, GW // NG) for j in range(NG)]
-    seq = [load(gh[j], ap(gh[j]), T.gn[:, GW // NG * j:GW // NG * (j + 1)], 2.4 + 0.45 * j) for j in range(NG)]
-    nh, at = [], 3.6
-    for i0, W, pieces in HV:
-        for pw in pieces if i0 == 0 else (W,):
-            if len(nh) == CFG["xat"]:
-                at += 2.0
-                seq.append(load(X, ap(X), T.x[:], at))
-            at += pw / 96.0
-            nh.append(part(nbi, 8 * i0, 8 * pw))
-            seq.append(load(nh[-1], ap(nh[-1]), T.nb[:, 8 * i0:8 * (i0 + pw)], at))
-            i0 += pw
+    seq = [load(gh[j], ap(gh[j]), T.gn[:, GW // NG * j:GW // NG * (j + 1)], 2.0 + 2.2 * (j + 1) / NG) for j in range(NG)]
+    nh = [part(nbi, 8 * i0, 8 * W) for i0, W, _ in HV]
+    seq += [load(nh[0], ap(nh[0]), T.nb[:, 0:nh[0]["n"]], 5.2), load(X, ap(X), T.x[:], 7.2), load(nh[1], ap(nh[1]), T.nb[:, nh[0]["n"]:GW], 8.2),
+            load(a0, ap(a0), T.a0[:], 8.5), load(thi, ap(thi), T.th[:], 8.7)]
     for u, v in zip(seq, seq[1:]):
         soft(v, u)
-    load(thi, ap(thi), T.th[:], 2.0, "S")
-    load(a0, ap(a0), T.a0[:], 2.2, "S")
 
     lab[0] = "const"
 
@@ -210,7 +218,7 @@ def rank_program(g, core, T, topo):
             scale=ap(scale) if isinstance(scale, dict) else scale, bias=ap(bias) if isinstance(bias, dict) else bias)
         return t
     PW = max(max(p) for _, _, p in HV)
-    ip, ckr, pni = tile("i32", 1), tile("i32", 16), tile("i32", 128)
+    ip, pni = tile("i32", 1), tile("i32", 128)
     im, kpat, mgf, ii0, il = tile("f32", 144), tile("bf", 16 * PW), tile("f32", 128), tile("f32", C), tile("bf", L)
     iota(ip, [[0, 1]], 0, 1, False)
     iota(im, [[1, 144]], 0, 0)
@@ -219,8 +227,7 @@ def rank_program(g, core, T, topo):
     iota(ii0, [[16, C]], 0, 0)
     iota(il, [[1, L]], 0, 0)
     iota(pni, [[0, 8], [1, 16]], 1, 1, False)
-    iota(ckr, [[-1, 16]], 16, 1, False)
-    for j in range(len(tasks) - 7, len(tasks)):
+    for j in range(len(tasks) - 6, len(tasks)):
         soft(j, j - 1)
     si = col([ip], ap(ip), 15, AL.bitwise_and, pool="i32")
     gi = col([ip], ap(ip), 4, AL.arith_shift_right, pool="i32")
@@ -233,29 +240,37 @@ def rank_program(g, core, T, topo):
     row.update({r: col([scol], ap(scol), float(r), AL.is_equal) for r in (3, 4)})
     rm3 = col([scol], ap(scol), 3.0, AL.is_ge)
     r01 = col([scol], ap(scol), 2.0, AL.is_lt)
-    Idw = col([im, pcol], ap(im), ap(pcol), AL.is_equal, n=144, pool="bf")
-    Idb = dict(Idw, n=128)
+    Idb = col([im, pcol], ap(im, 0, 128), ap(pcol), AL.is_equal, n=128, pool="bf")
     Blk = col([mgf, gcol], ap(mgf), ap(gcol), AL.is_equal, n=128, pool="bf")
-    lt = col([im, pcol], ap(im, 0, 128), ap(pcol), AL.is_gt, n=128, pool="bf")
     mask0 = col([kpat, scol], ap(kpat), ap(scol), AL.is_equal, n=16 * PW, pool="bf", f=0.5)
     Tri, M1, M2, PNm, Dm = tile("bf", 128), tile("bf", 128), tile("bf", 128), tile("bf", 128), tile("bf", 128)
-    Zn, Im, I16n, I512, I15 = acol(Zb, -1.0), acol(Idb, -1.0), acol(Idb, -16.0), acol(Idb, 512.0), acol(Idb, 15.0)
-    tt(Tri, ap(Tri), ap(lt), ap(Blk), AL.mult, [lt, Blk], 128, 2)
-    tt(M1, ap(M1), ap(Tri), ap(I16n), AL.add, [Tri, I16n], 128, 2)
-    tt(M2, ap(M2), ap(M1), ap(Zb, 15, 143), AL.add, [M1, Zb], 128, 2)
+    Zn, Im, I512, I15 = acol(Zb, -1.0), acol(Idb, -1.0), acol(Idb, 512.0), acol(Idb, 15.0)
+    keep(Tri, Blk, AL.is_gt, 0.0, 0)
+    keep(M1, Tri, AL.not_equal, -16.0, 0)
+    m2 = ps(7, 0, 128)
+    mms([m2], [Idb, M1, Zb], [[(ap(m2), ap(Idb), ap(M1)), (ap(m2), ap(Idb), ap(Zb, 15, 143))]], 256)
+    act(M2, ap(M2), ap(m2), AF.Copy, [m2], 128)
+    r15 = col([scol], ap(scol), 15.0, AL.is_lt)
+    PN0 = acol(Idb, acol(acol(scol, 1.0, 1.0, "f32"), r15, 0.0, "f32"))
     M3 = acol(M1, 1024.0)
     pn2 = col([pni], ap(pni), 15, AL.bitwise_and, n=128, pool="i32")
     tt(PNm, ap(PNm), ap(pn2), ap(Blk), AL.mult, [pn2, Blk], 128, 2)
     th1 = acol(scol, 1.0, 16.0, "f32")
-    th2 = acol(th1, 1.0, acol(row[0], -16.0, 0.0, "f32"), "f32")
+    E0 = acol(Idb, acol(row[0], 16.0, 0.0, "f32"))
     e3 = acol(scol, 32.0, -80.0, "f32")
-    tt(Dm, ap(Dm), ap(Idw, 0, 128), ap(Idw, 1, 129), AL.subtract, [Idw], 128, 2)
+    keep(Dm, Idb, AL.not_equal, -1.0, 1)
     D512, c320 = acol(Dm, 512.0), acol(scol, 0.0, -0.625)
     R3, R4n = acol(Blk, acol(row[3], 32.0, 0.0, "f32")), acol(Blk, acol(row[4], -1.0, 0.0, "f32"))
     K4, K01 = acol(Idb, row[4]), acol(Idb, r01)
     ones = acol(il, 0.0, 1.0)
-    oh0 = acol(ones, row[0], n=128)
     i8 = acol(il, 8.0)
+    twice, ring, turns = mk("twice", 0, 256), mk("ring", 0, 256), mk("turns", 0, 2048)
+    task("G", 0.7, [], [twice], lambda: [g.iota(T.twice[:], [[16, 8], [0, 2], [1, 16]], 0, 0, allow_small_or_imprecise_dtypes=True)])
+    ts(ring, T.ring[:], T.twice[:], ap(pcol), AL.is_equal, None, None, [twice, pcol], 256)
+    for k in range(16):
+        copy("S", turns, T.turns[:, k], T.ring[:, :, 16 - k:32 - k], [ring], 128)
+    ckr = tile("i32", 16)
+    iota(ckr, [[-1, 16]], 16, 1, False)
     cki = col([ckr], ap(ckr), 15, AL.bitwise_and, n=16, pool="i32")
     ck = col([cki], ap(cki), 0.0, AL.add, n=16, pool="bf")
     ii = col([ii0, scol], ap(ii0), ap(scol), AL.add, n=C)
@@ -267,32 +282,29 @@ def rank_program(g, core, T, topo):
             b3[W] = acol(scol, -1023.0, 2.0 * W - 16384.0, "f32")
         for t in range(2):
             d = dfl[i0, t] = tile("bf", 3 * cw)
-            acol(ii, 8.0 * (1 - t), a=c0, n=cw, out=d)
+            acol(ii, 1.0, -float(i0), a=c0, n=cw, out=d)
             acol(ii, 16.0, a=c0, n=cw, out=d, o=cw)
-            acol(ii, 1.0, -float(i0), a=c0, n=cw, out=d, o=2 * cw)
+            acol(ii, 8.0 * (1 - t), a=c0, n=cw, out=d, o=2 * cw)
     lab[0] = "conv"
     G = tile("f32", GW)
     for j in range(NG):
-        ts(G, ap(G, GW // NG * j, GW // NG * (j + 1)), ap(gh[j]), -1536.0, AL.add, None, None, [gh[j]], GW // NG, at=2.2 + 0.5 * j)
+        ts(G, ap(G, GW // NG * j, GW // NG * (j + 1)), ap(gh[j]), -1536.0, AL.add, None, None, [gh[j]], GW // NG, at=2.0 + 2.2 * (j + 1) / NG)
     G["mut"] = True
     El0, NB0 = [], []
     for h, (i0, W, pieces) in enumerate(HV):
-        El0.append([])
+        El0.append(tile("u16", W))
         when(0, 0, h, "hosts")
-        for j, pw in enumerate(pieces):
-            El0[h].append(tile("u16", pw))
-            o = 8 * (i0 + sum(pieces[:j]))
-            tcopy(El0[h][j], ap(El0[h][j]), ap(nbi, o, o + 8 * pw, 8), [nh[j] if h == 0 else nh[-1]], pw)
+        tcopy(El0[h], ap(El0[h]), ap(nh[h], 0, 8 * W, 8), [nh[h]], W)
         NB0.append(tile("hf", W))
         when(0, 0, h, "old")
-        tcopy(NB0[h], ap(NB0[h]), ap(nbi, 8 * i0, 8 * (i0 + W), 8), nh, W)
+        tcopy(NB0[h], ap(NB0[h]), ap(El0[h]), [El0[h]], W, 0.5)
 
     def Z(z, k):
         return ap(z, 15 - k, 143 - k)
 
     BW, BD, BY, BM = (0, 1), (2, 3), (4, 5, 6), 7
     ny = [0]
-    masks, yas = [tile("bf", 17 * W) for _, W, _ in HV], [tile("bf", 16 * W) for _, W, _ in HV]
+    yas = [tile("bf", 16 * W) for _, W, _ in HV]
     lim = nth
     a = [part(a0, i0, W) for i0, W, _ in HV]
     for p in a:
@@ -300,11 +312,11 @@ def rank_program(g, core, T, topo):
     for gen in range(GENS):
         lab[0] = "g%d mother" % gen
         when(gen, 0, 0, "mother")
-        mo, mother, win = tile("hf", L), tile("hf", L), tile("f32", L + 48)
-        own, come = part(win, 0, L), part(win, L, 48)
+        mo, mother, win = tile("hf", L), tile("hf", L), tile("f32", L + 96)
+        own, come, prev = part(win, 0, L), part(win, L, 48), part(win, L + 48, 48)
         ts(mo, ap(mo), ap(G, 0, GW, 8), ap(rm3), AL.mult, None, None, [G, rm3], L)
-        send([(mo, ap(mo), mother, ap(mother), 2)])
-        act(own, ap(own), ap(G, 0, GW, 8), AF.Copy, [G], L)
+        imo = send([(mo, ap(mo), mother, ap(mother), 2)])
+        copy("S", own, ap(own), ap(G, 0, GW, 8), [G], L)
         R, info = [None] * len(HV), [None] * len(HV)
         oh, cum, dau = tile("bf", L), tile("bf", L), tile("f32", L)
         for t in range(ST):
@@ -312,29 +324,43 @@ def rank_program(g, core, T, topo):
             for h, (i0, W, pieces) in enumerate(HV):
                 lab[0] = "g%d t%d h%d front" % (gen, t, h)
                 cw = W // 16
-                Gg, Wl, Tb = tile("hf", 17 * W), tile("u16", cw + W), tile("bf", 18 * W)
+                nx = 3 * W if last else 2 * W
+                Gx, Wl, Tb = tile("hf", nx + 17 * W), tile("u16", cw + W), tile("bf", 18 * W)
+                Gg = part(Gx, nx, 17 * W)
                 Wp, nM, Tt, recs = ps(BW[h], 0, cw + W), part(Gg, 0, W), part(Tb, 0, W), []
-                s = {"Tb": Tb, "Wp": Wp, "nM": nM, "T": Tt, "recs": recs}
+                s = {"Tb": Tb, "Wp": Wp, "nM": nM, "T": Tt, "recs": recs, "Gx": Gx}
                 if t == 0:
                     when(gen, t, h, "hosts")
                     ts(nM, ap(nM), ap(G, 8 * i0, 8 * (i0 + W), 8), ap(row[0]), AL.mult, None, None, [G, row[0]], W)
-                    s["oh"], s["nb"] = oh0, NB0[h]
+                    s["oh"], s["nb"] = ones, NB0[h]
                 else:
-                    Rp, Rm = R[h]
-                    when(gen, t, h, "mask")
-                    mask = part(masks[h], 0, 17 * W)
-                    s["oh"] = part(mask, 0, W)
-                    ts(s["oh"], ap(mask, 0, W), ap(Rp), ap(ck, 0, 1), AL.is_equal, None, None, [Rp, ck], W, 0.5)
-                    for k in range(16):
-                        ts(mask, ap(mask, W + k, 17 * W, 16), ap(Rp), ap(ck, k, k + 1), AL.is_equal, None, None, [Rp, ck], W, 0.5)
+                    mask, Rm = R[h]
+                    s["oh"], rows, s0 = mask, [], 0
+                    if h:
+                        when(gen, t, h, "mask")
+                        Rp, mask = mask, tile("bf", 17 * W)
+                        mask["n"] = W
+                        s["oh"], rows = mask, [mk(mask["b"], mask["lo"] + W, 16 * W)] * len(pieces)
+                        ts(mask, ap(mask), ap(Rp), ap(ck, 0, 1), AL.is_equal, None, None, [Rp, ck], W, 0.5)
+                        for k in range(16):
+                            ts(rows[0], ap(rows[0], k, 16 * W, 16), ap(Rp), ap(ck, k, k + 1), AL.is_equal, None, None, [Rp, ck], W, 0.5)
+                    for j, pw in enumerate(() if h else pieces):
+                        when(gen, t, h, "mask", j)
+                        mp = ps(BD[h] if j else BW[h], 0, 16 * pw)
+                        for c in range(2):
+                            mms([mp], [mask, turns], [[(ap(mp, k, 16 * pw, 16), T.turns[:, k], ap(mask, s0, s0 + pw)) for k in range(8 * c, 8 * c + 8)]],
+                                8 * 64, after=mp, ends=(c == 0, c == 1))
+                        rows.append(mk(mask["b"], mask["lo"] + W + 16 * s0, 16 * pw))
+                        copy("S", rows[j], ap(rows[j]), ap(mp), [mp], 16 * pw)
+                        s0 += pw
                     when(gen, t, h, "hosts")
                     El = mk(Rm["b"], Rm["lo"] + cw, W)
                     tcopy(El, ap(El), ap(nbi).indirect(ap(Rm)), nh + [Rm], dur=gc_(W))
                     if not last:
                         when(gen, t, h, "old")
-                        s["nb"], s["hw"] = tile("hf", W), tile("hf", cw)
-                        tcopy(s["nb"], ap(s["nb"]), ap(El), [El], W, 0.5)
-                        tcopy(s["hw"], ap(s["hw"]), ap(Rm), [Rm], cw)
+                        s["hw"] = tile("hf", cw + W)
+                        s["nb"] = dict(s["hw"], lo=s["hw"]["lo"] + cw, n=W)
+                        tcopy(s["hw"], ap(s["hw"]), ap(Rm, 0, cw + W), [El, Rm], cw + W, 0.5)
                 s0 = 0
                 for j, pw in enumerate(pieces):
                     e0, e1 = (0 if j == 0 else W + 16 * s0), W + 16 * (s0 + pw)
@@ -342,9 +368,9 @@ def rank_program(g, core, T, topo):
                     Gp = part(Gg, e0, e1 - e0)
                     when(gen, t, h, "names", j)
                     if t == 0:
-                        tt(Gp, ap(Gg, W + 16 * s0, e1), ap(G).indirect(ap(El0[h][j])), ap(mask0, 0, 16 * pw), AL.mult, [G, El0[h][j], mask0], dur=gc_(16 * pw))
+                        tt(Gp, ap(Gg, W + 16 * s0, e1), ap(G).indirect(ap(El0[h], s0, s0 + pw)), ap(mask0, 0, 16 * pw), AL.mult, [G, El0[h], mask0], dur=gc_(16 * pw))
                     else:
-                        tt(Gp, ap(Gp), ap(G).indirect(ap(Rm, l0, l1)), ap(mask, e0, e1), AL.mult, [G, El, mask, s["oh"]], dur=gc_(e1 - e0))
+                        tt(Gp, ap(Gp), ap(G).indirect(ap(Rm, l0, l1)), ap(mask, e0, e1), AL.mult, [G, El, mask, rows[j]], dur=gc_(e1 - e0))
                         if j == 0:
                             nM["wr"] = Gp["wr"]
                     Wq, pc = ps(BW[h], l0, l1 - l0), CFG["pcut"]
@@ -372,39 +398,45 @@ def rank_program(g, core, T, topo):
                 cw = W // 16
                 Tb, Tt, recs, Wp, nM = s["Tb"], s["T"], s["recs"], s["Wp"], s["nM"]
                 when(gen, t, h, "val")
-                val, x3 = ps(BW[h], 144, 2 * W), ps(BW[h], 144 + 2 * W, W)
-                grp, ins = [[(ap(val, W, 2 * W), ap(PNm), ap(s["oh"], 0, W))]], [PNm, s["oh"]]
+                val, x3 = ps(BW[h], 224, 2 * W), ps(BW[h], 224 + 2 * W, W)
+                pn = PNm if t else PN0
+                grp, ins = [[(ap(val, 0, W), ap(pn), ap(s["oh"], 0, W))]], [pn, s["oh"]]
                 if not last:
                     old = (ap(Im), ap(i8, i0, i0 + W)) if t == 0 else (ap(R4n), ap(info[h]))
-                    grp.append([(ap(val, 0, W), ap(Idb), ap(s["nb"])), (ap(val, 0, W),) + old])
+                    grp.append([(ap(val, W, 2 * W), ap(Idb), ap(s["nb"])), (ap(val, W, 2 * W),) + old])
                     ins += [Idb, s["nb"], Im, i8] + ([R4n, info[h]] if t else [])
-                mms([val], ins, grp, 3 * W)
-                D, Ys = ps(BD[h], 0, W), []
-                for q in range(16 // KG):
-                    Ys.append(ps(BY[ny[0] % len(BY)], 0, KG * W))
+                else:
+                    fo = ps(BW[h], cw + W, W)
+                    grp.append([(ap(fo), Z(Zb, 0), ap(nM))])
+                    ins += [Zb, nM]
+                mms([val] + ([fo] if last else []), ins, grp, 3 * W)
+                D, Ys, KS = ps(BD[h], 0, W), [], CFG["ks"]
+                for q, kg in enumerate(KS):
+                    Ys.append(ps(BY[ny[0] % len(BY)], 0, kg * W))
                     ny[0] += 1
-                    if q < CFG["pre"]:
+                    if q < len(BY):
                         when(gen, t, h, "pre", q)
-                        mms([Ys[q]], [Idb, Tt], [[(ap(Ys[q], k * W, k * W + W), ap(Idb), ap(Tt)) for k in range(KG)]], KG * W, ends=(True, False))
-                for q, Y in enumerate(Ys):
-                    ya = part(yas[h], q * KG * W, KG * W)
+                        mms([Ys[q]], [Idb, Tt], [[(ap(Ys[q], k * W, k * W + W), ap(Idb), ap(Tt)) for k in range(kg)]], kg * W, ends=(True, False))
+                for q, (Y, kg) in enumerate(zip(Ys, KS)):
+                    k0 = sum(KS[:q])
+                    ya = part(yas[h], k0 * W, kg * W)
                     when(gen, t, h, "add", q)
-                    vs = [(ap(Y, k * W, k * W + W), ap(Idb), ap(Tb, 2 * W + q * KG + k, 18 * W, 16)) for k in range(KG)]
-                    if q < CFG["pre"]:
-                        mms([Y], recs + [Idb], [vs], KG * W, after=Y, ends=(False, True))
+                    vs = [(ap(Y, k * W, k * W + W), ap(Idb), ap(Tb, 2 * W + k0 + k, 18 * W, 16)) for k in range(kg)]
+                    if q < len(BY):
+                        mms([Y], recs + [Idb], [vs], kg * W, after=Y, ends=(False, True))
                     else:
-                        mms([Y], recs + [Idb, Tt], [[v, (v[0], ap(Idb), ap(Tt))] for v in vs], 2 * KG * W)
+                        mms([Y], recs + [Idb, Tt], [[v, (v[0], ap(Idb), ap(Tt))] for v in vs], 2 * kg * W)
                     when(gen, t, h, "abs", q)
-                    act(ya, ap(ya), ap(Y), AF.Abs, [Y], KG * W, bias=-255.0)
+                    act(ya, ap(ya), ap(Y), AF.Abs, [Y], kg * W, bias=-255.0)
                     when(gen, t, h, "sum", q)
-                    mms([D], [ya, Zb], [[(ap(D), Z(Zb, q * KG + k), ap(ya, k * W, k * W + W)) for k in range(KG)]], KG * W, after=D, ends=(q == 0, q == 16 // KG - 1))
+                    mms([D], [ya, Zb], [[(ap(D), Z(Zb, k0 + k), ap(ya, k * W, k * W + W)) for k in range(kg)]], kg * W, after=D, ends=(q == 0, q == len(KS) - 1))
                 lab[0] = "g%d t%d h%d tail" % (gen, t, h)
                 sg = tile("bf", W)
                 when(gen, t, h, "sign")
                 act(sg, ap(sg), ap(D), AF.Sign, [D, lim], W, bias=ap(lim))
                 if last:
                     when(gen, t, h, "err")
-                    Ep = ps(BW[h], 144, W)
+                    Ep = ps(BW[h], 224 + W, W)
                     mms([Ep], [info[h], sg, R3, Blk], [[(ap(Ep), ap(R3), ap(info[h])), (ap(Ep), ap(Blk), ap(sg))]], 2 * W)
                     ohh, cm = part(oh, i0, W), part(cum, i0, W)
                     ts(ohh, ap(ohh), ap(Ep), ap(e3), AL.is_ge, None, None, [Ep, e3], W)
@@ -415,42 +447,47 @@ def rank_program(g, core, T, topo):
                     task("V", vc(W, 0.5), [ohh, ones] + ([before] if before else []), [cm], scan)
                     s["cum"], s["ohh"] = cm, ohh
                 when(gen, t, h, "first")
-                x = ps(BD[h], W, 2 * W)
-                mms([x], [sg, M1, M2], [[(ap(x, W, 2 * W), ap(M2), ap(sg))], [(ap(x, 0, W), ap(M1), ap(sg))]], 2 * W)
+                nx = 3 * W if last else 2 * W
+                x = ps(BD[h], W, nx)
+                mms([x], [sg, M1, M2, E0, ones], [[(ap(x, 0, W), ap(E0), ap(ones, 0, W)), (ap(x, 0, W), ap(M2), ap(sg))], [(ap(x, W, 2 * W), ap(M1), ap(sg))]]
+                    + ([[(ap(x, 2 * W, nx), Z(Zb, 0), ap(sg))]] if last else []), W + nx)
                 mms([x3], [sg, M3, I15, il], [[(ap(x3), ap(M3), ap(sg)), (ap(x3), ap(I15), ap(il, 0, W))]], 2 * W)
-                FI, F2, Q = tile("bf", W), tile("bf", W), tile("hf", 3 * W)
-                Qh, Qp, Ql = part(Q, 0, W), part(Q, W, W), part(Q, 2 * W, W)
-                ts(F2, ap(F2), ap(x, W, 2 * W), ap(th2), AL.is_ge, None, None, [x, th2], W)
-                tt(Qp, ap(Qp), ap(val, W, 2 * W), ap(F2), AL.mult, [val, F2], W)
+                FF, Q = part(s["Gx"], 0, nx), tile("hf", 3 * W)
+                Ql, Qv = part(Q, 0, W), part(Q, W, 2 * W)
+                FI, nq = dict(FF, lo=FF["lo"] + W, n=W), W if last else 2 * W
+                ts(FF, ap(FF), ap(x), ap(th1), AL.is_ge, None, None, [x, th1], nx)
+                tt(Qv, ap(Qv, 0, nq), ap(val, 0, nq), ap(FF, 0, nq), AL.mult, [val, FF], nq)
                 if not last:
                     pp, pb = ps(BM, 0, W), tile("bf", W)
-                    mms([pp], [Blk, Qp], [[(ap(pp), ap(Blk), ap(Qp))]], W)
+                    mms([pp], [Blk, Qv], [[(ap(pp), ap(Blk), ap(Qv, 0, W))]], W)
                 when(gen, t, h, "pick")
-                ts(FI, ap(FI), ap(x, 0, W), ap(th1), AL.is_ge, None, None, [x, th1], W)
-                if not last:
-                    tt(Qh, ap(Qh), ap(val, 0, W), ap(FI), AL.mult, [val, FI], W)
                 ts(Ql, ap(Ql), ap(x3), ap(b3[W]), AL.add, 0.0, AL.max, [x3, b3[W]], W)
                 if not last:
                     when(gen, t, h, "place")
-                    copy(CFG["pq"][h], pb, ap(pb), ap(pp), [pp], W)
-                    Rp, Rm = tile("bf", W), tile("u16", cw + W)
-                    Rm["n"] = cw
+                    if h:
+                        copy("V", pb, ap(pb), ap(pp), [pp], W)
+                    else:
+                        ts(pb, ap(pb), ap(pp), ap(scol), AL.is_equal, None, None, [pp, scol], W)
+                    Rp, Rm = tile("bf", W if h else 17 * W), tile("u16", cw + W)
+                    Rp["n"], Rm["n"] = W, cw
                     R[h] = (Rp, Rm)
                     im0 = send([(pb, ap(pb), Rp, ap(Rp), 1)])
+                    if gen == 0:
+                        soft(im0, imo)
                 when(gen, t, h, "wrap")
-                n, c0 = 3 * cw, cw if last else 0
+                n = (W + nq) // 16
                 Op, O, d = ps(BD[h], 0, n), tile("u16", n), dfl[i0, min(t, 1)]
-                gr = [(ap(Op), ap(Idb), ap(d))] + ([(ap(Op, 0, cw), ap(Idb), ap(s["hw"]))] if t == 1 else [])
-                gr += [(ap(Op, c0, n), Z(Zb, r), ap(Q, 16 * c0 + r, 3 * W, 16)) for r in range(16)]
-                mms([Op], [Qh, Qp, Ql, Zb, Idb, d] + ([s["hw"]] if t == 1 else []), [gr], 18 * 64)
+                gr = [(ap(Op), ap(Idb), ap(d, 0, n))] + ([(ap(Op, 2 * cw, n), ap(Idb), ap(s["hw"], 0, cw))] if t == 1 else [])
+                gr += [(ap(Op), Z(Zb, r), ap(Q, r, W + nq, 16)) for r in range(16)]
+                mms([Op], [Qv, Ql, Zb, Idb, d] + ([s["hw"]] if t == 1 else []), [gr], 18 * 64)
                 when(gen, t, h, "lists")
-                tcopy(O, ap(O, c0, n), ap(Op, c0, n), [Op], n - c0)
+                tcopy(O, ap(O), ap(Op), [Op], n)
                 if not last:
-                    im1 = send([(O, ap(O, 0, cw), Rm, ap(Rm), 1)])
+                    im1 = send([(O, ap(O, 2 * cw, n), Rm, ap(Rm), 1)])
                     soft(im1, im0)
                 an, a2 = tile("bf", W), tile("bf", W)
                 when(gen, t, h, "new")
-                copy(CFG["aq"][h], an, ap(an), ap(Tb).indirect(ap(O, 2 * cw, n)), recs + [Tt, O], dur=gc_(W))
+                copy("S", an, ap(an), ap(Tb).indirect(ap(O, 0, cw)), recs + [Tt, O], dur=gc_(W))
                 when(gen, t, h, "put")
 
                 def put(O=O, an=an, u=cw, v=2 * cw):
@@ -458,31 +495,35 @@ def rank_program(g, core, T, topo):
                 task("V", gc_(W, "scatter"), [O, an], [X], put)
                 lab[0] = "g%d t%d h%d info" % (gen, t, h)
                 when(gen, t, h, "name")
-                fo, ch = ps(BM, 0, W), ps(BM, 128 + i0, W)
+                ch = ps(BM, 128 + i0, W)
                 more = not (gen == GENS - 1 and last)
-                mms([fo, ch, cnt], [FI, Blk, ones], [[(ap(fo), ap(Blk), ap(FI))]] + ([[(ap(ch), ap(ones, 0, 128), ap(FI))]] if more else []), 2 * W)
-                Qe, Qn = tile("hf", W), tile("hf", W)
-                tt(Qe, ap(Qe), ap(Wp, cw, cw + W), ap(FI), AL.mult, [Wp, FI], W)
-                tt(Qn, ap(Qn), ap(fo), ap(nM), AL.mult, [fo, nM], W)
-                ip_ = ps(BM, 320 + i0, W)
-                gr = [(Z(Zb, t), ap(Qe)), (Z(Zb, t), ap(nM)), (Z(Zn, t), ap(Qn))]
-                ins = [Qe, Qn, nM, Zb, Zn]
+                if not last:
+                    fo = ps(BW[h], cw + W, W)
+                    mms([fo], [FF, Blk], [[(ap(fo), ap(Blk), ap(FI))]], W)
+                if more:
+                    mms([ch, cnt], [FF, ones], [[(ap(ch), ap(ones, 0, 128), ap(FI))]], W)
+                Qe = tile("hf", 2 * W)
+                tt(Qe, ap(Qe), ap(Wp, cw, cw + 2 * W), ap(s["Gx"], W, 3 * W), AL.mult, [Wp, fo, FF, nM], 2 * W)
+                ip_ = ps(BW[h], 224, W)
+                gr = [(Z(Zb, t), ap(Qe, 0, W))] + ([(Z(Zb, t), ap(Qe, W, 2 * W))] if last else [(Z(Zb, t), ap(nM)), (Z(Zn, t), ap(Qe, W, 2 * W))])
+                ins = [Qe, nM, Zb, Zn]
                 if t == 0:
-                    gr += [(Z(Zn, 3), ap(FI)), (Z(Zb, 4), ap(Qh)), (ap(K4), ap(i8, i0, i0 + W))]
-                    ins += [FI, Qh, K4, i8]
+                    gr += [(Z(Zn, 3), ap(FI)), (Z(Zb, 4), ap(Qv, W, 2 * W)), (ap(K4), ap(i8, i0, i0 + W))]
+                    ins += [FF, Qv, K4, i8]
                 elif not last:
                     gr += [(Z(Zn, 3), ap(FI)), (ap(Idb), ap(info[h]))]
-                    ins += [FI, Idb, info[h]]
+                    ins += [FF, Idb, info[h]]
                 else:
                     gr += [(ap(K01), ap(info[h])), (ap(Idb), ap(mother, i0, i0 + W))]
                     ins += [K01, Idb, info[h], mother]
                 when(gen, t, h, "rows out")
                 mms([ip_], ins, [[(ap(ip_),) + u for u in gr]], len(gr) * W)
                 if last:
-                    act(dau, ap(dau, i0, i0 + W), ap(ip_), AF.Copy, [ip_], W)
+                    copy("S", dau, ap(dau, i0, i0 + W), ap(ip_), [ip_], W)
                     send([(an, ap(an), a2, ap(a2), -2)])
                 else:
                     io, info[h] = tile("hf", W), tile("hf", W)
+                    wide[0] = CFG["wide"]
                     tcopy(io, ap(io), ap(ip_), [ip_], W)
                     soft(send([(an, ap(an), a2, ap(a2), 1), (io, ap(io), info[h], ap(info[h]), 1)]), im1)
                 a[h] = a2
@@ -497,15 +538,16 @@ def rank_program(g, core, T, topo):
                 ts(lim, ap(lim), ap(A2), -1.0, AL.mult, ap(nth), AL.add, [A2, nth], 1)
         lab[0] = "g%d order" % gen
         when(gen, t, h, "order")
-        xo, hs = ps(BY[ny[0] % len(BY)], 0, L + 1), [u[k] for u in st for k in ("cum", "ohh")]
-        mms([xo], hs + [Im, I512, Dm, D512, c320], [[(ap(xo, L), ap(Im), ap(cum, L - 1)), (ap(xo, L), ap(I512), ap(c320))],
-                                                    [(ap(xo, 0, L), ap(Dm), ap(cum)), (ap(xo, 0, L), ap(D512), ap(oh))]], 2 * L + 128)
+        xo = ps(BY[ny[0] % len(BY)], 0, L + 1)
+        for u, (i0, W, _) in zip(st, HV):
+            mms([xo], [u["cum"], u["ohh"], Dm, D512], [[(ap(xo, i0, i0 + W), ap(Dm), ap(u["cum"])), (ap(xo, i0, i0 + W), ap(D512), ap(u["ohh"]))]], 2 * W)
+        mms([xo], [u["cum"], Im, I512, c320], [[(ap(xo, L), ap(I512), ap(c320)), (ap(xo, L), ap(Im), ap(cum, L - 1))]], 128)
         q1 = tile("bf", L)
         ts(q1, ap(q1), ap(xo, 0, L), ap(xo, L), AL.add, 0.0, AL.max, [xo], L)
         op_ = ps(BY[(ny[0] + 1) % len(BY)], 0, C)
         ny[0] += 2
         mms([op_], [q1, Zb], [[(ap(op_), Z(Zb, r), ap(q1, r, L, 16)) for r in range(16)]], 1024)
-        po, pm, srt, prev = tile("u16", C), tile("u16", C), tile("f32", L), tile("f32", 48)
+        po, pm, srt = tile("u16", C), tile("u16", C), tile("f32", L)
         ts(po, ap(po), ap(op_), -1.0, AL.mult, float(L), AL.add, [op_], C)
         send([(po, ap(po), pm, ap(pm), -2)])
 
@@ -515,19 +557,20 @@ def rank_program(g, core, T, topo):
         send([(srt, ap(srt, L - 48, L), come, ap(come), -2), (srt, ap(srt, L - 48, L), prev, ap(prev), -1)])
         lab[0] = "g%d home" % gen
         when(gen, t, h, "home")
-        y1 = col([pm], ap(pm), -1.0, AL.mult, 239.0, AL.add, n=C)
-        y2 = col([pm], ap(pm), -256.0, AL.mult, 48.0 * 256, AL.add, n=C)
+        pi = col([pm], ap(pm), 0.0, AL.add, n=C, pool="i32")
+        odd = col([pi], ap(pi), 1, AL.bitwise_and, n=C, pool="i32")
+        y0, y1 = col([odd], ap(odd), 48.0, AL.mult, 239.0, AL.add, n=C), tile("f32", C)
+        tt(y1, ap(y1), ap(y0), ap(pi), AL.subtract, [y0, pi], C)
+        y2 = col([pm], ap(pm), -512.0, AL.mult, 48.0 * 512, AL.add, n=C)
         y3, y4, Ln = tile("f32", C), tile("f32", C), tile("u16", C)
         tt(y3, ap(y3), ap(y1), ap(y2), AL.min, [y1, y2], C)
         tt(y4, ap(y4), ap(y3), ap(ii), AL.max, [y3, ii], C)
         tcopy(Ln, ap(Ln), ap(y4), [y4], C)
-        merged = part(win, L, 48)
-        tcopy(merged, ap(come, 0, 48, 2), ap(prev, 0, 48, 2), [come, prev], 24)
         if gen < GENS - 1:
-            tcopy(G, ap(G, 0, GW, 8), ap(win).indirect(ap(Ln)), [own, merged, Ln], dur=gc_(L))
+            tcopy(G, ap(G, 0, GW, 8), ap(win).indirect(ap(Ln)), [own, come, prev, Ln], dur=gc_(L))
     lab[0] = "out"
     yo, ao, so = tile("f32", L), tile("f32", L), tile("f32", L)
-    ts(yo, ap(yo), ap(win).indirect(ap(Ln)), 1536.0, AL.add, None, None, [own, merged, Ln], L, dur=gc_(L))
+    ts(yo, ap(yo), ap(win).indirect(ap(Ln)), 1536.0, AL.add, None, None, [own, come, prev, Ln], L, dur=gc_(L))
     store(T.yg[:], ap(yo), [yo])
     for h, (i0, W, _) in enumerate(HV):
         act(ao, ap(ao, i0, i0 + W), ap(a[h]), AF.Copy, [a[h]], W)
@@ -543,29 +586,31 @@ def tid(d):
     return d[0] if isinstance(d, tuple) else d
 
 
-def turn_of(t):
+def turn_of(t, lag):
     if t["turn"] is None:
         return t["at"]
     gen, step, h, what, j = t["turn"]
-    return gen * PLAN["generation"] + PLAN["start"][step][h] + PLAN[what][0] + j * PLAN[what][1]
+    return gen * PLAN["generation"] + PLAN["start"][step] + h * lag + PLAN[what][0] + j * PLAN[what][1]
 
 
 def order(tasks):
     n = len(tasks)
-    q = [t["q"] for t in tasks]
-    dur = [0.05 if t["kind"] == "d" else t["dur"] for t in tasks]
-    tail, none = [t["dur"] - u for t, u in zip(tasks, dur)], [0.0] * n
+    durs = [[0.05 if t["kind"] == "d" else t["dur"][c] for t in tasks] for c in range(len(COSTS))]
+    dur = durs[0]
+    tail, none = [t["dur"][0] - u for t, u in zip(tasks, dur)], [0.0] * n
+    own = [CFG["own"] if t["q"] in "VS" else 0.0 for t in tasks]
+    either = [i for i, t in enumerate(tasks) if t["either"]]
 
-    def links(hop):
+    def links(c):
         pred, succ = [[] for _ in range(n)], [[] for _ in range(n)]
         for i, t in enumerate(tasks):
             for d, lag in t["deps"].items():
-                lag += (COST["sem"] if q[tid(d)] != q[i] else 0.0) + (hop if isinstance(d, tuple) else 0.0)
+                lag += c["hop"] / 2 if isinstance(d, tuple) else 0.0
                 pred[i].append((tid(d), lag))
                 succ[tid(d)].append((i, lag))
         return pred, succ
-    pred, succ = links(0.0)
-    others = [links(hop)[0] for hop in COST["spread"]]
+    pred, succ = links(COSTS[0])
+    others = [(links(c)[0], u, c["sem"]) for c, u in zip(COSTS, durs)][1:]
     line, need = [], [len(p) for p in pred]
     line += [i for i in range(n) if not need[i]]
     for i in line:
@@ -575,18 +620,20 @@ def order(tasks):
                 line.append(j)
     assert len(line) == n
 
-    def place(before, walk, key, first):
-        key = list(key)
+    def place(q, before, walk, key, first):
+        key, sem = list(key), COSTS[0]["sem"]
         for i in walk:
             for j, _ in before[i]:
                 if key[j] >= key[i]:
                     key[i] = key[j] + 1e-6
-        end, busy = [0.0] * n, {x: [] for x in q}
+        end, busy = [0.0] * n, {x: [] for x in "VSPGYW"}
         for i in sorted(walk, key=lambda j: key[j]):
-            st, slots = first[i], busy[q[i]]
+            st, mine = first[i], q[i]
             for j, lag in before[i]:
-                if end[j] + lag > st:
-                    st = end[j] + lag
+                u = end[j] + lag + (own[i] if q[j] == mine else sem)
+                if u > st:
+                    st = u
+            slots = busy[mine]
             at = len(slots)
             while at and slots[at - 1][1] > st:
                 at -= 1
@@ -596,34 +643,146 @@ def order(tasks):
             end[i] = st + dur[i]
         return end
 
-    def length(issue, before):
-        end, free = [0.0] * n, {x: 0.0 for x in q}
+    def length(q, issue, before, dur, sem, upto=None):
+        end, free = [0.0] * n, {x: 0.0 for x in "VSPGYW"}
         for i in issue:
-            st = free[q[i]]
+            mine = q[i]
+            st = free[mine]
             for j, lag in before[i]:
-                if end[j] + lag > st:
-                    st = end[j] + lag
-            end[i] = free[q[i]] = st + dur[i]
-        return max(e + u for e, u in zip(end, tail))
+                u = end[j] + lag + (own[i] if q[j] == mine else sem)
+                if u > st:
+                    st = u
+            end[i] = free[mine] = st + dur[i]
+        return max(e + u for e, u in zip(end, tail)) if upto is None else end[upto]
 
-    def closed(key):
-        end = place(pred, line, key, none)
-        back = place(succ, line[::-1], [-e - u for e, u in zip(end, tail)], tail)
-        end = min(end, place(pred, line, [-e for e in back], none), key=lambda x: max(e + u for e, u in zip(x, tail)))
+    def closed(q, key, limit):
+        end = place(q, pred, line, key, none)
+        back = place(q, succ, line[::-1], [-e - u for e, u in zip(end, tail)], tail)
+        end = min(end, place(q, pred, line, [-e for e in back], none), key=lambda x: max(e + u for e, u in zip(x, tail)))
+        span = max(e + u for e, u in zip(end, tail))
+        if span > limit:
+            return None
         start = [e - u for e, u in zip(end, dur)]
         issue = sorted(line, key=lambda i: start[i])
-        return 2 * max(e + u for e, u in zip(end, tail)) + sum(length(issue, p) for p in others), start, issue
-    best = now = closed([turn_of(t) for t in tasks])
+        return span + sum(length(q, issue, *o) for o in others), span, start, issue, q
+
+    def held(q, issue, before, dur, sem):
+        end, last, cause = [0.0] * n, {}, [None] * n
+        for i in issue:
+            mine = q[i]
+            st, cause[i] = (end[last[mine]], (last[mine], True)) if mine in last else (0.0, None)
+            for j, lag in before[i]:
+                u = end[j] + lag + (own[i] if q[j] == mine else sem)
+                if u >= st:
+                    st, cause[i] = u, (j, False)
+            end[i], last[mine] = st + dur[i], i
+        i, out = max(range(n), key=lambda j: end[j] + tail[j]), []
+        while cause[i]:
+            if cause[i][1]:
+                out.append((i, cause[i][0]))
+            i = cause[i][0]
+        return out
+    every, waits, other = [(pred, dur, COSTS[0]["sem"])] + others, [], {"V": "S", "S": "V"}
     rng = np.random.default_rng(CFG["seed"])
-    for _ in range(CFG["passes"]):
-        size, lo, wide = rng.random(3).tolist()
-        lo *= max(now[1])
-        new = closed([u + size * x if lo < u < lo + 5 + 20 * wide else u for u, x in zip(now[1], rng.normal(size=n).tolist())])
-        if new[0] <= now[0] + 0.3:
+
+    def shifted(now, passes):
+        best = now
+        del waits[:]
+        for m in range(passes):
+            size, lo, wide, move = rng.random(4).tolist()
+            lo, q, key = lo * now[1], list(now[4]), list(now[2])
+            if move < CFG["swap"]:
+                if not waits:
+                    waits.extend(held(q, now[3], *every[m % len(every)]))
+                i, j = waits.pop(int(rng.integers(len(waits))))
+                if tasks[j]["either"] and size < 0.3:
+                    q[j] = other[q[j]]
+                elif size < 0.65:
+                    key[i] = key[j] - 0.01 - wide * wide
+                else:
+                    key[j] = key[i] + 0.01 + wide * wide
+            else:
+                if move > 1 - CFG["flip"]:
+                    i = either[int(rng.integers(len(either)))]
+                    q[i], lo, size = other[q[i]], now[2][i] - 3, size / 2
+                key = [u + size * x if lo < u < lo + 3 + 15 * wide else u for u, x in zip(key, rng.normal(size=n).tolist())]
+            new = closed(q, key, now[1] + 1.5)
+            if new and new[0] <= now[0] + CFG["slack"] * (1 - m / passes):
+                now = new
+                del waits[:]
+                if new[0] < best[0]:
+                    best = new
+        return best
+    tries = [shifted(closed([t["q"] for t in tasks], [turn_of(t, lag) for t in tasks], 1e9), CFG["passes"]) for lag in CFG["lags"]]
+    joint = max(i for i, t in enumerate(tasks) if t["turn"] and t["turn"][0] == 0)
+    late = [t["turn"] is not None and t["turn"][0] > 0 for t in tasks]
+    for _ in range(CFG["rounds"]):
+        first = [sum(length(u[4], u[3], *o, upto=joint) for o in every) for u in tries]
+        u = tries[first.index(min(first))]
+        v = min(zip(tries, first), key=lambda w: w[0][0] - w[1])[0]
+        shift = u[2][joint] - v[2][joint]
+        both = closed([b if z else a for a, b, z in zip(u[4], v[4], late)], [b + shift if z else a for a, b, z in zip(u[2], v[2], late)], 1e9)
+        best = min(tries + [both], key=lambda w: w[0])
+        tries = [shifted(best, CFG["more"]) for _ in range(CFG["again"])]
+    best = min(tries, key=lambda w: w[0])
+
+    def moved(issue, i, j, forward):
+        a, b = issue.index(j), issue.index(i)
+        span = issue[a:b + 1]
+        if forward:
+            take = {i}
+            for u in reversed(span):
+                if u in take:
+                    take.update(v for v, _ in pred[u])
+        else:
+            take = {j}
+            for u in span:
+                if any(v in take for v, _ in pred[u]):
+                    take.add(u)
+        if i in take and j in take:
+            return None
+        return issue[:a] + [u for u in span if (u in take) == forward] + [u for u in span if (u in take) != forward] + issue[b + 1:]
+
+    def total(q, issue, a, old):
+        ends, last = [], {}
+        for i in issue[:a]:
+            last[q[i]] = i
+        for (before, dur, sem), end in zip(every, old):
+            end, free = list(end), {x: end[last[x]] if x in last else 0.0 for x in "VSPGYW"}
+            for i in issue[a:]:
+                mine = q[i]
+                st = free[mine]
+                for j, lag in before[i]:
+                    u = end[j] + lag + (own[i] if q[j] == mine else sem)
+                    if u > st:
+                        st = u
+                end[i] = free[mine] = st + dur[i]
+            ends.append(end)
+        return sum(max(end[i] + tail[i] for i in stores) for end in ends), issue, q, ends
+    stores = [i for i in range(n) if tail[i] > 0]
+    now = best = total(best[4], best[3], 0, [none] * len(every))
+    del waits[:]
+    for m in range(CFG["moves"]):
+        if not waits:
+            waits.extend(held(now[2], now[1], *every[m % len(every)]))
+        i, j = waits.pop(int(rng.integers(len(waits))))
+        kind, luck = rng.random(2).tolist()
+        issue, q = now[1], now[2]
+        if kind < 0.25 and (tasks[i]["either"] or tasks[j]["either"]):
+            u = i if tasks[i]["either"] and (kind < 0.12 or not tasks[j]["either"]) else j
+            q = list(q)
+            q[u] = other[q[u]]
+        else:
+            issue = moved(issue, i, j, kind < 0.65)
+            if issue is None:
+                continue
+        new = total(q, issue, now[1].index(j), now[3])
+        if new[0] <= now[0] - CFG["heat"] * (1 - m / CFG["moves"]) * np.log(luck + 1e-9):
             now = new
-        if new[0] < best[0]:
-            best = new
-    return best[2]
+            del waits[:]
+            if new[0] < best[0]:
+                best = now
+    return best[1], best[2]
 
 
 def emit(g, T, tasks):
@@ -633,14 +792,18 @@ def emit(g, T, tasks):
     known, done = {q: {} for q in eng}, {}
     sent, ends = 0, []
     if not ORDER:
-        ORDER.extend(order(tasks))
+        del QUEUE[:]
+        for u, v in zip((ORDER, QUEUE), order(tasks)):
+            u.extend(v)
     for i in ORDER:
         t = tasks[i]
         NOTE[0] = t["lab"]
-        q = t["q"]
+        q = QUEUE[i]
+        if q == "W":
+            continue
         k, need = known[q], {}
         for d in t["deps"]:
-            if d in t["soft"]:
+            if d in t["soft"] or QUEUE[tid(d)] == "W":
                 continue
             s, v, kn = done[d]
             if k.get(s, 0) < v and need.get(s, (0, None))[0] < v:

import numpy as np
from concourse.bass import DstId, RemoteDMATransfer
from concourse.mybir import AluOpType, ActivationFunctionType

AL, AF = AluOpType, ActivationFunctionType
NR, L, ST, GENS = 8, 192, 3, 2
GW, XW = 1536, 3072
C = 12
CFG = {"halves": [(0, 96, (32, 32, 32)), (96, 96, (32, 32, 32))],
       "rec": (("SSV", "SVV"), ("SSS", "SSV"), ("SSS", "SSV")),
       "ks": (4, 5, 5, 2), "own": 0.04, "pcut": 1, "wide": True,
       "lags": (4.0, 4.5, 5.0, 5.5), "passes": 500, "rounds": 3, "again": 2, "more": 400, "moves": 9000, "seed": 4, "flip": 0.15, "swap": 0.6, "slack": 0.4, "heat": 0.2}
PLAN = {"mask": (-3.4, 0.6), "hosts": (-2.3, 0), "names": (-2.3, 1.0), "rows": (-1.0, 1.5), "list": (-0.2, 1.0), "records": (0.2, 0.5), "T": (1.1, 0),
        "old": (2.0, 0), "val": (2.7, 0), "pre": (2.0, 0), "add": (3.0, 0.3), "abs": (3.4, 0.4), "sum": (3.9, 0.4), "sign": (5.4, 0), "err": (5.5, 0),
        "first": (5.8, 0), "pick": (5.8, 0), "place": (6.1, 0), "wrap": (6.8, 0), "lists": (7.0, 0), "new": (7.3, 0), "put": (7.5, 0), "name": (6.9, 0),
        "rows out": (7.9, 0), "count": (8.4, 0), "limit": (9.6, 0), "order": (5.9, 0), "home": (13.0, 0), "mother": (2.5, 0),
        "start": (6, 19, 33), "generation": 48}
POOL = {"f32": ("float32", 6000), "bf": ("bfloat16", 56000), "hf": ("float16", 33600), "u16": ("uint16", 6000), "i32": ("int32", 3600)}
SIZE = {"f32": 4, "bf": 2, "hf": 2, "u16": 2, "i32": 4}
SCRATCH = {"p_" + k: ("sbuf", [128, v[1]], v[0]) for k, v in POOL.items()}
SCRATCH.update({"bank%d" % b: ("psum", [128, 512], "float32") for b in range(8)})
SCRATCH.update({"turns": ("sbuf", [128, 16, 8, 16], "bfloat16"), "ring": ("sbuf", [128, 8, 32], "bfloat16"), "twice": ("sbuf", [128, 8, 32], "float32")})
SEMAPHORES = ["sV", "sS", "sP", "sG", "left"] + ["d%d" % i for i in range(20)] + ["r%d" % i for i in range(60)]
CY = 0.00083
COSTS = [{"f": 1.25, "fix": 0.01, "min": 64, "gather": 1.56, "scatter": 3.5, "pe": 0.00034, "issue": 0.9, "hop": 2.3, "row": 0.04, "sem": 0.08},
         {"f": 1.1, "fix": 0.03, "min": 64, "gather": 1.3, "scatter": 2.5, "pe": 0.00038, "issue": 0.8, "hop": 2.2, "row": 0.01, "sem": 0.25},
         {"f": 1.5, "fix": 0.01, "min": 64, "gather": 2.0, "scatter": 5.0, "pe": 0.00042, "issue": 1.2, "hop": 3.0, "row": 0.04, "sem": 0.12},
         {"f": 1.3, "fix": 0.02, "min": 64, "gather": 1.7, "scatter": 4.0, "pe": 0.00036, "issue": 1.1, "hop": 3.0, "row": 0.1, "sem": 0.1}]
NOTE, ORDER, QUEUE = [""], [], []


def rank_program(g, core, T, topo):
    rank = T.rank_of(core)
    if rank is None:
        return
    tasks, used = [], {k: 0 for k in POOL}
    bank_use = [{"q": None, "now": [], "before": []} for _ in range(8)]
    ndma, nrem, lab, turn, wide = [0], [0], [""], [None], [False]

    def mk(b, lo, n, mut=False):
        return {"b": b, "lo": lo, "n": n, "wr": [], "rd": [], "mut": mut}

    def tile(pool, n, mut=False):
        lo, al = used[pool], 32 // SIZE[pool]
        used[pool] = (lo + n + al - 1) // al * al
        assert used[pool] <= POOL[pool][1], pool
        return mk("p_" + pool, lo, n, mut)

    def part(t, a, n):
        return mk(t["b"], t["lo"] + a, n)

    def ps(bank, lo=0, n=512):
        t = mk("bank%d" % bank, lo, n)
        t["bank"] = bank
        return t

    def ap(t, a=0, b=None, st=1):
        b = t["n"] if b is None else b
        buf = T[t["b"]]
        return buf[:, t["lo"] + a:t["lo"] + b] if st == 1 else buf[:, t["lo"] + a:t["lo"] + b:st]

    def task(q, dur, ins, outs, fn, kind="c", extra=None, at=0.0, either=False):
        i, deps = len(tasks), {}
        for t in ins:
            for w, lag in t["wr"]:
                deps[w] = max(deps.get(w, 0), lag)
        for t in outs:
            if t["mut"]:
                for w, lag in t["wr"]:
                    deps[w] = max(deps.get(w, 0), lag)
                for r in t["rd"]:
                    deps.setdefault(r, 0)
        for t in list(ins) + list(outs):
            if "bank" in t:
                bu = bank_use[t["bank"]]
                if bu["q"] != q or either:
                    bu.update(q=i if either else q, now=[], before=bu["now"])
                for j in bu["before"]:
                    deps.setdefault(j, 0)
                bu["now"].append(i)
        deps.pop(i, None)
        tasks.append({"q": q, "dur": (dur + np.zeros(len(COSTS))).tolist(), "deps": deps, "fn": fn, "kind": kind, "x": extra, "soft": set(),
                      "turn": turn[0], "at": at or 0.07 * (i - 16), "lab": lab[0], "either": either})
        for t in outs:
            if t["mut"]:
                t["wr"], t["rd"] = [], []
            t["wr"].append((i, 0))
        for t in ins:
            t["rd"].append(i)
        return i

    def soft(i, j):
        if j not in tasks[i]["deps"]:
            tasks[i]["deps"][j] = 0
            tasks[i]["soft"].add(j)

    def when(gen, t, h, what, j=0):
        turn[0] = (gen, t, h, what, j)

    def vc(n, f=1.0):
        return np.array([(c["fix"] + max(c["min"], n * f) * CY) * c["f"] for c in COSTS])

    def gc_(n, k="gather"):
        return np.array([(0.06 + n * c[k] * CY) * c["f"] for c in COSTS])

    def ts(out, oa, in0, s1, op0, s2, op1, ins, n, f=1.0, at=0.0, dur=None):
        def fn():
            if op1 is None:
                return [g.vector.tensor_scalar(oa, in0, s1, None, op0)]
            return [g.vector.tensor_scalar(oa, in0, s1, s2, op0, op1)]
        return task("V", vc(n, f) if dur is None else dur, ins, [out], fn, at=at)

    def tt(out, oa, in0, in1, op, ins, n=0, f=1.0, dur=None):
        return task("V", vc(n, f) if dur is None else dur, ins, [out], lambda: [g.vector.tensor_tensor(oa, in0, in1, op)])

    def tcopy(out, oa, in0, ins, n=0, f=1.0, dur=None):
        return task("V", vc(n, f) if dur is None else dur, ins, [out], lambda: [g.vector.tensor_copy(oa, in0)])

    def act(out, oa, in0, func, ins, n=0, dur=None, bias=0.0, scale=1.0, acc=None):
        return task("S", vc(n) if dur is None else dur, ins, [out] + ([acc] if acc else []),
                    lambda: [g.scalar.activation(oa, in0, func, bias=bias, scale=scale, accum_out=ap(acc) if acc else None)])

    def copy(q, out, oa, in0, ins, n=0, dur=None):
        def fn():
            return [g.vector.tensor_copy(oa, in0) if QUEUE[i] == "V" else g.scalar.activation(oa, in0, AF.Copy)]
        i = task(q, vc(n) if dur is None else dur, ins, [out], fn, either=True)
        return i

    def iota(out, pat, base, cm, flag=True):
        task("G", 0.16 + 2.5 * out["n"] * CY, [], [out], lambda: [g.iota(ap(out), pat, base, cm, allow_small_or_imprecise_dtypes=flag)])

    def keep(out, src, op, fill, base):
        task("G", 0.5, [src], [out], lambda: [g.affine_select(ap(out), ap(src), [[1, 128]], op, fill, base, -1)])

    def mms(outs, ins, groups, n, after=None, ends=(True, True)):
        def fn():
            r = []
            for gr in groups:
                for j, (o, l, x) in enumerate(gr):
                    m = g.tensor.matmul(o, l, x, ends[0] and j == 0, ends[1] and j == len(gr) - 1)
                r.append(m)
            return r
        i = task("P", np.array([(0.02 + n * c["pe"]) * c["f"] for c in COSTS]), ins, outs, fn)
        if after:
            for w, _ in after["wr"][:-1]:
                soft(i, w)
        return i

    def load(out, oa, src, dur, q="Y"):
        i = task(q, 0.05, [], [out], lambda: [(g.sync if q == "Y" else g.scalar).dma_start(oa, src)], "d", ndma[0], at=-5.0)
        out["wr"] = [(w, dur if w == i else lg) for w, lg in out["wr"]]
        ndma[0] += 1
        return i

    def store(dst, oa, ins):
        task("Y", 2.0, ins, [], lambda: [g.sync.dma_start(dst, oa)], "d", ndma[0])
        ndma[0] += 1

    far = [e for e in range(32) if all(e in topo.engines(u, v) for u in T.cores for v in T.cores if u != v)]

    def engines(r, m, moves):
        ways = [topo.engines(T.cores[r], T.cores[(r + u[4]) % NR]) if wide[0] else far for u in moves]
        if len(set(len(w) for w in ways)) > 1:
            return far if ways[m] == far else [e for e in ways[m] if e not in far]
        return ways[m][m * len(ways[m]) // len(moves):(m + 1) * len(ways[m]) // len(moves)]

    def send(moves):
        got, out, n, trs = [], [], len(moves), []
        for m, (src, sa, dst, da, d) in enumerate(moves):
            name = "r%d" % nrem[0]
            nrem[0] += 1
            rid, pid, _ = topo.addr(T.cores[(rank + d) % NR])
            es = engines(rank, m, moves)
            trs.append((rid, pid, sum(1 << e for e in es), name, sa, da))
            got.append((name, len(engines((rank - d) % NR, m, moves))))
            out.append(len(es))

        def fn():
            if n == 1:
                rid, pid, mask, name, sa, da = trs[0]
                g.remote_dma(da, sa, T.sem[name], T.sem.left, pid, rid, mask)
            else:
                g.remote_dma_fused([RemoteDMATransfer(dst_ids=[DstId(rid=rid, pnc=pid)], dma_engine_mask=mask, remote_sem=T.sem[name], src=sa, dst=da)
                                    for rid, pid, mask, name, sa, da in trs], local_sem=T.sem.left)
            return []
        i = task("G", np.array([c["issue"] for c in COSTS]) + (3.5 if nrem[0] == 1 else 0), [m[0] for m in moves], [], fn, "r", (got, sum(out)))
        dst = moves[0][2]
        w = task("W", np.array([16 * n * c["row"] for c in COSTS]) + n * dst["n"] * SIZE[dst["b"][2:]] * 128 / 90000.0, [], [], None, "w")
        tasks[w]["deps"][i, 0] = 0.0
        for m, (src, sa, dst, da, d) in enumerate(moves):
            dst["wr"] += [((i, m), 0.0), ((w, 0), 0.0)]
        return i

    HV = CFG["halves"]
    gni, nbi, thi = tile("i32", GW), tile("i32", GW), tile("i32", 1)
    X, a0 = tile("bf", XW, True), tile("bf", L)
    NG = 2
    gh = [part(gni, GW // NG * j, GW // NG) for j in range(NG)]
    seq = [load(gh[j], ap(gh[j]), T.gn[:, GW // NG * j:GW // NG * (j + 1)], 2.0 + 2.2 * (j + 1) / NG) for j in range(NG)]
    nh = [part(nbi, 8 * i0, 8 * W) for i0, W, _ in HV]
    seq += [load(nh[0], ap(nh[0]), T.nb[:, 0:nh[0]["n"]], 5.2), load(X, ap(X), T.x[:], 7.2), load(nh[1], ap(nh[1]), T.nb[:, nh[0]["n"]:GW], 8.2),
            load(a0, ap(a0), T.a0[:], 8.5), load(thi, ap(thi), T.th[:], 8.7)]
    for u, v in zip(seq, seq[1:]):
        soft(v, u)

    lab[0] = "const"

    def col(ins, src, s1, op0, s2=None, op1=None, n=1, pool="f32", f=1.0):
        t = tile(pool, n)
        ts(t, ap(t), src, s1, op0, s2, op1, ins, n, f)
        return t

    def acol(src, scale, bias=0.0, pool="bf", a=0, n=None, out=None, o=0):
        n = src["n"] if n is None else n
        t = out or tile(pool, n)
        cols = [c for c in (scale, bias) if isinstance(c, dict)]
        act(t, ap(t, o, o + n), ap(src, a, a + n), AF.Identity, [src] + cols, n,
            scale=ap(scale) if isinstance(scale, dict) else scale, bias=ap(bias) if isinstance(bias, dict) else bias)
        return t
    PW = max(max(p) for _, _, p in HV)
    ip, pni = tile("i32", 1), tile("i32", 128)
    im, kpat, mgf, ii0, il = tile("f32", 144), tile("bf", 16 * PW), tile("f32", 128), tile("f32", C), tile("bf", L)
    iota(ip, [[0, 1]], 0, 1, False)
    iota(im, [[1, 144]], 0, 0)
    iota(mgf, [[1, 8], [0, 16]], 0, 0)
    iota(kpat, [[0, PW], [1, 16]], 0, 0)
    iota(ii0, [[16, C]], 0, 0)
    iota(il, [[1, L]], 0, 0)
    iota(pni, [[0, 8], [1, 16]], 1, 1, False)
    for j in range(len(tasks) - 6, len(tasks)):
        soft(j, j - 1)
    si = col([ip], ap(ip), 15, AL.bitwise_and, pool="i32")
    gi = col([ip], ap(ip), 4, AL.arith_shift_right, pool="i32")
    scol = col([si], ap(si), 0.0, AL.add)
    zc = col([gi], ap(gi), 16.0, AL.mult, 15.0, AL.add)
    row = {0: col([scol], ap(scol), 0.0, AL.is_equal)}
    Zb = col([im, zc], ap(im), ap(zc), AL.is_equal, n=144, pool="bf")
    gcol = col([gi], ap(gi), 0.0, AL.add)
    pcol = col([ip], ap(ip), 0.0, AL.add)
    row.update({r: col([scol], ap(scol), float(r), AL.is_equal) for r in (3, 4)})
    rm3 = col([scol], ap(scol), 3.0, AL.is_ge)
    r01 = col([scol], ap(scol), 2.0, AL.is_lt)
    Idb = col([im, pcol], ap(im, 0, 128), ap(pcol), AL.is_equal, n=128, pool="bf")
    Blk = col([mgf, gcol], ap(mgf), ap(gcol), AL.is_equal, n=128, pool="bf")
    mask0 = col([kpat, scol], ap(kpat), ap(scol), AL.is_equal, n=16 * PW, pool="bf", f=0.5)
    Tri, M1, M2, PNm, Dm = tile("bf", 128), tile("bf", 128), tile("bf", 128), tile("bf", 128), tile("bf", 128)
    Zn, Im, I512, I15 = acol(Zb, -1.0), acol(Idb, -1.0), acol(Idb, 512.0), acol(Idb, 15.0)
    keep(Tri, Blk, AL.is_gt, 0.0, 0)
    keep(M1, Tri, AL.not_equal, -16.0, 0)
    m2 = ps(7, 0, 128)
    mms([m2], [Idb, M1, Zb], [[(ap(m2), ap(Idb), ap(M1)), (ap(m2), ap(Idb), ap(Zb, 15, 143))]], 256)
    act(M2, ap(M2), ap(m2), AF.Copy, [m2], 128)
    r15 = col([scol], ap(scol), 15.0, AL.is_lt)
    PN0 = acol(Idb, acol(acol(scol, 1.0, 1.0, "f32"), r15, 0.0, "f32"))
    M3 = acol(M1, 1024.0)
    pn2 = col([pni], ap(pni), 15, AL.bitwise_and, n=128, pool="i32")
    tt(PNm, ap(PNm), ap(pn2), ap(Blk), AL.mult, [pn2, Blk], 128, 2)
    th1 = acol(scol, 1.0, 16.0, "f32")
    E0 = acol(Idb, acol(row[0], 16.0, 0.0, "f32"))
    e3 = acol(scol, 32.0, -80.0, "f32")
    keep(Dm, Idb, AL.not_equal, -1.0, 1)
    D512, c320 = acol(Dm, 512.0), acol(scol, 0.0, -0.625)
    R3, R4n = acol(Blk, acol(row[3], 32.0, 0.0, "f32")), acol(Blk, acol(row[4], -1.0, 0.0, "f32"))
    K4, K01 = acol(Idb, row[4]), acol(Idb, r01)
    ones = acol(il, 0.0, 1.0)
    i8 = acol(il, 8.0)
    twice, ring, turns = mk("twice", 0, 256), mk("ring", 0, 256), mk("turns", 0, 2048)
    task("G", 0.7, [], [twice], lambda: [g.iota(T.twice[:], [[16, 8], [0, 2], [1, 16]], 0, 0, allow_small_or_imprecise_dtypes=True)])
    ts(ring, T.ring[:], T.twice[:], ap(pcol), AL.is_equal, None, None, [twice, pcol], 256)
    for k in range(16):
        copy("S", turns, T.turns[:, k], T.ring[:, :, 16 - k:32 - k], [ring], 128)
    ckr = tile("i32", 16)
    iota(ckr, [[-1, 16]], 16, 1, False)
    cki = col([ckr], ap(ckr), 15, AL.bitwise_and, n=16, pool="i32")
    ck = col([cki], ap(cki), 0.0, AL.add, n=16, pool="bf")
    ii = col([ii0, scol], ap(ii0), ap(scol), AL.add, n=C)
    nth = col([thi], ap(thi), -1.0, AL.mult, -0.5, AL.add)
    b3, dfl = {}, {}
    for i0, W, _ in HV:
        cw, c0 = W // 16, i0 // 16
        if W not in b3:
            b3[W] = acol(scol, -1023.0, 2.0 * W - 16384.0, "f32")
        for t in range(2):
            d = dfl[i0, t] = tile("bf", 3 * cw)
            acol(ii, 1.0, -float(i0), a=c0, n=cw, out=d)
            acol(ii, 16.0, a=c0, n=cw, out=d, o=cw)
            acol(ii, 8.0 * (1 - t), a=c0, n=cw, out=d, o=2 * cw)
    lab[0] = "conv"
    G = tile("f32", GW)
    for j in range(NG):
        ts(G, ap(G, GW // NG * j, GW // NG * (j + 1)), ap(gh[j]), -1536.0, AL.add, None, None, [gh[j]], GW // NG, at=2.0 + 2.2 * (j + 1) / NG)
    G["mut"] = True
    El0, NB0 = [], []
    for h, (i0, W, pieces) in enumerate(HV):
        El0.append(tile("u16", W))
        when(0, 0, h, "hosts")
        tcopy(El0[h], ap(El0[h]), ap(nh[h], 0, 8 * W, 8), [nh[h]], W)
        NB0.append(tile("hf", W))
        when(0, 0, h, "old")
        tcopy(NB0[h], ap(NB0[h]), ap(El0[h]), [El0[h]], W, 0.5)

    def Z(z, k):
        return ap(z, 15 - k, 143 - k)

    BW, BD, BY, BM = (0, 1), (2, 3), (4, 5, 6), 7
    ny = [0]
    yas = [tile("bf", 16 * W) for _, W, _ in HV]
    lim = nth
    a = [part(a0, i0, W) for i0, W, _ in HV]
    for p in a:
        p["wr"] = a0["wr"]
    for gen in range(GENS):
        lab[0] = "g%d mother" % gen
        when(gen, 0, 0, "mother")
        mo, mother, win = tile("hf", L), tile("hf", L), tile("f32", L + 96)
        own, come, prev = part(win, 0, L), part(win, L, 48), part(win, L + 48, 48)
        ts(mo, ap(mo), ap(G, 0, GW, 8), ap(rm3), AL.mult, None, None, [G, rm3], L)
        imo = send([(mo, ap(mo), mother, ap(mother), 2)])
        copy("S", own, ap(own), ap(G, 0, GW, 8), [G], L)
        R, info = [None] * len(HV), [None] * len(HV)
        oh, cum, dau = tile("bf", L), tile("bf", L), tile("f32", L)
        for t in range(ST):
            last, st = t == ST - 1, []
            for h, (i0, W, pieces) in enumerate(HV):
                lab[0] = "g%d t%d h%d front" % (gen, t, h)
                cw = W // 16
                nx = 3 * W if last else 2 * W
                Gx, Wl, Tb = tile("hf", nx + 17 * W), tile("u16", cw + W), tile("bf", 18 * W)
                Gg = part(Gx, nx, 17 * W)
                Wp, nM, Tt, recs = ps(BW[h], 0, cw + W), part(Gg, 0, W), part(Tb, 0, W), []
                s = {"Tb": Tb, "Wp": Wp, "nM": nM, "T": Tt, "recs": recs, "Gx": Gx}
                if t == 0:
                    when(gen, t, h, "hosts")
                    ts(nM, ap(nM), ap(G, 8 * i0, 8 * (i0 + W), 8), ap(row[0]), AL.mult, None, None, [G, row[0]], W)
                    s["oh"], s["nb"] = ones, NB0[h]
                else:
                    mask, Rm = R[h]
                    s["oh"], rows, s0 = mask, [], 0
                    if h:
                        when(gen, t, h, "mask")
                        Rp, mask = mask, tile("bf", 17 * W)
                        mask["n"] = W
                        s["oh"], rows = mask, [mk(mask["b"], mask["lo"] + W, 16 * W)] * len(pieces)
                        ts(mask, ap(mask), ap(Rp), ap(ck, 0, 1), AL.is_equal, None, None, [Rp, ck], W, 0.5)
                        for k in range(16):
                            ts(rows[0], ap(rows[0], k, 16 * W, 16), ap(Rp), ap(ck, k, k + 1), AL.is_equal, None, None, [Rp, ck], W, 0.5)
                    for j, pw in enumerate(() if h else pieces):
                        when(gen, t, h, "mask", j)
                        mp = ps(BD[h] if j else BW[h], 0, 16 * pw)
                        for c in range(2):
                            mms([mp], [mask, turns], [[(ap(mp, k, 16 * pw, 16), T.turns[:, k], ap(mask, s0, s0 + pw)) for k in range(8 * c, 8 * c + 8)]],
                                8 * 64, after=mp, ends=(c == 0, c == 1))
                        rows.append(mk(mask["b"], mask["lo"] + W + 16 * s0, 16 * pw))
                        copy("S", rows[j], ap(rows[j]), ap(mp), [mp], 16 * pw)
                        s0 += pw
                    when(gen, t, h, "hosts")
                    El = mk(Rm["b"], Rm["lo"] + cw, W)
                    tcopy(El, ap(El), ap(nbi).indirect(ap(Rm)), nh + [Rm], dur=gc_(W))
                    if not last:
                        when(gen, t, h, "old")
                        s["hw"] = tile("hf", cw + W)
                        s["nb"] = dict(s["hw"], lo=s["hw"]["lo"] + cw, n=W)
                        tcopy(s["hw"], ap(s["hw"]), ap(Rm, 0, cw + W), [El, Rm], cw + W, 0.5)
                s0 = 0
                for j, pw in enumerate(pieces):
                    e0, e1 = (0 if j == 0 else W + 16 * s0), W + 16 * (s0 + pw)
                    l0, l1 = e0 // 16, e1 // 16
                    Gp = part(Gg, e0, e1 - e0)
                    when(gen, t, h, "names", j)
                    if t == 0:
                        tt(Gp, ap(Gg, W + 16 * s0, e1), ap(G).indirect(ap(El0[h], s0, s0 + pw)), ap(mask0, 0, 16 * pw), AL.mult, [G, El0[h], mask0], dur=gc_(16 * pw))
                    else:
                        tt(Gp, ap(Gp), ap(G).indirect(ap(Rm, l0, l1)), ap(mask, e0, e1), AL.mult, [G, El, mask, rows[j]], dur=gc_(e1 - e0))
                        if j == 0:
                            nM["wr"] = Gp["wr"]
                    Wq, pc = ps(BW[h], l0, l1 - l0), CFG["pcut"]
                    when(gen, t, h, "rows", j)
                    for c in range(pc):
                        mms([Wq, Wp], [Gp, nM, Zb], [[(ap(Wq), Z(Zb, k), ap(Gp, k, e1 - e0, 16)) for k in range(16 * c // pc, 16 * (c + 1) // pc)]],
                            16 // pc * max(64, l1 - l0), after=Wq, ends=(c == 0, c == pc - 1))
                    Wj, rec = part(Wl, l0, l1 - l0), part(Tb, W + e0, e1 - e0)
                    when(gen, t, h, "list", j)
                    ts(Wj, ap(Wj), ap(Wq), 1536.0, AL.add, None, None, [Wq], l1 - l0)
                    when(gen, t, h, "records", j)
                    copy(CFG["rec"][t][h][j], rec, ap(rec), ap(X).indirect(ap(Wj)), [X, Wj], dur=gc_(e1 - e0))
                    recs.append(rec)
                    if j == 0:
                        when(gen, t, h, "T")
                        dq = ps(BD[h], 0, W)
                        mms([dq], [rec, a[h], Idb, Im], [[(ap(dq), ap(Idb), ap(rec, 0, W)), (ap(dq), ap(Im), ap(a[h]))]], 2 * W)
                        act(Tt, ap(Tt), ap(dq), AF.Abs, [dq], W)
                    s0 += pw
                st.append(s)
            cnt = ps(BM, 128, L)
            for h, (i0, W, pieces) in enumerate(HV):
                lab[0] = "g%d t%d h%d mid" % (gen, t, h)
                s = st[h]
                cw = W // 16
                Tb, Tt, recs, Wp, nM = s["Tb"], s["T"], s["recs"], s["Wp"], s["nM"]
                when(gen, t, h, "val")
                val, x3 = ps(BW[h], 224, 2 * W), ps(BW[h], 224 + 2 * W, W)
                pn = PNm if t else PN0
                grp, ins = [[(ap(val, 0, W), ap(pn), ap(s["oh"], 0, W))]], [pn, s["oh"]]
                if not last:
                    old = (ap(Im), ap(i8, i0, i0 + W)) if t == 0 else (ap(R4n), ap(info[h]))
                    grp.append([(ap(val, W, 2 * W), ap(Idb), ap(s["nb"])), (ap(val, W, 2 * W),) + old])
                    ins += [Idb, s["nb"], Im, i8] + ([R4n, info[h]] if t else [])
                else:
                    fo = ps(BW[h], cw + W, W)
                    grp.append([(ap(fo), Z(Zb, 0), ap(nM))])
                    ins += [Zb, nM]
                mms([val] + ([fo] if last else []), ins, grp, 3 * W)
                D, Ys, KS = ps(BD[h], 0, W), [], CFG["ks"]
                for q, kg in enumerate(KS):
                    Ys.append(ps(BY[ny[0] % len(BY)], 0, kg * W))
                    ny[0] += 1
                    if q < len(BY):
                        when(gen, t, h, "pre", q)
                        mms([Ys[q]], [Idb, Tt], [[(ap(Ys[q], k * W, k * W + W), ap(Idb), ap(Tt)) for k in range(kg)]], kg * W, ends=(True, False))
                for q, (Y, kg) in enumerate(zip(Ys, KS)):
                    k0 = sum(KS[:q])
                    ya = part(yas[h], k0 * W, kg * W)
                    when(gen, t, h, "add", q)
                    vs = [(ap(Y, k * W, k * W + W), ap(Idb), ap(Tb, 2 * W + k0 + k, 18 * W, 16)) for k in range(kg)]
                    if q < len(BY):
                        mms([Y], recs + [Idb], [vs], kg * W, after=Y, ends=(False, True))
                    else:
                        mms([Y], recs + [Idb, Tt], [[v, (v[0], ap(Idb), ap(Tt))] for v in vs], 2 * kg * W)
                    when(gen, t, h, "abs", q)
                    act(ya, ap(ya), ap(Y), AF.Abs, [Y], kg * W, bias=-255.0)
                    when(gen, t, h, "sum", q)
                    mms([D], [ya, Zb], [[(ap(D), Z(Zb, k0 + k), ap(ya, k * W, k * W + W)) for k in range(kg)]], kg * W, after=D, ends=(q == 0, q == len(KS) - 1))
                lab[0] = "g%d t%d h%d tail" % (gen, t, h)
                sg = tile("bf", W)
                when(gen, t, h, "sign")
                act(sg, ap(sg), ap(D), AF.Sign, [D, lim], W, bias=ap(lim))
                if last:
                    when(gen, t, h, "err")
                    Ep = ps(BW[h], 224 + W, W)
                    mms([Ep], [info[h], sg, R3, Blk], [[(ap(Ep), ap(R3), ap(info[h])), (ap(Ep), ap(Blk), ap(sg))]], 2 * W)
                    ohh, cm = part(oh, i0, W), part(cum, i0, W)
                    ts(ohh, ap(ohh), ap(Ep), ap(e3), AL.is_ge, None, None, [Ep, e3], W)
                    before = st[h - 1]["cum"] if h else None

                    def scan(ohh=ohh, cm=cm, W=W, before=before):
                        return [g.vector.tensor_tensor_scan(ap(cm), ap(ones, 0, W), ap(ohh), ap(before, before["n"] - 1) if before else 0.0, AL.mult, AL.add)]
                    task("V", vc(W, 0.5), [ohh, ones] + ([before] if before else []), [cm], scan)
                    s["cum"], s["ohh"] = cm, ohh
                when(gen, t, h, "first")
                nx = 3 * W if last else 2 * W
                x = ps(BD[h], W, nx)
                mms([x], [sg, M1, M2, E0, ones], [[(ap(x, 0, W), ap(E0), ap(ones, 0, W)), (ap(x, 0, W), ap(M2), ap(sg))], [(ap(x, W, 2 * W), ap(M1), ap(sg))]]
                    + ([[(ap(x, 2 * W, nx), Z(Zb, 0), ap(sg))]] if last else []), W + nx)
                mms([x3], [sg, M3, I15, il], [[(ap(x3), ap(M3), ap(sg)), (ap(x3), ap(I15), ap(il, 0, W))]], 2 * W)
                FF, Q = part(s["Gx"], 0, nx), tile("hf", 3 * W)
                Ql, Qv = part(Q, 0, W), part(Q, W, 2 * W)
                FI, nq = dict(FF, lo=FF["lo"] + W, n=W), W if last else 2 * W
                ts(FF, ap(FF), ap(x), ap(th1), AL.is_ge, None, None, [x, th1], nx)
                tt(Qv, ap(Qv, 0, nq), ap(val, 0, nq), ap(FF, 0, nq), AL.mult, [val, FF], nq)
                if not last:
                    pp, pb = ps(BM, 0, W), tile("bf", W)
                    mms([pp], [Blk, Qv], [[(ap(pp), ap(Blk), ap(Qv, 0, W))]], W)
                when(gen, t, h, "pick")
                ts(Ql, ap(Ql), ap(x3), ap(b3[W]), AL.add, 0.0, AL.max, [x3, b3[W]], W)
                if not last:
                    when(gen, t, h, "place")
                    if h:
                        copy("V", pb, ap(pb), ap(pp), [pp], W)
                    else:
                        ts(pb, ap(pb), ap(pp), ap(scol), AL.is_equal, None, None, [pp, scol], W)
                    Rp, Rm = tile("bf", W if h else 17 * W), tile("u16", cw + W)
                    Rp["n"], Rm["n"] = W, cw
                    R[h] = (Rp, Rm)
                    im0 = send([(pb, ap(pb), Rp, ap(Rp), 1)])
                    if gen == 0:
                        soft(im0, imo)
                when(gen, t, h, "wrap")
                n = (W + nq) // 16
                Op, O, d = ps(BD[h], 0, n), tile("u16", n), dfl[i0, min(t, 1)]
                gr = [(ap(Op), ap(Idb), ap(d, 0, n))] + ([(ap(Op, 2 * cw, n), ap(Idb), ap(s["hw"], 0, cw))] if t == 1 else [])
                gr += [(ap(Op), Z(Zb, r), ap(Q, r, W + nq, 16)) for r in range(16)]
                mms([Op], [Qv, Ql, Zb, Idb, d] + ([s["hw"]] if t == 1 else []), [gr], 18 * 64)
                when(gen, t, h, "lists")
                tcopy(O, ap(O), ap(Op), [Op], n)
                if not last:
                    im1 = send([(O, ap(O, 2 * cw, n), Rm, ap(Rm), 1)])
                    soft(im1, im0)
                an, a2 = tile("bf", W), tile("bf", W)
                when(gen, t, h, "new")
                copy("S", an, ap(an), ap(Tb).indirect(ap(O, 0, cw)), recs + [Tt, O], dur=gc_(W))
                when(gen, t, h, "put")

                def put(O=O, an=an, u=cw, v=2 * cw):
                    return [g.vector.tensor_copy(ap(X).indirect(ap(O, u, v)), ap(an))]
                task("V", gc_(W, "scatter"), [O, an], [X], put)
                lab[0] = "g%d t%d h%d info" % (gen, t, h)
                when(gen, t, h, "name")
                ch = ps(BM, 128 + i0, W)
                more = not (gen == GENS - 1 and last)
                if not last:
                    fo = ps(BW[h], cw + W, W)
                    mms([fo], [FF, Blk], [[(ap(fo), ap(Blk), ap(FI))]], W)
                if more:
                    mms([ch, cnt], [FF, ones], [[(ap(ch), ap(ones, 0, 128), ap(FI))]], W)
                Qe = tile("hf", 2 * W)
                tt(Qe, ap(Qe), ap(Wp, cw, cw + 2 * W), ap(s["Gx"], W, 3 * W), AL.mult, [Wp, fo, FF, nM], 2 * W)
                ip_ = ps(BW[h], 224, W)
                gr = [(Z(Zb, t), ap(Qe, 0, W))] + ([(Z(Zb, t), ap(Qe, W, 2 * W))] if last else [(Z(Zb, t), ap(nM)), (Z(Zn, t), ap(Qe, W, 2 * W))])
                ins = [Qe, nM, Zb, Zn]
                if t == 0:
                    gr += [(Z(Zn, 3), ap(FI)), (Z(Zb, 4), ap(Qv, W, 2 * W)), (ap(K4), ap(i8, i0, i0 + W))]
                    ins += [FF, Qv, K4, i8]
                elif not last:
                    gr += [(Z(Zn, 3), ap(FI)), (ap(Idb), ap(info[h]))]
                    ins += [FF, Idb, info[h]]
                else:
                    gr += [(ap(K01), ap(info[h])), (ap(Idb), ap(mother, i0, i0 + W))]
                    ins += [K01, Idb, info[h], mother]
                when(gen, t, h, "rows out")
                mms([ip_], ins, [[(ap(ip_),) + u for u in gr]], len(gr) * W)
                if last:
                    copy("S", dau, ap(dau, i0, i0 + W), ap(ip_), [ip_], W)
                    send([(an, ap(an), a2, ap(a2), -2)])
                else:
                    io, info[h] = tile("hf", W), tile("hf", W)
                    wide[0] = CFG["wide"]
                    tcopy(io, ap(io), ap(ip_), [ip_], W)
                    soft(send([(an, ap(an), a2, ap(a2), 1), (io, ap(io), info[h], ap(info[h]), 1)]), im1)
                a[h] = a2
            if more:
                lab[0] = "g%d t%d lim" % (gen, t)
                when(gen, t, h, "count")
                junk, acc, A1, A2, lim = tile("bf", L), tile("f32", 1), tile("i32", 1), tile("i32", 1), tile("f32", 1)
                act(junk, ap(junk), ap(cnt), AF.Identity, [cnt], L, scale=-1.0, bias=8.0, acc=acc, dur=vc(L) + 0.14)
                when(gen, t, h, "limit")
                tcopy(A1, ap(A1), ap(acc), [acc], 1)
                ts(A2, ap(A2), ap(A1), 63, AL.bitwise_and, None, None, [A1], 1)
                ts(lim, ap(lim), ap(A2), -1.0, AL.mult, ap(nth), AL.add, [A2, nth], 1)
        lab[0] = "g%d order" % gen
        when(gen, t, h, "order")
        xo = ps(BY[ny[0] % len(BY)], 0, L + 1)
        for u, (i0, W, _) in zip(st, HV):
            mms([xo], [u["cum"], u["ohh"], Dm, D512], [[(ap(xo, i0, i0 + W), ap(Dm), ap(u["cum"])), (ap(xo, i0, i0 + W), ap(D512), ap(u["ohh"]))]], 2 * W)
        mms([xo], [u["cum"], Im, I512, c320], [[(ap(xo, L), ap(I512), ap(c320)), (ap(xo, L), ap(Im), ap(cum, L - 1))]], 128)
        q1 = tile("bf", L)
        ts(q1, ap(q1), ap(xo, 0, L), ap(xo, L), AL.add, 0.0, AL.max, [xo], L)
        op_ = ps(BY[(ny[0] + 1) % len(BY)], 0, C)
        ny[0] += 2
        mms([op_], [q1, Zb], [[(ap(op_), Z(Zb, r), ap(q1, r, L, 16)) for r in range(16)]], 1024)
        po, pm, srt = tile("u16", C), tile("u16", C), tile("f32", L)
        ts(po, ap(po), ap(op_), -1.0, AL.mult, float(L), AL.add, [op_], C)
        send([(po, ap(po), pm, ap(pm), -2)])

        def scat(srt=srt, po=po, dau=dau):
            return [g.vector.tensor_copy(ap(srt).indirect(ap(po)), ap(dau))]
        task("V", gc_(L, "scatter"), [po, dau], [srt], scat)
        send([(srt, ap(srt, L - 48, L), come, ap(come), -2), (srt, ap(srt, L - 48, L), prev, ap(prev), -1)])
        lab[0] = "g%d home" % gen
        when(gen, t, h, "home")
        pi = col([pm], ap(pm), 0.0, AL.add, n=C, pool="i32")
        odd = col([pi], ap(pi), 1, AL.bitwise_and, n=C, pool="i32")
        y0, y1 = col([odd], ap(odd), 48.0, AL.mult, 239.0, AL.add, n=C), tile("f32", C)
        tt(y1, ap(y1), ap(y0), ap(pi), AL.subtract, [y0, pi], C)
        y2 = col([pm], ap(pm), -512.0, AL.mult, 48.0 * 512, AL.add, n=C)
        y3, y4, Ln = tile("f32", C), tile("f32", C), tile("u16", C)
        tt(y3, ap(y3), ap(y1), ap(y2), AL.min, [y1, y2], C)
        tt(y4, ap(y4), ap(y3), ap(ii), AL.max, [y3, ii], C)
        tcopy(Ln, ap(Ln), ap(y4), [y4], C)
        if gen < GENS - 1:
            tcopy(G, ap(G, 0, GW, 8), ap(win).indirect(ap(Ln)), [own, come, prev, Ln], dur=gc_(L))
    lab[0] = "out"
    yo, ao, so = tile("f32", L), tile("f32", L), tile("f32", L)
    ts(yo, ap(yo), ap(win).indirect(ap(Ln)), 1536.0, AL.add, None, None, [own, come, prev, Ln], L, dur=gc_(L))
    store(T.yg[:], ap(yo), [yo])
    for h, (i0, W, _) in enumerate(HV):
        act(ao, ap(ao, i0, i0 + W), ap(a[h]), AF.Copy, [a[h]], W)
    store(T.ya[:], ap(ao), [ao])
    sp = ps(BW[0], 0, L)
    mms([sp], [X, Idb], [[(ap(sp), ap(Idb), ap(X, s, XW, 16)) for s in range(16)]], 16 * L)
    act(so, ap(so), ap(sp), AF.Copy, [sp], L)
    store(T.ys[:], ap(so), [so])
    emit(g, T, tasks)


def tid(d):
    return d[0] if isinstance(d, tuple) else d


def turn_of(t, lag):
    if t["turn"] is None:
        return t["at"]
    gen, step, h, what, j = t["turn"]
    return gen * PLAN["generation"] + PLAN["start"][step] + h * lag + PLAN[what][0] + j * PLAN[what][1]


def order(tasks):
    n = len(tasks)
    durs = [[0.05 if t["kind"] == "d" else t["dur"][c] for t in tasks] for c in range(len(COSTS))]
    dur = durs[0]
    tail, none = [t["dur"][0] - u for t, u in zip(tasks, dur)], [0.0] * n
    own = [CFG["own"] if t["q"] in "VS" else 0.0 for t in tasks]
    either = [i for i, t in enumerate(tasks) if t["either"]]

    def links(c):
        pred, succ = [[] for _ in range(n)], [[] for _ in range(n)]
        for i, t in enumerate(tasks):
            for d, lag in t["deps"].items():
                lag += c["hop"] / 2 if isinstance(d, tuple) else 0.0
                pred[i].append((tid(d), lag))
                succ[tid(d)].append((i, lag))
        return pred, succ
    pred, succ = links(COSTS[0])
    others = [(links(c)[0], u, c["sem"]) for c, u in zip(COSTS, durs)][1:]
    line, need = [], [len(p) for p in pred]
    line += [i for i in range(n) if not need[i]]
    for i in line:
        for j, _ in succ[i]:
            need[j] -= 1
            if not need[j]:
                line.append(j)
    assert len(line) == n

    def place(q, before, walk, key, first):
        key, sem = list(key), COSTS[0]["sem"]
        for i in walk:
            for j, _ in before[i]:
                if key[j] >= key[i]:
                    key[i] = key[j] + 1e-6
        end, busy = [0.0] * n, {x: [] for x in "VSPGYW"}
        for i in sorted(walk, key=lambda j: key[j]):
            st, mine = first[i], q[i]
            for j, lag in before[i]:
                u = end[j] + lag + (own[i] if q[j] == mine else sem)
                if u > st:
                    st = u
            slots = busy[mine]
            at = len(slots)
            while at and slots[at - 1][1] > st:
                at -= 1
            while at < len(slots) and slots[at][0] < st + dur[i] - 1e-9:
                st, at = max(st, slots[at][1]), at + 1
            slots.insert(at, (st, st + dur[i]))
            end[i] = st + dur[i]
        return end

    def length(q, issue, before, dur, sem, upto=None):
        end, free = [0.0] * n, {x: 0.0 for x in "VSPGYW"}
        for i in issue:
            mine = q[i]
            st = free[mine]
            for j, lag in before[i]:
                u = end[j] + lag + (own[i] if q[j] == mine else sem)
                if u > st:
                    st = u
            end[i] = free[mine] = st + dur[i]
        return max(e + u for e, u in zip(end, tail)) if upto is None else end[upto]

    def closed(q, key, limit):
        end = place(q, pred, line, key, none)
        back = place(q, succ, line[::-1], [-e - u for e, u in zip(end, tail)], tail)
        end = min(end, place(q, pred, line, [-e for e in back], none), key=lambda x: max(e + u for e, u in zip(x, tail)))
        span = max(e + u for e, u in zip(end, tail))
        if span > limit:
            return None
        start = [e - u for e, u in zip(end, dur)]
        issue = sorted(line, key=lambda i: start[i])
        return span + sum(length(q, issue, *o) for o in others), span, start, issue, q

    def held(q, issue, before, dur, sem):
        end, last, cause = [0.0] * n, {}, [None] * n
        for i in issue:
            mine = q[i]
            st, cause[i] = (end[last[mine]], (last[mine], True)) if mine in last else (0.0, None)
            for j, lag in before[i]:
                u = end[j] + lag + (own[i] if q[j] == mine else sem)
                if u >= st:
                    st, cause[i] = u, (j, False)
            end[i], last[mine] = st + dur[i], i
        i, out = max(range(n), key=lambda j: end[j] + tail[j]), []
        while cause[i]:
            if cause[i][1]:
                out.append((i, cause[i][0]))
            i = cause[i][0]
        return out
    every, waits, other = [(pred, dur, COSTS[0]["sem"])] + others, [], {"V": "S", "S": "V"}
    rng = np.random.default_rng(CFG["seed"])

    def shifted(now, passes):
        best = now
        del waits[:]
        for m in range(passes):
            size, lo, wide, move = rng.random(4).tolist()
            lo, q, key = lo * now[1], list(now[4]), list(now[2])
            if move < CFG["swap"]:
                if not waits:
                    waits.extend(held(q, now[3], *every[m % len(every)]))
                i, j = waits.pop(int(rng.integers(len(waits))))
                if tasks[j]["either"] and size < 0.3:
                    q[j] = other[q[j]]
                elif size < 0.65:
                    key[i] = key[j] - 0.01 - wide * wide
                else:
                    key[j] = key[i] + 0.01 + wide * wide
            else:
                if move > 1 - CFG["flip"]:
                    i = either[int(rng.integers(len(either)))]
                    q[i], lo, size = other[q[i]], now[2][i] - 3, size / 2
                key = [u + size * x if lo < u < lo + 3 + 15 * wide else u for u, x in zip(key, rng.normal(size=n).tolist())]
            new = closed(q, key, now[1] + 1.5)
            if new and new[0] <= now[0] + CFG["slack"] * (1 - m / passes):
                now = new
                del waits[:]
                if new[0] < best[0]:
                    best = new
        return best
    tries = [shifted(closed([t["q"] for t in tasks], [turn_of(t, lag) for t in tasks], 1e9), CFG["passes"]) for lag in CFG["lags"]]
    joint = max(i for i, t in enumerate(tasks) if t["turn"] and t["turn"][0] == 0)
    late = [t["turn"] is not None and t["turn"][0] > 0 for t in tasks]
    for _ in range(CFG["rounds"]):
        first = [sum(length(u[4], u[3], *o, upto=joint) for o in every) for u in tries]
        u = tries[first.index(min(first))]
        v = min(zip(tries, first), key=lambda w: w[0][0] - w[1])[0]
        shift = u[2][joint] - v[2][joint]
        both = closed([b if z else a for a, b, z in zip(u[4], v[4], late)], [b + shift if z else a for a, b, z in zip(u[2], v[2], late)], 1e9)
        best = min(tries + [both], key=lambda w: w[0])
        tries = [shifted(best, CFG["more"]) for _ in range(CFG["again"])]
    best = min(tries, key=lambda w: w[0])

    def moved(issue, i, j, forward):
        a, b = issue.index(j), issue.index(i)
        span = issue[a:b + 1]
        if forward:
            take = {i}
            for u in reversed(span):
                if u in take:
                    take.update(v for v, _ in pred[u])
        else:
            take = {j}
            for u in span:
                if any(v in take for v, _ in pred[u]):
                    take.add(u)
        if i in take and j in take:
            return None
        return issue[:a] + [u for u in span if (u in take) == forward] + [u for u in span if (u in take) != forward] + issue[b + 1:]

    def total(q, issue, a, old):
        ends, last = [], {}
        for i in issue[:a]:
            last[q[i]] = i
        for (before, dur, sem), end in zip(every, old):
            end, free = list(end), {x: end[last[x]] if x in last else 0.0 for x in "VSPGYW"}
            for i in issue[a:]:
                mine = q[i]
                st = free[mine]
                for j, lag in before[i]:
                    u = end[j] + lag + (own[i] if q[j] == mine else sem)
                    if u > st:
                        st = u
                end[i] = free[mine] = st + dur[i]
            ends.append(end)
        return sum(max(end[i] + tail[i] for i in stores) for end in ends), issue, q, ends
    stores = [i for i in range(n) if tail[i] > 0]
    now = best = total(best[4], best[3], 0, [none] * len(every))
    del waits[:]
    for m in range(CFG["moves"]):
        if not waits:
            waits.extend(held(now[2], now[1], *every[m % len(every)]))
        i, j = waits.pop(int(rng.integers(len(waits))))
        kind, luck = rng.random(2).tolist()
        issue, q = now[1], now[2]
        if kind < 0.25 and (tasks[i]["either"] or tasks[j]["either"]):
            u = i if tasks[i]["either"] and (kind < 0.12 or not tasks[j]["either"]) else j
            q = list(q)
            q[u] = other[q[u]]
        else:
            issue = moved(issue, i, j, kind < 0.65)
            if issue is None:
                continue
        new = total(q, issue, now[1].index(j), now[3])
        if new[0] <= now[0] - CFG["heat"] * (1 - m / CFG["moves"]) * np.log(luck + 1e-9):
            now = new
            del waits[:]
            if new[0] < best[0]:
                best = now
    return best[1], best[2]


def emit(g, T, tasks):
    eng = {"V": g.vector, "S": g.scalar, "P": g.tensor, "G": g, "Y": g.sync}
    sem_of = {"V": "sV", "S": "sS", "P": "sP", "G": "sG"}
    count = {s: 0 for s in sem_of.values()}
    known, done = {q: {} for q in eng}, {}
    sent, ends = 0, []
    if not ORDER:
        del QUEUE[:]
        for u, v in zip((ORDER, QUEUE), order(tasks)):
            u.extend(v)
    for i in ORDER:
        t = tasks[i]
        NOTE[0] = t["lab"]
        q = QUEUE[i]
        if q == "W":
            continue
        k, need = known[q], {}
        for d in t["deps"]:
            if d in t["soft"] or QUEUE[tid(d)] == "W":
                continue
            s, v, kn = done[d]
            if k.get(s, 0) < v and need.get(s, (0, None))[0] < v:
                need[s] = (v, kn)
        for s in sorted(need, key=lambda s: -len(need[s][1])):
            v, kn = need[s]
            if k.get(s, 0) >= v or any(o != s and need[o][1].get(s, 0) >= v and k.get(o, 0) < need[o][0] for o in need):
                continue
            eng[q].wait_ge(T.sem[s], v)
            for b, w in kn.items():
                k[b] = max(k.get(b, 0), w)
            k[s] = max(v, k.get(s, 0))
        for s, (v, kn) in need.items():
            if k.get(s, 0) < v:
                eng[q].wait_ge(T.sem[s], v)
                k[s] = v
        ins = t["fn"]()
        if t["kind"] == "c":
            s = sem_of[q]
            for m in ins:
                m.then_inc(T.sem[s], 1)
            count[s] += len(ins)
            done[i] = (s, count[s], dict(k))
        elif t["kind"] == "d":
            s = "d%d" % t["x"]
            ins[0].then_inc(T.sem[s], 16)
            done[i] = (s, 16, dict(k))
            ends.append((s, 16))
        else:
            got, out = t["x"]
            sent += out
            for m, (name, c) in enumerate(got):
                done[(i, m)] = (name, c, {})
                ends.append((name, c))
    for s, v in ends + [("left", sent)] + list(count.items()):
        if known["Y"].get(s, 0) < v:
            g.sync.wait_ge(T.sem[s], v)
